import numpy as np
import ml_dtypes


def mxq(x, axis, fmt="e4m3"):
    dtype, down = {"e4m3": (ml_dtypes.float8_e4m3fn, 7), "e5m2": (ml_dtypes.float8_e5m2, 14)}[fmt]
    v = np.moveaxis(np.asarray(x, np.float32).astype(ml_dtypes.bfloat16).astype(np.float64), axis, -1)
    blocks = v.reshape(v.shape[:-1] + (-1, 32))
    amax = np.abs(blocks).max(-1, keepdims=True)
    byte = np.maximum(np.where(amax > 0, np.frexp(amax)[1] - 1 + 127, 0) - down, 1)
    scale = np.exp2(byte - 127.0)
    codes = (blocks / scale).astype(np.float32).astype(dtype).astype(np.float64)
    return np.moveaxis((codes * scale).reshape(v.shape), -1, axis)


WIDE = False


def mx_kscale(k):
    if not WIDE:
        return np.ones(k)
    levels = np.array([10, -10, 5, -5, 0])
    if k % 512:
        return np.exp2(np.random.permutation(np.resize(levels, k // 32))).repeat(32)
    a = np.empty((k // 512, 16))
    for p in range(k // 512):
        a[p, :8] = np.random.permutation(np.resize(levels, 8))
        for g in range(8):
            far = levels[np.abs(levels - a[p, g]) >= 10]
            a[p, g + 8] = far[np.random.randint(len(far))]
    return np.exp2(a.ravel()).repeat(32)


BF16 = ml_dtypes.bfloat16


def bf(x):
    return np.asarray(x, np.float32).astype(BF16)


def f64(x):
    return np.asarray(x).astype(np.float64)


E2M1 = np.array([0.0, 0.5, 1.0, 1.5, 2.0, 3.0, 4.0, 6.0, -0.0, -0.5, -1.0, -1.5, -2.0, -3.0, -4.0, -6.0])


def pack_weight(w, fmt):
    k, n = w.shape
    w = f64(bf(w)).reshape(k // 32, 32, n)
    amax = np.abs(w).max(1)
    if fmt == "e4m3":
        byte = np.frexp(amax)[1] - 1 + 127 - 7
    else:
        mant, ex = np.frexp(amax / 6.0)
        byte = np.where(mant > 0.5, ex, ex - 1) + 127
    byte = np.clip(np.where(amax > 0, byte, 1), 1, 254)
    scaled = (w * np.exp2(127.0 - byte)[:, None, :]).reshape(k, n).astype(np.float32)
    by_word = np.ascontiguousarray(scaled.reshape(k // 512, 128, 4, n).transpose(0, 1, 3, 2))
    if fmt == "e4m3":
        words = by_word.astype(ml_dtypes.float8_e4m3fn).view(np.uint8)
    else:
        c = by_word.astype(ml_dtypes.float4_e2m1fn).view(np.uint8) & 0xF
        words = c[..., 0::2] | (c[..., 1::2] << 4)
    return np.ascontiguousarray(words), np.ascontiguousarray(byte.astype(np.uint8).reshape(k // 512, 16, n))


def unpack_weight(words, scales, fmt):
    g, p, n, _ = words.shape
    if fmt == "e4m3":
        vals = np.ascontiguousarray(words).view(ml_dtypes.float8_e4m3fn).astype(np.float64)
    else:
        nib = np.empty((g, p, n, 4), np.uint8)
        nib[..., 0::2] = words & 0xF
        nib[..., 1::2] = words >> 4
        vals = E2M1[nib]
    vals = vals * np.repeat(np.exp2(scales.astype(np.float64) - 127.0), 8, axis=1)[..., None]
    return vals.transpose(0, 1, 3, 2).reshape(g * 512, n)
def pack4(w):
    words, scales = pack_weight(w, "e2m1")
    return words.reshape(words.shape[0], 128, -1), scales


def unpack4(words, scales):
    return unpack_weight(words.reshape(words.shape[0], 128, -1, 2), scales, "e2m1")


def planes(Y):
    n, m = Y.shape
    b = f64(bf(Y)).reshape(n // 32, 32, m)
    amax = np.abs(b).max(1)
    byte = np.clip(np.where(amax > 0, np.frexp(amax)[1] - 1 + 127 - 7, 1), 1, 254)
    codes = (b * np.exp2(127.0 - byte)[:, None, :]).reshape(n, m).astype(np.float32).astype(ml_dtypes.float8_e4m3fn).view(np.uint8)
    words = codes.reshape(n // 512, 128, 4, m).transpose(0, 1, 3, 2)
    return np.ascontiguousarray(words), np.ascontiguousarray(byte.astype(np.uint8).reshape(n // 512, 16, m))


N, D, H, R, M, T = 2048, 1024, 1024, 16, 8, 8


def logsumexp(v, axis, keepdims=False):
    m = v.max(axis=axis, keepdims=True)
    r = m + np.log(np.sum(np.exp(v - m), axis=axis, keepdims=True))
    return r if keepdims else np.squeeze(r, axis=axis)


def setup_inputs():
    s, u = mx_kscale(D), mx_kscale(H)
    x = bf(np.random.standard_normal((N, D)) * s)
    w1_words, w1_scales = pack4(np.random.standard_normal((D, H)) / np.sqrt(D) / s[:, None] * u)
    return {
        "x": x,
        "w1_words": w1_words,
        "w1_scales": w1_scales,
        "b1": bf(0.3 * np.random.standard_normal(H) * u),
        "ws": bf(1.4 * np.random.standard_normal((H, R, M)) / np.sqrt(H) / u[:, None, None]),
        "wc": bf(1.4 * np.random.standard_normal((H, R, M)) / np.sqrt(H) / u[:, None, None]),
        "wp": bf(1.4 * np.random.standard_normal((H, R, M)) / np.sqrt(H) / u[:, None, None]),
        "t": bf(np.random.uniform(0.5, 2.0, T)),
    }


def head(hq, w):
    return (hq @ mxq(f64(w).reshape(H, R * M), 0, "e4m3")).reshape(N, R, M)


def core(x, w1_words, w1_scales, b1, ws, wc, wp, t):
    h = np.maximum((mxq(f64(x), 1, "e4m3") @ unpack4(w1_words, w1_scales)) + f64(b1)[None, :], 0.0)
    hq = mxq(h, 1, "e4m3")
    s = head(hq, ws)
    c = head(hq, wc)
    p = head(hq, wp)
    k = np.exp(0.5 * np.tanh(s))
    l = np.tanh(c)
    q = p - logsumexp(p, 2, keepdims=True)
    log_t = np.log(f64(t))[None, None, :, None]
    cum = np.exp(k[:, :, None, :] * (log_t - l[:, :, None, :]))
    return logsumexp(q[:, :, None, :] - cum, 3)


def reference(x, w1_words, w1_scales, b1, ws, wc, wp, t):
    R_out = core(x, w1_words, w1_scales, b1, ws, wc, wp, t)
    words, scales = planes(np.moveaxis(R_out, 0, 0).reshape(2048, -1))
    return R_out, words, scales

@@ -1,0 +1,783 @@
+from contextlib import ExitStack
+
+import concourse.mybir as mybir
+from concourse.masks import make_identity
+
+N, D, H, R, M, T = 2048, 1024, 1024, 16, 8, 8
+FLOPS = 2 * N * D * H + 3 * 2 * N * H * R * M
+
+F32 = mybir.dt.float32
+BF16 = mybir.dt.bfloat16
+I32 = mybir.dt.int32
+U32 = mybir.dt.uint32
+U8 = mybir.dt.uint8
+FP8X4 = mybir.dt.float8_e4m3fn_x4
+FP4X4 = mybir.dt.float4_e2m1fn_x4
+ACT = mybir.ActivationFunctionType
+ALU = mybir.AluOpType
+AX = mybir.AxisListType
+
+P = 128
+G = 512
+GROUPS = N // G
+SR = 4 * R
+AL = 64
+
+
+def tile_deepsurvivalmachinesweibullriskcurves_x2_kernel(
+    tc, x, w1_words, w1_scales, b1, ws, wc, wp, t, out_0, out_1, out_2
+):
+    nc = tc.nc
+    with ExitStack() as ctx:
+        keep = ctx.enter_context(tc.tile_pool(name="keep", bufs=1))
+        work = ctx.enter_context(tc.tile_pool(name="work", bufs=2))
+        psum = ctx.enter_context(tc.psum_pool(name="psum", bufs=1))
+        ctx.enter_context(tc.manual_schedule())
+
+        ident = keep.tile([P, P], F32, name="ident")
+        w1_raw = keep.tile([P, 2, 2 * H], U8, name="w1_raw", align_bytes=AL)
+        s1_raw = keep.tile([P, 2, H], U8, name="s1_raw", align_bytes=AL)
+        w1c = [keep.tile([P, 2, 2 * G], U8, name="w1c%d" % j, align_bytes=AL) for j in range(2)]
+        w1s = [keep.tile([P, 2, G], U8, name="w1s%d" % j, align_bytes=AL) for j in range(2)]
+        bias = keep.tile([P, 2, 4], BF16, name="bias")
+        t_sb = keep.tile([P, T], BF16, name="t_sb")
+        logt = keep.tile([P, T], F32, name="logt")
+        hw_raw = [keep.tile([P, 2, 4, P], BF16, name="hw_raw%d" % j) for j in range(3)]
+        hwc = [keep.tile([P, 2, P], U32, name="hwc%d" % j, align_bytes=AL) for j in range(3)]
+        hws = [keep.tile([P, 2, P], U8, name="hws%d" % j, align_bytes=AL) for j in range(3)]
+        x_sb = [[keep.tile([P, 4, G], BF16, name="x_sb%d_%d" % (g, kg)) for kg in range(2)] for g in range(GROUPS)]
+        wmin = [keep.tile([P, T, SR], F32, name="wmin%d" % g) for g in range(GROUPS)]
+        sums = [keep.tile([P, 4, P], F32, name="sums%d" % g) for g in range(GROUPS)]
+        norm = [keep.tile([P, 2, P], F32, name="norm%d" % g) for g in range(GROUPS)]
+        out_scales = keep.tile([P, GROUPS, P], U8, name="out_scales", align_bytes=AL)
+
+        def load_x(g, kg):
+            rows = x[G * g : G * (g + 1), G * kg : G * (kg + 1)]
+            nc.sync.dma_start(out=x_sb[g][kg][:], in_=rows.rearrange("(p s) k -> p s k", s=4))
+
+        nc.vector.memset(s1_raw[:].bitcast(I32), 0)
+        make_identity(nc, ident[:])
+        nc.scalar.dma_start(out=t_sb[:], in_=t.partition_broadcast(P))
+        for q in range(4):
+            nc.scalar.dma_start(
+                out=s1_raw[32 * q : 32 * q + 4].bitcast(I32),
+                in_=w1_scales[:, 4 * q : 4 * q + 4, :].rearrange("g r n -> r g n").bitcast(I32),
+            )
+        load_x(0, 0)
+        nc.sync.dma_start(out=w1_raw[:].bitcast(I32), in_=w1_words.rearrange("g p b -> p g b").bitcast(I32))
+        load_x(0, 1)
+        nc.sync.dma_start(out=bias[:], in_=b1.rearrange("(g p j) -> p g j", g=2, j=4))
+        load_x(1, 0)
+        for j, w in enumerate((ws, wc, wp)):
+            nc.sync.dma_start(out=hw_raw[j][:], in_=w.rearrange("(g p j) r m -> p g j (r m)", g=2, j=4))
+        load_x(1, 1)
+        for g in range(2, GROUPS):
+            load_x(g, 0)
+            load_x(g, 1)
+        nc.scalar.activation(out=logt[:], in_=t_sb[:], func=ACT.Ln)
+        warm = keep.tile([P, 1], F32, name="warm")
+        nc.scalar.activation(out=warm[:], in_=logt[:, 0:1], func=ACT.Tanh)
+
+        def order_w1(hg):
+            for kg in range(2):
+                src = w1_raw[:, kg, 2 * G * hg : 2 * G * (hg + 1)]
+                nc.vector.tensor_copy(
+                    out=w1c[hg][:, kg, :].rearrange("p (j m e) -> p j m e", j=4, e=2),
+                    in_=src.rearrange("p (m j e) -> p j m e", j=4, e=2),
+                )
+            nc.vector.tensor_copy(
+                out=w1s[hg][:].rearrange("p g (j m) -> p g j m", j=4),
+                in_=s1_raw[:, :, G * hg : G * (hg + 1)].rearrange("p g (m j) -> p g j m", j=4),
+            )
+
+        def lay_head(j):
+            laid = work.tile([P, 2, P, 4], BF16, name="head_laid", bufs=3, align_bytes=AL)
+            nc.vector.tensor_copy(out=laid[:], in_=hw_raw[j][:].rearrange("p g j n -> p g n j"))
+            st["head", j] = laid
+
+        def quant_head(j):
+            nc.vector.quantize_mx(
+                out=hwc[j][:].rearrange("p g n -> p (g n)").bitcast(FP8X4),
+                scales=hws[j][:].rearrange("p g n -> p (g n)"),
+                in_=st["head", j][:].rearrange("p g n j -> p (g n j)"),
+            )
+
+        st = {}
+
+        def front_bank():
+            return psum.tile([P, G], F32, name="front", bufs=3)
+
+        def turn_x(g, kg, sp):
+            if ("xg", g, kg) not in st:
+                st["xg", g, kg] = work.tile([P, G, 4], BF16, name="xg", bufs=3, align_bytes=AL)
+            bank = front_bank()
+            words = x_sb[g][kg][:].bitcast(F32)
+            for s in range(2):
+                for u in range(2):
+                    c = P * (2 * s + u)
+                    nc.tensor.transpose(bank[:, c : c + P], words[:, 2 * sp + s, u : 256 : 2], ident[:])
+            st["xb", g, kg, sp] = bank
+
+        def copy_x(g, kg, sp, eng):
+            dst = st["xg", g, kg][:, 256 * sp : 256 * (sp + 1), :].bitcast(F32).rearrange("p (s n) u -> p s n u", s=2)
+            src = st["xb", g, kg, sp][:].rearrange("p (s u n) -> p s n u", s=2, u=2)
+            if eng == "A":
+                nc.scalar.copy(out=dst, in_=src)
+            else:
+                nc.vector.tensor_copy(out=dst, in_=src)
+
+        def quant_x(g, kg):
+            codes = work.tile([P, G], U32, name="xc", bufs=4, align_bytes=AL)
+            scales = work.tile([P, G], U8, name="xs", bufs=4, align_bytes=AL)
+            nc.vector.quantize_mx(
+                out=codes[:].bitcast(FP8X4), scales=scales[:], in_=st["xg", g, kg][:].rearrange("p n j -> p (n j)")
+            )
+            st["xq", g, kg] = (codes, scales)
+
+        def layer1(g, hg, j):
+            bank = front_bank()
+            for kg in range(2):
+                codes, scales = st["xq", g, kg]
+                nc.tensor.matmul_mx(
+                    out=bank[:],
+                    lhsT=w1c[hg][:, kg, 2 * P * j : 2 * P * (j + 1)].bitcast(FP4X4),
+                    lhsT_scale=w1s[hg][:, kg, P * j : P * (j + 1)],
+                    rhs=codes[:].bitcast(FP8X4),
+                    rhs_scale=scales[:],
+                    start=(kg == 0),
+                    stop=(kg == 1),
+                )
+            st["hb", g, hg, j] = bank
+
+        def relu_h(g, hg, j, eng):
+            if ("h", g, hg) not in st:
+                st["h", g, hg] = work.tile([P, 4, G], BF16, name="h", bufs=2)
+            dst, src, b = st["h", g, hg][:, j, :], st["hb", g, hg, j][:], bias[:, hg, j : j + 1]
+            if eng == "A":
+                nc.scalar.activation(out=dst, in_=src, func=ACT.Relu, bias=b)
+            else:
+                nc.vector.tensor_scalar(out=dst, in0=src, scalar1=b, scalar2=0.0, op0=ALU.add, op1=ALU.max)
+
+        def lay_h(g, hg):
+            laid = work.tile([P, G, 4], BF16, name="h_laid", bufs=2, align_bytes=AL)
+            nc.vector.tensor_copy(out=laid[:], in_=st["h", g, hg][:].rearrange("p j n -> p n j"))
+            st["hl", g, hg] = laid
+
+        def quant_h(g, hg):
+            codes = work.tile([P, G], U32, name="hc", bufs=2, align_bytes=AL)
+            scales = work.tile([P, G], U8, name="hs", bufs=2, align_bytes=AL)
+            nc.vector.quantize_mx(
+                out=codes[:].bitcast(FP8X4), scales=scales[:], in_=st["hl", g, hg][:].rearrange("p n j -> p (n j)")
+            )
+            st["hq", g, hg] = (codes, scales)
+
+        def head(g, j):
+            bank = front_bank()
+            for hg in range(2):
+                codes, scales = st["hq", g, hg]
+                nc.tensor.matmul_mx(
+                    out=bank[:],
+                    lhsT=hwc[j][:, hg, :].bitcast(FP8X4),
+                    lhsT_scale=hws[j][:, hg, :],
+                    rhs=codes[:].bitcast(FP8X4),
+                    rhs_scale=scales[:],
+                    start=(hg == 0),
+                    stop=(hg == 1),
+                )
+            st["head_bank", g, j] = bank
+
+        def shape_k(g):
+            ths = work.tile([P, G], F32, name="ths", bufs=1)
+            nc.scalar.activation(out=ths[:], in_=st["head_bank", g, 0][:], func=ACT.Tanh)
+            lsc = work.tile([P, G], F32, name="lsc", bufs=1)
+            nc.scalar.activation(out=lsc[:], in_=st["head_bank", g, 1][:], func=ACT.Tanh)
+            k = work.tile([P, G], F32, name="k", bufs=2)
+            nc.scalar.activation(out=k[:], in_=ths[:], func=ACT.Exp, scale=0.5)
+            st["k", g] = k
+            st["l", g] = lsc
+
+        def neg_p(g, eng):
+            negp = work.tile([P, G], F32, name="negp", bufs=2)
+            src = st["head_bank", g, 2][:]
+            if eng == "A":
+                nc.scalar.activation(out=negp[:], in_=src, func=ACT.Copy, scale=-1.0)
+            else:
+                nc.vector.tensor_scalar(out=negp[:], in0=src, scalar1=-1.0, scalar2=None, op0=ALU.mult)
+            st["np", g] = negp
+
+        def k_times_l(g, eng):
+            kl = work.tile([P, G], F32, name="kl", bufs=1)
+            (nc.vector if eng == "V" else nc.gpsimd).tensor_tensor(out=kl[:], in0=st["k", g][:], in1=st["l", g][:], op=ALU.mult)
+            st["kl", g] = kl
+
+        def amp(g):
+            a = work.tile([P, G], F32, name="amp", bufs=2)
+            nc.scalar.activation(out=a[:], in_=st["kl", g][:], func=ACT.Exp, scale=-1.0)
+            st["A", g] = a
+
+        def turn_p(g):
+            bank = psum.tile([P, G], F32, name="misc", bufs=1)
+            for s in range(4):
+                nc.tensor.transpose(bank[:, P * s : P * (s + 1)], st["np", g][:, P * s : P * (s + 1)], ident[:])
+            st["p0", g] = bank
+
+        def min_p(g):
+            w0 = work.tile([P, 2, SR], F32, name="w0", bufs=1)
+            nc.vector.tensor_reduce(
+                out=w0[:, 0, :], in_=st["p0", g][:].rearrange("p (c m) -> p c m", m=M), axis=AX.X, op=ALU.min
+            )
+            nc.gpsimd.tensor_copy(out=w0[:, 1, :], in_=w0[:, 0, :])
+            st["w0", g] = w0
+
+        def sub_p(g):
+            z0 = work.tile([P, M, SR], F32, name="z0", bufs=1)
+            nc.vector.tensor_tensor(
+                out=z0[:],
+                in0=st["p0", g][:].rearrange("p (c m) -> p m c", m=M),
+                in1=st["w0", g][:, 0:1, :].to_broadcast([P, M, SR]),
+                op=ALU.subtract,
+            )
+            st["z0", g] = z0
+
+        def exp_p(g):
+            e0 = work.tile([P, M + 1, SR], F32, name="e0", bufs=1)
+            nc.scalar.activation(out=e0[:, 0:M, :], in_=st["z0", g][:], func=ACT.Exp, scale=-1.0)
+            nc.scalar.activation(out=e0[:, M, :], in_=st["z0", g][:, 0, :], func=ACT.Exp, scale=-1.0)
+            st["e0", g] = e0
+
+        def sum_p(g):
+            bank = psum.tile([P, G], F32, name="misc", bufs=1)
+            e0 = st["e0", g][:].rearrange("p m c -> p (m c)")
+            for m in range(M):
+                nc.tensor.matmul(
+                    bank[:, 0:P], e0[:, SR * m : SR * m + P], ident[:], start=(m == 0), stop=(m == M - 1), is_transpose=True
+                )
+            nc.tensor.transpose(bank[:, P : 2 * P], st["w0", g][:].rearrange("p d c -> p (d c)"), ident[:])
+            st["s0", g] = bank
+
+        def move(eng, dst, src):
+            if eng == "A":
+                nc.scalar.copy(out=dst, in_=src)
+            else:
+                nc.vector.tensor_copy(out=dst, in_=src)
+
+        def keep_norm(g, eng):
+            move(eng, norm[g][:].rearrange("p d c -> p (d c)"), st["s0", g][:, 0 : 2 * P])
+
+        def power(g, i):
+            e = work.tile([P, G], F32, name="pow", bufs=3)
+            nc.scalar.activation(out=e[:], in_=st["k", g][:], func=ACT.Exp, scale=logt[:, i : i + 1])
+            st["E", g, i] = e
+
+        def hazard(g, i, eng):
+            cum = work.tile([P, G], F32, name="cum", bufs=3)
+            (nc.vector if eng == "V" else nc.gpsimd).tensor_tensor(out=cum[:], in0=st["E", g, i][:], in1=st["A", g][:], op=ALU.mult)
+            st["cum", g, i] = cum
+
+        def turn_w(g, i):
+            bank = psum.tile([P, G], F32, name="wbank", bufs=3)
+            for s in range(4):
+                cols = slice(P * s, P * (s + 1))
+                nc.tensor.matmul(bank[:, cols], st["cum", g, i][:, cols], ident[:], start=True, stop=False, is_transpose=True)
+                nc.tensor.matmul(bank[:, cols], st["np", g][:, cols], ident[:], start=False, stop=True, is_transpose=True)
+            st["w", g, i] = bank
+
+        def min_w(g, i):
+            nc.vector.tensor_reduce(
+                out=wmin[g][:, i, :], in_=st["w", g, i][:].rearrange("p (c m) -> p c m", m=M), axis=AX.X, op=ALU.min
+            )
+
+        def sub_w(g, i):
+            if i % 2 == 0:
+                st["z", g, i // 2] = work.tile([P, M, 2, SR], F32, name="z", bufs=3)
+            nc.vector.tensor_tensor(
+                out=st["z", g, i // 2][:, :, i % 2, :],
+                in0=st["w", g, i][:].rearrange("p (c m) -> p m c", m=M),
+                in1=wmin[g][:, i : i + 1, :].to_broadcast([P, M, SR]),
+                op=ALU.subtract,
+            )
+
+        def exp_w(g, q):
+            e = work.tile([P, M, P], F32, name="e", bufs=2)
+            nc.scalar.activation(
+                out=e[:], in_=st["z", g, q][:].rearrange("p m d c -> p m (d c)"), func=ACT.Exp, scale=-1.0
+            )
+            st["e", g, q] = e
+
+        def sum_w(g, q):
+            if q == 0:
+                st["s", g] = psum.tile([P, G], F32, name="sbank", bufs=1)
+            for m in range(M):
+                nc.tensor.matmul(
+                    st["s", g][:, P * q : P * (q + 1)], st["e", g, q][:, m, :], ident[:],
+                    start=(m == 0), stop=(m == M - 1), is_transpose=True,
+                )
+
+        def keep_sums(g, eng):
+            move(eng, sums[g][:].rearrange("p q c -> p (q c)"), st["s", g][:])
+
+        def logs(g):
+            ln0 = work.tile([P, P], F32, name="ln0", bufs=4)
+            nc.scalar.activation(out=ln0[:], in_=norm[g][:, 0, :], func=ACT.Ln)
+            lns = work.tile([P, G], F32, name="lns", bufs=4)
+            src = st["s", g][:] if g == GROUPS - 1 else sums[g][:].rearrange("p q c -> p (q c)")
+            nc.scalar.activation(out=lns[:], in_=src, func=ACT.Ln)
+            st["ln", g] = (ln0, lns)
+
+        def offset(g):
+            c0 = work.tile([P, P], F32, name="c0", bufs=4)
+            nc.vector.tensor_tensor(out=c0[:], in0=norm[g][:, 1, :], in1=st["ln", g][0][:], op=ALU.subtract)
+            st["c0", g] = c0
+
+        def turn_back(g):
+            bank = front_bank()
+            for q in range(4):
+                cols = slice(P * q, P * (q + 1))
+                nc.tensor.matmul(bank[:, cols], st["ln", g][1][:, cols], ident[:], start=True, stop=False, is_transpose=True)
+                nc.tensor.matmul(bank[:, cols], st["c0", g][:], ident[:], start=False, stop=True, is_transpose=True)
+            st["fin", g] = bank
+
+        def result(g):
+            res = work.tile([P, SR, T], F32, name="res", bufs=4)
+            for hf in range(2):
+                nc.vector.tensor_tensor(
+                    out=res[:, :, 4 * hf : 4 * hf + 4],
+                    in0=st["fin", g][:].rearrange("p (i c) -> p c i", i=T)[:, :, 4 * hf : 4 * hf + 4],
+                    in1=wmin[g][:].rearrange("p i c -> p c i")[:, :, 4 * hf : 4 * hf + 4],
+                    op=ALU.subtract,
+                )
+            nc.sync.dma_start(
+                out=out_0[G * g : G * (g + 1)].rearrange("(p s) r i -> p (s r) i", s=4), in_=res[:]
+            )
+            st["res", g] = res
+
+        def lay_out(g, eng):
+            laid = work.tile([P, P, 4], BF16, name="out_laid", bufs=4, align_bytes=AL)
+            src = st["res", g][:].rearrange("p (s r) i -> p (r i) s", s=4)
+            if eng == "A":
+                nc.scalar.copy(out=laid[:], in_=src)
+            else:
+                nc.vector.tensor_copy(out=laid[:], in_=src)
+            st["ol", g] = laid
+
+        def quant_out(g):
+            codes = work.tile([P, P], U32, name="out_codes", bufs=4, align_bytes=AL)
+            nc.vector.quantize_mx(
+                out=codes[:].bitcast(FP8X4), scales=out_scales[:, g, :], in_=st["ol", g][:].rearrange("p n j -> p (n j)")
+            )
+            nc.sync.dma_start(out=out_1[g].rearrange("p m j -> p (m j)").bitcast(I32), in_=codes[:].bitcast(I32))
+
+        plan = []
+
+        def at(when, fn, *args):
+            plan.append((when, len(plan), fn, args))
+
+        at(0, order_w1, 1)
+        at(1, turn_x, 0, 0, 1)
+        at(2, turn_x, 0, 0, 0)
+        at(3, copy_x, 0, 0, 0, "A")
+        at(4, turn_x, 0, 1, 1)
+        at(5, copy_x, 0, 0, 1, "A")
+        at(6, quant_x, 0, 0)
+        at(7, copy_x, 0, 1, 1, "A")
+        at(8, order_w1, 0)
+        at(9, turn_x, 0, 1, 0)
+        at(10, copy_x, 0, 1, 0, "A")
+        at(11, quant_x, 0, 1)
+        at(12, layer1, 0, 0, 2)
+        at(13, layer1, 0, 0, 0)
+        at(14, layer1, 0, 0, 1)
+        at(15, lay_head, 0)
+        at(16, relu_h, 0, 0, 2, "A")
+        at(17, lay_head, 2)
+        at(18, relu_h, 0, 0, 0, "A")
+        at(19, lay_head, 1)
+        at(20, quant_head, 0)
+        at(21, layer1, 0, 0, 3)
+        at(22, relu_h, 0, 0, 1, "A")
+        at(23, layer1, 0, 1, 3)
+        at(24, layer1, 0, 1, 1)
+        at(25, relu_h, 0, 0, 3, "V")
+        at(26, relu_h, 0, 1, 3, "A")
+        at(27, relu_h, 0, 1, 1, "A")
+        at(28, lay_h, 0, 0)
+        at(29, layer1, 0, 1, 0)
+        at(30, relu_h, 0, 1, 0, "V")
+        at(31, layer1, 0, 1, 2)
+        at(32, relu_h, 0, 1, 2, "A")
+        at(33, turn_x, 1, 0, 1)
+        at(34, quant_head, 2)
+        at(35, lay_h, 0, 1)
+        at(36, turn_x, 1, 0, 0)
+        at(37, copy_x, 1, 0, 1, "A")
+        at(38, quant_h, 0, 0)
+        at(39, copy_x, 1, 0, 0, "A")
+        at(40, turn_x, 1, 1, 0)
+        at(41, turn_x, 1, 1, 1)
+        at(42, quant_h, 0, 1)
+        at(43, copy_x, 1, 1, 0, "A")
+        at(44, head, 0, 2)
+        at(45, quant_head, 1)
+        at(46, copy_x, 1, 1, 1, "A")
+        at(47, quant_x, 1, 0)
+        at(48, head, 0, 0)
+        at(49, head, 0, 1)
+        at(50, quant_x, 1, 1)
+        at(51, neg_p, 0, "A")
+        at(52, layer1, 1, 0, 1)
+        at(53, shape_k, 0)
+        at(54, relu_h, 1, 0, 1, "V")
+        at(55, layer1, 1, 0, 0)
+        at(56, turn_p, 0)
+        at(57, relu_h, 1, 0, 0, "A")
+        at(58, layer1, 1, 0, 2)
+        at(59, k_times_l, 0, "V")
+        at(60, power, 0, 0)
+        at(61, min_p, 0)
+        at(62, sub_p, 0)
+        at(63, amp, 0)
+        at(64, relu_h, 1, 0, 2, "V")
+        at(65, layer1, 1, 0, 3)
+        at(66, power, 0, 1)
+        at(67, layer1, 1, 1, 1)
+        at(68, layer1, 1, 1, 3)
+        at(69, hazard, 0, 0, "P")
+        at(70, relu_h, 1, 0, 3, "A")
+        at(71, exp_p, 0)
+        at(72, power, 0, 2)
+        at(73, layer1, 1, 1, 0)
+        at(74, turn_w, 0, 0)
+        at(75, hazard, 0, 1, "V")
+        at(76, power, 0, 3)
+        at(77, relu_h, 1, 1, 0, "A")
+        at(78, lay_h, 1, 0)
+        at(79, sum_p, 0)
+        at(80, min_w, 0, 0)
+        at(81, turn_w, 0, 1)
+        at(82, hazard, 0, 2, "P")
+        at(83, relu_h, 1, 1, 1, "A")
+        at(84, layer1, 1, 1, 2)
+        at(85, power, 0, 4)
+        at(86, relu_h, 1, 1, 2, "A")
+        at(87, relu_h, 1, 1, 3, "V")
+        at(88, sub_w, 0, 0)
+        at(89, min_w, 0, 1)
+        at(90, turn_w, 0, 2)
+        at(91, hazard, 0, 3, "P")
+        at(92, turn_x, 2, 0, 0)
+        at(93, power, 0, 5)
+        at(94, turn_x, 2, 1, 0)
+        at(95, sub_w, 0, 1)
+        at(96, min_w, 0, 2)
+        at(97, turn_w, 0, 3)
+        at(98, lay_h, 1, 1)
+        at(99, turn_x, 2, 0, 1)
+        at(100, copy_x, 2, 0, 0, "A")
+        at(101, quant_h, 1, 0)
+        at(102, hazard, 0, 4, "P")
+        at(103, copy_x, 2, 1, 0, "A")
+        at(104, exp_w, 0, 0)
+        at(105, power, 0, 6)
+        at(106, turn_x, 2, 1, 1)
+        at(107, quant_h, 1, 1)
+        at(108, copy_x, 2, 0, 1, "A")
+        at(109, sub_w, 0, 2)
+        at(110, copy_x, 2, 1, 1, "A")
+        at(111, min_w, 0, 3)
+        at(112, turn_w, 0, 4)
+        at(113, head, 1, 2)
+        at(114, keep_norm, 0, "V")
+        at(115, head, 1, 0)
+        at(116, hazard, 0, 5, "V")
+        at(117, head, 1, 1)
+        at(118, neg_p, 1, "A")
+        at(119, power, 0, 7)
+        at(120, turn_p, 1)
+        at(121, quant_x, 2, 0)
+        at(122, sum_w, 0, 0)
+        at(123, sub_w, 0, 3)
+        at(124, min_w, 0, 4)
+        at(125, turn_w, 0, 5)
+        at(126, shape_k, 1)
+        at(127, hazard, 0, 6, "P")
+        at(128, exp_w, 0, 1)
+        at(129, power, 1, 0)
+        at(130, quant_x, 2, 1)
+        at(131, k_times_l, 1, "P")
+        at(132, sub_w, 0, 4)
+        at(133, amp, 1)
+        at(134, min_w, 0, 5)
+        at(135, turn_w, 0, 6)
+        at(136, layer1, 2, 0, 1)
+        at(137, hazard, 0, 7, "P")
+        at(138, relu_h, 2, 0, 1, "A")
+        at(139, layer1, 2, 0, 3)
+        at(140, layer1, 2, 0, 0)
+        at(141, power, 1, 1)
+        at(142, min_p, 1)
+        at(143, sum_w, 0, 1)
+        at(144, sub_w, 0, 5)
+        at(145, min_w, 0, 6)
+        at(146, turn_w, 0, 7)
+        at(147, sub_p, 1)
+        at(148, layer1, 2, 0, 2)
+        at(149, hazard, 1, 0, "P")
+        at(150, relu_h, 2, 0, 3, "A")
+        at(151, exp_w, 0, 2)
+        at(152, layer1, 2, 1, 3)
+        at(153, power, 1, 2)
+        at(154, relu_h, 2, 0, 2, "A")
+        at(155, sub_w, 0, 6)
+        at(156, min_w, 0, 7)
+        at(157, turn_w, 1, 0)
+        at(158, hazard, 1, 1, "V")
+        at(159, relu_h, 2, 1, 3, "A")
+        at(160, relu_h, 2, 0, 0, "V")
+        at(161, power, 1, 3)
+        at(162, sum_w, 0, 2)
+        at(163, sub_w, 0, 7)
+        at(164, layer1, 2, 1, 1)
+        at(165, min_w, 1, 0)
+        at(166, turn_w, 1, 1)
+        at(167, hazard, 1, 2, "P")
+        at(168, layer1, 2, 1, 2)
+        at(169, exp_w, 0, 3)
+        at(170, power, 1, 4)
+        at(171, lay_h, 2, 0)
+        at(172, relu_h, 2, 1, 1, "A")
+        at(173, layer1, 2, 1, 0)
+        at(174, sub_w, 1, 0)
+        at(175, min_w, 1, 1)
+        at(176, turn_w, 1, 2)
+        at(177, relu_h, 2, 1, 2, "A")
+        at(178, hazard, 1, 3, "P")
+        at(179, relu_h, 2, 1, 0, "V")
+        at(180, turn_x, 3, 0, 0)
+        at(181, power, 1, 5)
+        at(182, sum_w, 0, 3)
+        at(183, turn_x, 3, 1, 0)
+        at(184, sub_w, 1, 1)
+        at(185, min_w, 1, 2)
+        at(186, turn_w, 1, 3)
+        at(187, turn_x, 3, 0, 1)
+        at(188, exp_p, 1)
+        at(189, copy_x, 3, 0, 0, "A")
+        at(190, hazard, 1, 4, "P")
+        at(191, copy_x, 3, 1, 0, "A")
+        at(192, exp_w, 1, 0)
+        at(193, lay_h, 2, 1)
+        at(194, power, 1, 6)
+        at(195, turn_x, 3, 1, 1)
+        at(196, quant_h, 2, 0)
+        at(197, quant_h, 2, 1)
+        at(198, sum_p, 1)
+        at(199, copy_x, 3, 0, 1, "A")
+        at(200, sub_w, 1, 2)
+        at(201, keep_sums, 0, "V")
+        at(202, copy_x, 3, 1, 1, "A")
+        at(203, min_w, 1, 3)
+        at(204, turn_w, 1, 4)
+        at(205, keep_norm, 1, "V")
+        at(206, hazard, 1, 5, "V")
+        at(207, head, 2, 2)
+        at(208, head, 2, 0)
+        at(209, head, 2, 1)
+        at(210, power, 1, 7)
+        at(211, neg_p, 2, "A")
+        at(212, quant_x, 3, 0)
+        at(213, sum_w, 1, 0)
+        at(214, sub_w, 1, 3)
+        at(215, min_w, 1, 4)
+        at(216, turn_w, 1, 5)
+        at(217, shape_k, 2)
+        at(218, hazard, 1, 6, "P")
+        at(219, exp_w, 1, 1)
+        at(220, k_times_l, 2, "P")
+        at(221, turn_p, 2)
+        at(222, power, 2, 0)
+        at(223, quant_x, 3, 1)
+        at(224, sub_w, 1, 4)
+        at(225, min_w, 1, 5)
+        at(226, turn_w, 1, 6)
+        at(227, layer1, 3, 0, 1)
+        at(228, hazard, 1, 7, "P")
+        at(229, relu_h, 3, 0, 1, "A")
+        at(230, layer1, 3, 0, 3)
+        at(231, min_p, 2)
+        at(232, layer1, 3, 0, 0)
+        at(233, power, 2, 1)
+        at(234, sum_w, 1, 1)
+        at(235, amp, 2)
+        at(236, sub_w, 1, 5)
+        at(237, min_w, 1, 6)
+        at(238, turn_w, 1, 7)
+        at(239, layer1, 3, 0, 2)
+        at(240, hazard, 2, 0, "P")
+        at(241, relu_h, 3, 0, 3, "A")
+        at(242, exp_w, 1, 2)
+        at(243, layer1, 3, 1, 3)
+        at(244, power, 2, 2)
+        at(245, relu_h, 3, 0, 2, "A")
+        at(246, sub_p, 2)
+        at(247, sub_w, 1, 6)
+        at(248, min_w, 1, 7)
+        at(249, turn_w, 2, 0)
+        at(250, hazard, 2, 1, "V")
+        at(251, relu_h, 3, 1, 3, "A")
+        at(252, relu_h, 3, 0, 0, "V")
+        at(253, power, 2, 3)
+        at(254, sum_w, 1, 2)
+        at(255, exp_p, 2)
+        at(256, sub_w, 1, 7)
+        at(257, layer1, 3, 1, 1)
+        at(258, min_w, 2, 0)
+        at(259, turn_w, 2, 1)
+        at(260, hazard, 2, 2, "P")
+        at(261, layer1, 3, 1, 2)
+        at(262, exp_w, 1, 3)
+        at(263, power, 2, 4)
+        at(264, lay_h, 3, 0)
+        at(265, relu_h, 3, 1, 1, "A")
+        at(266, layer1, 3, 1, 0)
+        at(267, sub_w, 2, 0)
+        at(268, min_w, 2, 1)
+        at(269, turn_w, 2, 2)
+        at(270, relu_h, 3, 1, 2, "A")
+        at(271, hazard, 2, 3, "P")
+        at(272, relu_h, 3, 1, 0, "V")
+        at(273, power, 2, 5)
+        at(274, sum_w, 1, 3)
+        at(275, sub_w, 2, 1)
+        at(276, min_w, 2, 2)
+        at(277, turn_w, 2, 3)
+        at(278, keep_sums, 1, "A")
+        at(279, hazard, 2, 4, "P")
+        at(280, exp_w, 2, 0)
+        at(281, lay_h, 3, 1)
+        at(282, power, 2, 6)
+        at(283, quant_h, 3, 0)
+        at(284, quant_h, 3, 1)
+        at(285, sub_w, 2, 2)
+        at(286, min_w, 2, 3)
+        at(287, turn_w, 2, 4)
+        at(288, sum_p, 2)
+        at(289, hazard, 2, 5, "V")
+        at(290, head, 3, 2)
+        at(291, head, 3, 0)
+        at(292, head, 3, 1)
+        at(293, power, 2, 7)
+        at(294, neg_p, 3, "A")
+        at(295, sum_w, 2, 0)
+        at(296, sub_w, 2, 3)
+        at(297, min_w, 2, 4)
+        at(298, turn_w, 2, 5)
+        at(299, shape_k, 3)
+        at(300, hazard, 2, 6, "P")
+        at(301, exp_w, 2, 1)
+        at(302, keep_norm, 2, "V")
+        at(303, k_times_l, 3, "P")
+        at(304, turn_p, 3)
+        at(305, power, 3, 0)
+        at(306, sub_w, 2, 4)
+        at(307, min_w, 2, 5)
+        at(308, turn_w, 2, 6)
+        at(309, hazard, 2, 7, "P")
+        at(310, min_p, 3)
+        at(311, power, 3, 1)
+        at(312, sum_w, 2, 1)
+        at(313, amp, 3)
+        at(314, sub_w, 2, 5)
+        at(315, min_w, 2, 6)
+        at(316, turn_w, 2, 7)
+        at(317, hazard, 3, 0, "P")
+        at(318, exp_w, 2, 2)
+        at(319, power, 3, 2)
+        at(320, sub_p, 3)
+        at(321, sub_w, 2, 6)
+        at(322, min_w, 2, 7)
+        at(323, turn_w, 3, 0)
+        at(324, hazard, 3, 1, "P")
+        at(325, power, 3, 3)
+        at(326, sum_w, 2, 2)
+        at(327, exp_p, 3)
+        at(328, sub_w, 2, 7)
+        at(329, min_w, 3, 0)
+        at(330, turn_w, 3, 1)
+        at(331, hazard, 3, 2, "P")
+        at(332, exp_w, 2, 3)
+        at(333, power, 3, 4)
+        at(334, sub_w, 3, 0)
+        at(335, min_w, 3, 1)
+        at(336, turn_w, 3, 2)
+        at(337, hazard, 3, 3, "P")
+        at(338, power, 3, 5)
+        at(339, sum_w, 2, 3)
+        at(340, sub_w, 3, 1)
+        at(341, min_w, 3, 2)
+        at(342, turn_w, 3, 3)
+        at(343, hazard, 3, 4, "P")
+        at(344, exp_w, 3, 0)
+        at(345, keep_sums, 2, "A")
+        at(346, power, 3, 6)
+        at(347, sub_w, 3, 2)
+        at(348, min_w, 3, 3)
+        at(349, turn_w, 3, 4)
+        at(350, sum_p, 3)
+        at(351, hazard, 3, 5, "P")
+        at(352, power, 3, 7)
+        at(353, sum_w, 3, 0)
+        at(354, sub_w, 3, 3)
+        at(355, min_w, 3, 4)
+        at(356, turn_w, 3, 5)
+        at(357, hazard, 3, 6, "P")
+        at(358, exp_w, 3, 1)
+        at(359, keep_norm, 3, "V")
+        at(360, sub_w, 3, 4)
+        at(361, min_w, 3, 5)
+        at(362, turn_w, 3, 6)
+        at(363, hazard, 3, 7, "P")
+        at(364, logs, 0)
+        at(365, sum_w, 3, 1)
+        at(366, sub_w, 3, 5)
+        at(367, min_w, 3, 6)
+        at(368, turn_w, 3, 7)
+        at(369, exp_w, 3, 2)
+        at(370, offset, 0)
+        at(371, sub_w, 3, 6)
+        at(372, min_w, 3, 7)
+        at(373, sum_w, 3, 2)
+        at(374, sub_w, 3, 7)
+        at(375, exp_w, 3, 3)
+        at(376, logs, 2)
+        at(377, sum_w, 3, 3)
+        at(378, logs, 3)
+        at(379, offset, 2)
+        at(380, turn_back, 0)
+        at(381, result, 0)
+        at(382, logs, 1)
+        at(383, offset, 3)
+        at(384, turn_back, 2)
+        at(385, lay_out, 0, "A")
+        at(386, turn_back, 3)
+        at(387, result, 2)
+        at(388, offset, 1)
+        at(389, lay_out, 2, "A")
+        at(390, result, 3)
+        at(391, turn_back, 1)
+        at(392, quant_out, 2)
+        at(393, result, 1)
+        at(394, quant_out, 0)
+        at(395, lay_out, 3, "A")
+        at(396, lay_out, 1, "V")
+        at(397, quant_out, 3)
+        at(398, quant_out, 1)
+
+        for when, n, fn, args in sorted(plan, key=lambda e: e[0:2]):
+            fn(*args)
+
+        for q in range(4):
+            eng = nc.sync if q % 2 == 0 else nc.scalar
+            eng.dma_start(
+                out=out_2[:, 4 * q : 4 * q + 4, :].rearrange("g r m -> r g m").bitcast(I32),
+                in_=out_scales[32 * q : 32 * q + 4].bitcast(I32),
+            )

@@ -35,7 +35,7 @@ def tile_deepsurvivalmachinesweibullriskcurves_x2_kernel(
         ctx.enter_context(tc.manual_schedule())
 
         ident = keep.tile([P, P], F32, name="ident")
-        w1_raw = keep.tile([P, 2, 2 * H], U8, name="w1_raw", align_bytes=AL)
+        w1_raw = [keep.tile([P, 2, 2 * G], U8, name="w1_raw%d" % j, align_bytes=AL) for j in range(2)]
         s1_raw = keep.tile([P, 2, H], U8, name="s1_raw", align_bytes=AL)
         w1c = [keep.tile([P, 2, 2 * G], U8, name="w1c%d" % j, align_bytes=AL) for j in range(2)]
         w1s = [keep.tile([P, 2, G], U8, name="w1s%d" % j, align_bytes=AL) for j in range(2)]
@@ -55,6 +55,10 @@ def tile_deepsurvivalmachinesweibullriskcurves_x2_kernel(
             rows = x[G * g : G * (g + 1), G * kg : G * (kg + 1)]
             nc.sync.dma_start(out=x_sb[g][kg][:], in_=rows.rearrange("(p s) k -> p s k", s=4))
 
+        def load_w1(hg):
+            src = w1_words[:, :, 2 * G * hg : 2 * G * (hg + 1)].rearrange("g p b -> p g b")
+            nc.sync.dma_start(out=w1_raw[hg][:].bitcast(I32), in_=src.bitcast(I32))
+
         nc.vector.memset(s1_raw[:].bitcast(I32), 0)
         make_identity(nc, ident[:])
         nc.scalar.dma_start(out=t_sb[:], in_=t.partition_broadcast(P))
@@ -64,8 +68,9 @@ def tile_deepsurvivalmachinesweibullriskcurves_x2_kernel(
                 in_=w1_scales[:, 4 * q : 4 * q + 4, :].rearrange("g r n -> r g n").bitcast(I32),
             )
         load_x(0, 0)
-        nc.sync.dma_start(out=w1_raw[:].bitcast(I32), in_=w1_words.rearrange("g p b -> p g b").bitcast(I32))
+        load_w1(0)
         load_x(0, 1)
+        load_w1(1)
         nc.sync.dma_start(out=bias[:], in_=b1.rearrange("(g p j) -> p g j", g=2, j=4))
         load_x(1, 0)
         for j, w in enumerate((ws, wc, wp)):
@@ -78,13 +83,18 @@ def tile_deepsurvivalmachinesweibullriskcurves_x2_kernel(
         warm = keep.tile([P, 1], F32, name="warm")
         nc.scalar.activation(out=warm[:], in_=logt[:, 0:1], func=ACT.Tanh)
 
-        def order_w1(hg):
-            for kg in range(2):
-                src = w1_raw[:, kg, 2 * G * hg : 2 * G * (hg + 1)]
-                nc.vector.tensor_copy(
-                    out=w1c[hg][:, kg, :].rearrange("p (j m e) -> p j m e", j=4, e=2),
-                    in_=src.rearrange("p (m j e) -> p j m e", j=4, e=2),
-                )
+        warm_bank = psum.tile([P, G], F32, name="sbank", bufs=1)
+
+        def warm_pe(j):
+            nc.tensor.matmul(warm_bank[:, P * (j % 4) : P * (j % 4 + 1)], ident[:], ident[:], start=True, stop=True)
+
+        def order_w1(hg, kg):
+            nc.vector.tensor_copy(
+                out=w1c[hg][:, kg, :].rearrange("p (j m e) -> p j m e", j=4, e=2),
+                in_=w1_raw[hg][:, kg, :].rearrange("p (m j e) -> p j m e", j=4, e=2),
+            )
+
+        def order_s1(hg):
             nc.vector.tensor_copy(
                 out=w1s[hg][:].rearrange("p g (j m) -> p g j m", j=4),
                 in_=s1_raw[:, :, G * hg : G * (hg + 1)].rearrange("p g (m j) -> p g j m", j=4),
@@ -107,10 +117,13 @@ def tile_deepsurvivalmachinesweibullriskcurves_x2_kernel(
         def front_bank():
             return psum.tile([P, G], F32, name="front", bufs=3)
 
+        def w_bank():
+            return psum.tile([P, G], F32, name="wbank", bufs=3)
+
         def turn_x(g, kg, sp):
             if ("xg", g, kg) not in st:
                 st["xg", g, kg] = work.tile([P, G, 4], BF16, name="xg", bufs=3, align_bytes=AL)
-            bank = front_bank()
+            bank = w_bank() if g < 2 else front_bank()
             words = x_sb[g][kg][:].bitcast(F32)
             for s in range(2):
                 for u in range(2):
@@ -151,21 +164,27 @@ def tile_deepsurvivalmachinesweibullriskcurves_x2_kernel(
 
         def relu_h(g, hg, j, eng):
             if ("h", g, hg) not in st:
-                st["h", g, hg] = work.tile([P, 4, G], BF16, name="h", bufs=2)
+                st["h", g, hg] = work.tile([P, 4, G], BF16, name="h", bufs=3)
             dst, src, b = st["h", g, hg][:, j, :], st["hb", g, hg, j][:], bias[:, hg, j : j + 1]
             if eng == "A":
                 nc.scalar.activation(out=dst, in_=src, func=ACT.Relu, bias=b)
             else:
                 nc.vector.tensor_scalar(out=dst, in0=src, scalar1=b, scalar2=0.0, op0=ALU.add, op1=ALU.max)
 
-        def lay_h(g, hg):
-            laid = work.tile([P, G, 4], BF16, name="h_laid", bufs=2, align_bytes=AL)
-            nc.vector.tensor_copy(out=laid[:], in_=st["h", g, hg][:].rearrange("p j n -> p n j"))
-            st["hl", g, hg] = laid
+        def lay_h(g, hg, half, eng):
+            if ("hl", g, hg) not in st:
+                st["hl", g, hg] = work.tile([P, G, 4], BF16, name="h_laid", bufs=2, align_bytes=AL)
+            cols = slice(256 * half, 256 * (half + 1))
+            dst = st["hl", g, hg][:, cols, :].rearrange("p (c i) j -> p c j i", i=4)
+            src = st["h", g, hg][:, :, cols].rearrange("p j (c i) -> p c j i", i=4)
+            if eng == "P":
+                nc.gpsimd.tensor_scalar(out=dst, in0=src, scalar1=1.0, scalar2=0.0, op0=ALU.mult, op1=ALU.add)
+            else:
+                move(eng, dst, src)
 
         def quant_h(g, hg):
-            codes = work.tile([P, G], U32, name="hc", bufs=2, align_bytes=AL)
-            scales = work.tile([P, G], U8, name="hs", bufs=2, align_bytes=AL)
+            codes = work.tile([P, G], U32, name="hc", bufs=3, align_bytes=AL)
+            scales = work.tile([P, G], U8, name="hs", bufs=3, align_bytes=AL)
             nc.vector.quantize_mx(
                 out=codes[:].bitcast(FP8X4), scales=scales[:], in_=st["hl", g, hg][:].rearrange("p n j -> p (n j)")
             )
@@ -189,12 +208,17 @@ def tile_deepsurvivalmachinesweibullriskcurves_x2_kernel(
         def shape_k(g):
             ths = work.tile([P, G], F32, name="ths", bufs=1)
             nc.scalar.activation(out=ths[:], in_=st["head_bank", g, 0][:], func=ACT.Tanh)
+            st["ths", g] = ths
+
+        def log_scale(g):
             lsc = work.tile([P, G], F32, name="lsc", bufs=1)
             nc.scalar.activation(out=lsc[:], in_=st["head_bank", g, 1][:], func=ACT.Tanh)
-            k = work.tile([P, G], F32, name="k", bufs=2)
-            nc.scalar.activation(out=k[:], in_=ths[:], func=ACT.Exp, scale=0.5)
-            st["k", g] = k
             st["l", g] = lsc
+
+        def exp_k(g):
+            k = work.tile([P, G], F32, name="k", bufs=2)
+            nc.scalar.activation(out=k[:], in_=st["ths", g][:], func=ACT.Exp, scale=0.5)
+            st["k", g] = k
 
         def neg_p(g, eng):
             negp = work.tile([P, G], F32, name="negp", bufs=2)
@@ -226,8 +250,10 @@ def tile_deepsurvivalmachinesweibullriskcurves_x2_kernel(
             nc.vector.tensor_reduce(
                 out=w0[:, 0, :], in_=st["p0", g][:].rearrange("p (c m) -> p c m", m=M), axis=AX.X, op=ALU.min
             )
-            nc.gpsimd.tensor_copy(out=w0[:, 1, :], in_=w0[:, 0, :])
             st["w0", g] = w0
+
+        def dup_p(g):
+            nc.gpsimd.tensor_copy(out=st["w0", g][:, 1, :], in_=st["w0", g][:, 0, :])
 
         def sub_p(g):
             z0 = work.tile([P, M, SR], F32, name="z0", bufs=1)
@@ -265,21 +291,21 @@ def tile_deepsurvivalmachinesweibullriskcurves_x2_kernel(
             move(eng, norm[g][:].rearrange("p d c -> p (d c)"), st["s0", g][:, 0 : 2 * P])
 
         def power(g, i):
-            e = work.tile([P, G], F32, name="pow", bufs=3)
+            e = work.tile([P, G], F32, name="pow", bufs=4)
             nc.scalar.activation(out=e[:], in_=st["k", g][:], func=ACT.Exp, scale=logt[:, i : i + 1])
             st["E", g, i] = e
 
         def hazard(g, i, eng):
-            cum = work.tile([P, G], F32, name="cum", bufs=3)
+            cum = work.tile([P, G], F32, name="cum", bufs=4)
             (nc.vector if eng == "V" else nc.gpsimd).tensor_tensor(out=cum[:], in0=st["E", g, i][:], in1=st["A", g][:], op=ALU.mult)
             st["cum", g, i] = cum
 
-        def turn_w(g, i):
-            bank = psum.tile([P, G], F32, name="wbank", bufs=3)
+        def turn_w(g, i, eng):
+            bank = w_bank()
             for s in range(4):
                 cols = slice(P * s, P * (s + 1))
                 nc.tensor.matmul(bank[:, cols], st["cum", g, i][:, cols], ident[:], start=True, stop=False, is_transpose=True)
-                nc.tensor.matmul(bank[:, cols], st["np", g][:, cols], ident[:], start=False, stop=True, is_transpose=True)
+                nc.tensor.matmul(bank[:, cols], st["np", g][:, cols], ident[:], start=False, stop=True, is_transpose=(eng == "T" or s > 0))
             st["w", g, i] = bank
 
         def min_w(g, i):
@@ -288,7 +314,7 @@ def tile_deepsurvivalmachinesweibullriskcurves_x2_kernel(
             )
 
         def sub_w(g, i):
-            if i % 2 == 0:
+            if ("z", g, i // 2) not in st:
                 st["z", g, i // 2] = work.tile([P, M, 2, SR], F32, name="z", bufs=3)
             nc.vector.tensor_tensor(
                 out=st["z", g, i // 2][:, :, i % 2, :],
@@ -305,7 +331,7 @@ def tile_deepsurvivalmachinesweibullriskcurves_x2_kernel(
             st["e", g, q] = e
 
         def sum_w(g, q):
-            if q == 0:
+            if ("s", g) not in st:
                 st["s", g] = psum.tile([P, G], F32, name="sbank", bufs=1)
             for m in range(M):
                 nc.tensor.matmul(
@@ -316,25 +342,28 @@ def tile_deepsurvivalmachinesweibullriskcurves_x2_kernel(
         def keep_sums(g, eng):
             move(eng, sums[g][:].rearrange("p q c -> p (q c)"), st["s", g][:])
 
-        def logs(g):
+        def log_norm(g):
             ln0 = work.tile([P, P], F32, name="ln0", bufs=4)
             nc.scalar.activation(out=ln0[:], in_=norm[g][:, 0, :], func=ACT.Ln)
+            st["ln0", g] = ln0
+
+        def logs(g):
             lns = work.tile([P, G], F32, name="lns", bufs=4)
             src = st["s", g][:] if g == GROUPS - 1 else sums[g][:].rearrange("p q c -> p (q c)")
             nc.scalar.activation(out=lns[:], in_=src, func=ACT.Ln)
-            st["ln", g] = (ln0, lns)
+            st["ln", g] = lns
 
-        def offset(g):
+        def offset(g, eng):
             c0 = work.tile([P, P], F32, name="c0", bufs=4)
-            nc.vector.tensor_tensor(out=c0[:], in0=norm[g][:, 1, :], in1=st["ln", g][0][:], op=ALU.subtract)
+            (nc.vector if eng == "V" else nc.gpsimd).tensor_tensor(out=c0[:], in0=norm[g][:, 1, :], in1=st["ln0", g][:], op=ALU.subtract)
             st["c0", g] = c0
 
-        def turn_back(g):
+        def turn_back(g, eng):
             bank = front_bank()
             for q in range(4):
                 cols = slice(P * q, P * (q + 1))
-                nc.tensor.matmul(bank[:, cols], st["ln", g][1][:, cols], ident[:], start=True, stop=False, is_transpose=True)
-                nc.tensor.matmul(bank[:, cols], st["c0", g][:], ident[:], start=False, stop=True, is_transpose=True)
+                nc.tensor.matmul(bank[:, cols], st["ln", g][:, cols], ident[:], start=True, stop=False, is_transpose=True)
+                nc.tensor.matmul(bank[:, cols], st["c0", g][:], ident[:], start=False, stop=True, is_transpose=(eng == "T" or q > 0))
             st["fin", g] = bank
 
         def result(g):
@@ -354,10 +383,10 @@ def tile_deepsurvivalmachinesweibullriskcurves_x2_kernel(
         def lay_out(g, eng):
             laid = work.tile([P, P, 4], BF16, name="out_laid", bufs=4, align_bytes=AL)
             src = st["res", g][:].rearrange("p (s r) i -> p (r i) s", s=4)
-            if eng == "A":
-                nc.scalar.copy(out=laid[:], in_=src)
+            if eng == "P":
+                nc.gpsimd.tensor_scalar(out=laid[:], in0=src, scalar1=1.0, scalar2=0.0, op0=ALU.mult, op1=ALU.add)
             else:
-                nc.vector.tensor_copy(out=laid[:], in_=src)
+                move(eng, laid[:], src)
             st["ol", g] = laid
 
         def quant_out(g):
@@ -372,405 +401,445 @@ def tile_deepsurvivalmachinesweibullriskcurves_x2_kernel(
         def at(when, fn, *args):
             plan.append((when, len(plan), fn, args))
 
-        at(0, order_w1, 1)
-        at(1, turn_x, 0, 0, 1)
-        at(2, turn_x, 0, 0, 0)
-        at(3, copy_x, 0, 0, 0, "A")
-        at(4, turn_x, 0, 1, 1)
-        at(5, copy_x, 0, 0, 1, "A")
-        at(6, quant_x, 0, 0)
-        at(7, copy_x, 0, 1, 1, "A")
-        at(8, order_w1, 0)
-        at(9, turn_x, 0, 1, 0)
-        at(10, copy_x, 0, 1, 0, "A")
-        at(11, quant_x, 0, 1)
-        at(12, layer1, 0, 0, 2)
-        at(13, layer1, 0, 0, 0)
-        at(14, layer1, 0, 0, 1)
-        at(15, lay_head, 0)
-        at(16, relu_h, 0, 0, 2, "A")
-        at(17, lay_head, 2)
-        at(18, relu_h, 0, 0, 0, "A")
-        at(19, lay_head, 1)
-        at(20, quant_head, 0)
-        at(21, layer1, 0, 0, 3)
-        at(22, relu_h, 0, 0, 1, "A")
-        at(23, layer1, 0, 1, 3)
-        at(24, layer1, 0, 1, 1)
-        at(25, relu_h, 0, 0, 3, "V")
-        at(26, relu_h, 0, 1, 3, "A")
-        at(27, relu_h, 0, 1, 1, "A")
-        at(28, lay_h, 0, 0)
-        at(29, layer1, 0, 1, 0)
-        at(30, relu_h, 0, 1, 0, "V")
-        at(31, layer1, 0, 1, 2)
-        at(32, relu_h, 0, 1, 2, "A")
-        at(33, turn_x, 1, 0, 1)
-        at(34, quant_head, 2)
-        at(35, lay_h, 0, 1)
-        at(36, turn_x, 1, 0, 0)
-        at(37, copy_x, 1, 0, 1, "A")
-        at(38, quant_h, 0, 0)
-        at(39, copy_x, 1, 0, 0, "A")
-        at(40, turn_x, 1, 1, 0)
-        at(41, turn_x, 1, 1, 1)
-        at(42, quant_h, 0, 1)
-        at(43, copy_x, 1, 1, 0, "A")
-        at(44, head, 0, 2)
+        at(0, warm_pe, 8)
+        at(1, warm_pe, 4)
+        at(2, turn_x, 0, 0, 1)
+        at(3, warm_pe, 7)
+        at(4, warm_pe, 3)
+        at(5, turn_x, 0, 0, 0)
+        at(6, turn_x, 0, 1, 1)
+        at(7, order_s1, 0)
+        at(8, order_w1, 0, 0)
+        at(9, copy_x, 0, 0, 1, "A")
+        at(10, order_w1, 0, 1)
+        at(11, warm_pe, 5)
+        at(12, order_s1, 1)
+        at(13, order_w1, 1, 1)
+        at(14, copy_x, 0, 0, 0, "A")
+        at(15, turn_x, 0, 1, 0)
+        at(16, copy_x, 0, 1, 1, "A")
+        at(17, quant_x, 0, 0)
+        at(18, warm_pe, 9)
+        at(19, copy_x, 0, 1, 0, "A")
+        at(20, quant_x, 0, 1)
+        at(21, turn_x, 1, 0, 0)
+        at(22, copy_x, 1, 0, 0, "A")
+        at(23, layer1, 0, 0, 1)
+        at(24, order_w1, 1, 0)
+        at(25, layer1, 0, 0, 0)
+        at(26, relu_h, 0, 0, 1, "A")
+        at(27, relu_h, 0, 0, 0, "A")
+        at(28, layer1, 0, 0, 2)
+        at(29, relu_h, 0, 0, 2, "A")
+        at(30, layer1, 0, 0, 3)
+        at(31, relu_h, 0, 0, 3, "A")
+        at(32, layer1, 0, 1, 0)
+        at(33, relu_h, 0, 1, 0, "A")
+        at(34, layer1, 0, 1, 3)
+        at(35, layer1, 0, 1, 2)
+        at(36, relu_h, 0, 1, 3, "A")
+        at(37, lay_head, 1)
+        at(38, relu_h, 0, 1, 2, "A")
+        at(39, layer1, 0, 1, 1)
+        at(40, lay_head, 0)
+        at(41, turn_x, 1, 0, 1)
+        at(42, relu_h, 0, 1, 1, "A")
+        at(43, turn_x, 2, 0, 0)
+        at(44, copy_x, 2, 0, 0, "A")
         at(45, quant_head, 1)
-        at(46, copy_x, 1, 1, 1, "A")
-        at(47, quant_x, 1, 0)
-        at(48, head, 0, 0)
-        at(49, head, 0, 1)
-        at(50, quant_x, 1, 1)
-        at(51, neg_p, 0, "A")
-        at(52, layer1, 1, 0, 1)
-        at(53, shape_k, 0)
-        at(54, relu_h, 1, 0, 1, "V")
-        at(55, layer1, 1, 0, 0)
-        at(56, turn_p, 0)
-        at(57, relu_h, 1, 0, 0, "A")
-        at(58, layer1, 1, 0, 2)
-        at(59, k_times_l, 0, "V")
-        at(60, power, 0, 0)
-        at(61, min_p, 0)
-        at(62, sub_p, 0)
-        at(63, amp, 0)
-        at(64, relu_h, 1, 0, 2, "V")
-        at(65, layer1, 1, 0, 3)
-        at(66, power, 0, 1)
-        at(67, layer1, 1, 1, 1)
-        at(68, layer1, 1, 1, 3)
-        at(69, hazard, 0, 0, "P")
-        at(70, relu_h, 1, 0, 3, "A")
-        at(71, exp_p, 0)
-        at(72, power, 0, 2)
-        at(73, layer1, 1, 1, 0)
-        at(74, turn_w, 0, 0)
-        at(75, hazard, 0, 1, "V")
-        at(76, power, 0, 3)
-        at(77, relu_h, 1, 1, 0, "A")
-        at(78, lay_h, 1, 0)
-        at(79, sum_p, 0)
-        at(80, min_w, 0, 0)
-        at(81, turn_w, 0, 1)
-        at(82, hazard, 0, 2, "P")
-        at(83, relu_h, 1, 1, 1, "A")
-        at(84, layer1, 1, 1, 2)
-        at(85, power, 0, 4)
-        at(86, relu_h, 1, 1, 2, "A")
-        at(87, relu_h, 1, 1, 3, "V")
-        at(88, sub_w, 0, 0)
-        at(89, min_w, 0, 1)
-        at(90, turn_w, 0, 2)
-        at(91, hazard, 0, 3, "P")
-        at(92, turn_x, 2, 0, 0)
-        at(93, power, 0, 5)
-        at(94, turn_x, 2, 1, 0)
-        at(95, sub_w, 0, 1)
-        at(96, min_w, 0, 2)
-        at(97, turn_w, 0, 3)
-        at(98, lay_h, 1, 1)
-        at(99, turn_x, 2, 0, 1)
-        at(100, copy_x, 2, 0, 0, "A")
-        at(101, quant_h, 1, 0)
-        at(102, hazard, 0, 4, "P")
-        at(103, copy_x, 2, 1, 0, "A")
-        at(104, exp_w, 0, 0)
-        at(105, power, 0, 6)
-        at(106, turn_x, 2, 1, 1)
-        at(107, quant_h, 1, 1)
-        at(108, copy_x, 2, 0, 1, "A")
-        at(109, sub_w, 0, 2)
-        at(110, copy_x, 2, 1, 1, "A")
-        at(111, min_w, 0, 3)
-        at(112, turn_w, 0, 4)
-        at(113, head, 1, 2)
-        at(114, keep_norm, 0, "V")
-        at(115, head, 1, 0)
-        at(116, hazard, 0, 5, "V")
-        at(117, head, 1, 1)
-        at(118, neg_p, 1, "A")
-        at(119, power, 0, 7)
-        at(120, turn_p, 1)
-        at(121, quant_x, 2, 0)
-        at(122, sum_w, 0, 0)
-        at(123, sub_w, 0, 3)
-        at(124, min_w, 0, 4)
-        at(125, turn_w, 0, 5)
-        at(126, shape_k, 1)
-        at(127, hazard, 0, 6, "P")
-        at(128, exp_w, 0, 1)
-        at(129, power, 1, 0)
-        at(130, quant_x, 2, 1)
-        at(131, k_times_l, 1, "P")
-        at(132, sub_w, 0, 4)
-        at(133, amp, 1)
-        at(134, min_w, 0, 5)
-        at(135, turn_w, 0, 6)
-        at(136, layer1, 2, 0, 1)
-        at(137, hazard, 0, 7, "P")
-        at(138, relu_h, 2, 0, 1, "A")
-        at(139, layer1, 2, 0, 3)
-        at(140, layer1, 2, 0, 0)
-        at(141, power, 1, 1)
-        at(142, min_p, 1)
-        at(143, sum_w, 0, 1)
-        at(144, sub_w, 0, 5)
-        at(145, min_w, 0, 6)
-        at(146, turn_w, 0, 7)
-        at(147, sub_p, 1)
-        at(148, layer1, 2, 0, 2)
-        at(149, hazard, 1, 0, "P")
-        at(150, relu_h, 2, 0, 3, "A")
-        at(151, exp_w, 0, 2)
-        at(152, layer1, 2, 1, 3)
-        at(153, power, 1, 2)
-        at(154, relu_h, 2, 0, 2, "A")
-        at(155, sub_w, 0, 6)
-        at(156, min_w, 0, 7)
-        at(157, turn_w, 1, 0)
-        at(158, hazard, 1, 1, "V")
-        at(159, relu_h, 2, 1, 3, "A")
-        at(160, relu_h, 2, 0, 0, "V")
-        at(161, power, 1, 3)
-        at(162, sum_w, 0, 2)
-        at(163, sub_w, 0, 7)
-        at(164, layer1, 2, 1, 1)
-        at(165, min_w, 1, 0)
-        at(166, turn_w, 1, 1)
-        at(167, hazard, 1, 2, "P")
-        at(168, layer1, 2, 1, 2)
-        at(169, exp_w, 0, 3)
-        at(170, power, 1, 4)
-        at(171, lay_h, 2, 0)
-        at(172, relu_h, 2, 1, 1, "A")
-        at(173, layer1, 2, 1, 0)
-        at(174, sub_w, 1, 0)
-        at(175, min_w, 1, 1)
-        at(176, turn_w, 1, 2)
-        at(177, relu_h, 2, 1, 2, "A")
-        at(178, hazard, 1, 3, "P")
-        at(179, relu_h, 2, 1, 0, "V")
-        at(180, turn_x, 3, 0, 0)
-        at(181, power, 1, 5)
-        at(182, sum_w, 0, 3)
-        at(183, turn_x, 3, 1, 0)
-        at(184, sub_w, 1, 1)
-        at(185, min_w, 1, 2)
-        at(186, turn_w, 1, 3)
-        at(187, turn_x, 3, 0, 1)
-        at(188, exp_p, 1)
-        at(189, copy_x, 3, 0, 0, "A")
-        at(190, hazard, 1, 4, "P")
-        at(191, copy_x, 3, 1, 0, "A")
-        at(192, exp_w, 1, 0)
-        at(193, lay_h, 2, 1)
-        at(194, power, 1, 6)
-        at(195, turn_x, 3, 1, 1)
-        at(196, quant_h, 2, 0)
-        at(197, quant_h, 2, 1)
-        at(198, sum_p, 1)
-        at(199, copy_x, 3, 0, 1, "A")
-        at(200, sub_w, 1, 2)
-        at(201, keep_sums, 0, "V")
-        at(202, copy_x, 3, 1, 1, "A")
-        at(203, min_w, 1, 3)
-        at(204, turn_w, 1, 4)
-        at(205, keep_norm, 1, "V")
-        at(206, hazard, 1, 5, "V")
-        at(207, head, 2, 2)
-        at(208, head, 2, 0)
-        at(209, head, 2, 1)
-        at(210, power, 1, 7)
-        at(211, neg_p, 2, "A")
-        at(212, quant_x, 3, 0)
-        at(213, sum_w, 1, 0)
-        at(214, sub_w, 1, 3)
-        at(215, min_w, 1, 4)
-        at(216, turn_w, 1, 5)
-        at(217, shape_k, 2)
-        at(218, hazard, 1, 6, "P")
-        at(219, exp_w, 1, 1)
-        at(220, k_times_l, 2, "P")
-        at(221, turn_p, 2)
-        at(222, power, 2, 0)
-        at(223, quant_x, 3, 1)
-        at(224, sub_w, 1, 4)
-        at(225, min_w, 1, 5)
-        at(226, turn_w, 1, 6)
-        at(227, layer1, 3, 0, 1)
-        at(228, hazard, 1, 7, "P")
-        at(229, relu_h, 3, 0, 1, "A")
-        at(230, layer1, 3, 0, 3)
-        at(231, min_p, 2)
-        at(232, layer1, 3, 0, 0)
-        at(233, power, 2, 1)
-        at(234, sum_w, 1, 1)
-        at(235, amp, 2)
-        at(236, sub_w, 1, 5)
-        at(237, min_w, 1, 6)
-        at(238, turn_w, 1, 7)
-        at(239, layer1, 3, 0, 2)
-        at(240, hazard, 2, 0, "P")
-        at(241, relu_h, 3, 0, 3, "A")
-        at(242, exp_w, 1, 2)
-        at(243, layer1, 3, 1, 3)
-        at(244, power, 2, 2)
-        at(245, relu_h, 3, 0, 2, "A")
-        at(246, sub_p, 2)
-        at(247, sub_w, 1, 6)
-        at(248, min_w, 1, 7)
-        at(249, turn_w, 2, 0)
-        at(250, hazard, 2, 1, "V")
-        at(251, relu_h, 3, 1, 3, "A")
-        at(252, relu_h, 3, 0, 0, "V")
-        at(253, power, 2, 3)
-        at(254, sum_w, 1, 2)
-        at(255, exp_p, 2)
-        at(256, sub_w, 1, 7)
-        at(257, layer1, 3, 1, 1)
-        at(258, min_w, 2, 0)
-        at(259, turn_w, 2, 1)
-        at(260, hazard, 2, 2, "P")
-        at(261, layer1, 3, 1, 2)
-        at(262, exp_w, 1, 3)
-        at(263, power, 2, 4)
-        at(264, lay_h, 3, 0)
-        at(265, relu_h, 3, 1, 1, "A")
-        at(266, layer1, 3, 1, 0)
-        at(267, sub_w, 2, 0)
-        at(268, min_w, 2, 1)
-        at(269, turn_w, 2, 2)
-        at(270, relu_h, 3, 1, 2, "A")
-        at(271, hazard, 2, 3, "P")
-        at(272, relu_h, 3, 1, 0, "V")
-        at(273, power, 2, 5)
-        at(274, sum_w, 1, 3)
-        at(275, sub_w, 2, 1)
-        at(276, min_w, 2, 2)
-        at(277, turn_w, 2, 3)
-        at(278, keep_sums, 1, "A")
-        at(279, hazard, 2, 4, "P")
-        at(280, exp_w, 2, 0)
-        at(281, lay_h, 3, 1)
-        at(282, power, 2, 6)
-        at(283, quant_h, 3, 0)
-        at(284, quant_h, 3, 1)
-        at(285, sub_w, 2, 2)
-        at(286, min_w, 2, 3)
-        at(287, turn_w, 2, 4)
-        at(288, sum_p, 2)
-        at(289, hazard, 2, 5, "V")
-        at(290, head, 3, 2)
-        at(291, head, 3, 0)
-        at(292, head, 3, 1)
-        at(293, power, 2, 7)
-        at(294, neg_p, 3, "A")
-        at(295, sum_w, 2, 0)
-        at(296, sub_w, 2, 3)
-        at(297, min_w, 2, 4)
-        at(298, turn_w, 2, 5)
-        at(299, shape_k, 3)
-        at(300, hazard, 2, 6, "P")
-        at(301, exp_w, 2, 1)
-        at(302, keep_norm, 2, "V")
-        at(303, k_times_l, 3, "P")
-        at(304, turn_p, 3)
-        at(305, power, 3, 0)
-        at(306, sub_w, 2, 4)
-        at(307, min_w, 2, 5)
-        at(308, turn_w, 2, 6)
-        at(309, hazard, 2, 7, "P")
-        at(310, min_p, 3)
-        at(311, power, 3, 1)
-        at(312, sum_w, 2, 1)
-        at(313, amp, 3)
-        at(314, sub_w, 2, 5)
-        at(315, min_w, 2, 6)
-        at(316, turn_w, 2, 7)
-        at(317, hazard, 3, 0, "P")
-        at(318, exp_w, 2, 2)
-        at(319, power, 3, 2)
-        at(320, sub_p, 3)
-        at(321, sub_w, 2, 6)
-        at(322, min_w, 2, 7)
-        at(323, turn_w, 3, 0)
-        at(324, hazard, 3, 1, "P")
-        at(325, power, 3, 3)
-        at(326, sum_w, 2, 2)
-        at(327, exp_p, 3)
-        at(328, sub_w, 2, 7)
-        at(329, min_w, 3, 0)
-        at(330, turn_w, 3, 1)
-        at(331, hazard, 3, 2, "P")
-        at(332, exp_w, 2, 3)
-        at(333, power, 3, 4)
-        at(334, sub_w, 3, 0)
-        at(335, min_w, 3, 1)
-        at(336, turn_w, 3, 2)
-        at(337, hazard, 3, 3, "P")
-        at(338, power, 3, 5)
-        at(339, sum_w, 2, 3)
-        at(340, sub_w, 3, 1)
-        at(341, min_w, 3, 2)
-        at(342, turn_w, 3, 3)
-        at(343, hazard, 3, 4, "P")
-        at(344, exp_w, 3, 0)
-        at(345, keep_sums, 2, "A")
-        at(346, power, 3, 6)
-        at(347, sub_w, 3, 2)
-        at(348, min_w, 3, 3)
-        at(349, turn_w, 3, 4)
-        at(350, sum_p, 3)
-        at(351, hazard, 3, 5, "P")
-        at(352, power, 3, 7)
-        at(353, sum_w, 3, 0)
-        at(354, sub_w, 3, 3)
-        at(355, min_w, 3, 4)
-        at(356, turn_w, 3, 5)
-        at(357, hazard, 3, 6, "P")
-        at(358, exp_w, 3, 1)
-        at(359, keep_norm, 3, "V")
-        at(360, sub_w, 3, 4)
-        at(361, min_w, 3, 5)
-        at(362, turn_w, 3, 6)
-        at(363, hazard, 3, 7, "P")
-        at(364, logs, 0)
-        at(365, sum_w, 3, 1)
-        at(366, sub_w, 3, 5)
-        at(367, min_w, 3, 6)
-        at(368, turn_w, 3, 7)
-        at(369, exp_w, 3, 2)
-        at(370, offset, 0)
-        at(371, sub_w, 3, 6)
-        at(372, min_w, 3, 7)
-        at(373, sum_w, 3, 2)
-        at(374, sub_w, 3, 7)
-        at(375, exp_w, 3, 3)
-        at(376, logs, 2)
-        at(377, sum_w, 3, 3)
-        at(378, logs, 3)
-        at(379, offset, 2)
-        at(380, turn_back, 0)
-        at(381, result, 0)
-        at(382, logs, 1)
-        at(383, offset, 3)
-        at(384, turn_back, 2)
-        at(385, lay_out, 0, "A")
-        at(386, turn_back, 3)
-        at(387, result, 2)
-        at(388, offset, 1)
-        at(389, lay_out, 2, "A")
-        at(390, result, 3)
-        at(391, turn_back, 1)
-        at(392, quant_out, 2)
-        at(393, result, 1)
-        at(394, quant_out, 0)
-        at(395, lay_out, 3, "A")
-        at(396, lay_out, 1, "V")
-        at(397, quant_out, 3)
-        at(398, quant_out, 1)
+        at(46, lay_head, 2)
+        at(47, quant_head, 0)
+        at(48, lay_h, 0, 0, 0, "V")
+        at(49, warm_pe, 0)
+        at(50, lay_h, 0, 0, 1, "V")
+        at(51, quant_h, 0, 0)
+        at(52, copy_x, 1, 0, 1, "A")
+        at(53, lay_h, 0, 1, 1, "V")
+        at(54, lay_h, 0, 1, 0, "V")
+        at(55, turn_x, 1, 1, 0)
+        at(56, quant_h, 0, 1)
+        at(57, copy_x, 1, 1, 0, "A")
+        at(58, turn_x, 1, 1, 1)
+        at(59, turn_x, 2, 0, 1)
+        at(60, quant_x, 1, 0)
+        at(61, copy_x, 1, 1, 1, "A")
+        at(62, quant_x, 1, 1)
+        at(63, head, 0, 0)
+        at(64, head, 0, 1)
+        at(65, copy_x, 2, 0, 1, "A")
+        at(66, shape_k, 0)
+        at(67, log_scale, 0)
+        at(68, layer1, 1, 1, 1)
+        at(69, quant_x, 2, 0)
+        at(70, quant_head, 2)
+        at(71, exp_k, 0)
+        at(72, layer1, 1, 1, 3)
+        at(73, relu_h, 1, 1, 1, "V")
+        at(74, relu_h, 1, 1, 3, "A")
+        at(75, layer1, 1, 0, 2)
+        at(76, power, 0, 0)
+        at(77, layer1, 1, 1, 0)
+        at(78, k_times_l, 0, "V")
+        at(79, layer1, 1, 1, 2)
+        at(80, amp, 0)
+        at(81, relu_h, 1, 1, 0, "A")
+        at(82, relu_h, 1, 0, 2, "V")
+        at(83, head, 0, 2)
+        at(84, power, 0, 5)
+        at(85, power, 0, 1)
+        at(86, layer1, 1, 0, 3)
+        at(87, relu_h, 1, 1, 2, "V")
+        at(88, neg_p, 0, "V")
+        at(89, layer1, 1, 0, 0)
+        at(90, layer1, 1, 0, 1)
+        at(91, hazard, 0, 0, "P")
+        at(92, relu_h, 1, 0, 3, "A")
+        at(93, turn_x, 2, 1, 0)
+        at(94, power, 0, 3)
+        at(95, lay_h, 1, 1, 0, "V")
+        at(96, hazard, 0, 5, "V")
+        at(97, turn_p, 0)
+        at(98, hazard, 0, 1, "V")
+        at(99, turn_w, 0, 1, "T")
+        at(100, relu_h, 1, 0, 0, "A")
+        at(101, relu_h, 1, 0, 1, "A")
+        at(102, lay_h, 1, 1, 1, "V")
+        at(103, turn_w, 0, 0, "M")
+        at(104, turn_x, 2, 1, 1)
+        at(105, turn_x, 3, 1, 1)
+        at(106, power, 0, 4)
+        at(107, copy_x, 2, 1, 0, "A")
+        at(108, hazard, 0, 3, "V")
+        at(109, min_w, 0, 1)
+        at(110, power, 0, 6)
+        at(111, lay_h, 1, 0, 0, "P")
+        at(112, copy_x, 2, 1, 1, "A")
+        at(113, warm_pe, 1)
+        at(114, copy_x, 3, 1, 1, "A")
+        at(115, turn_w, 0, 3, "T")
+        at(116, sub_w, 0, 1)
+        at(117, power, 0, 2)
+        at(118, min_w, 0, 0)
+        at(119, sub_w, 0, 0)
+        at(120, quant_x, 2, 1)
+        at(121, exp_w, 0, 0)
+        at(122, turn_w, 0, 5, "T")
+        at(123, layer1, 2, 0, 2)
+        at(124, warm_pe, 11)
+        at(125, power, 0, 7)
+        at(126, hazard, 0, 4, "P")
+        at(127, lay_h, 1, 0, 1, "V")
+        at(128, layer1, 2, 0, 3)
+        at(129, relu_h, 2, 0, 2, "A")
+        at(130, relu_h, 2, 0, 3, "A")
+        at(131, quant_h, 1, 1)
+        at(132, quant_h, 1, 0)
+        at(133, layer1, 2, 1, 2)
+        at(134, head, 1, 0)
+        at(135, head, 1, 1)
+        at(136, min_w, 0, 3)
+        at(137, min_p, 0)
+        at(138, relu_h, 2, 1, 2, "A")
+        at(139, shape_k, 1)
+        at(140, sub_w, 0, 3)
+        at(141, layer1, 2, 0, 1)
+        at(142, hazard, 0, 7, "P")
+        at(143, log_scale, 1)
+        at(144, exp_k, 1)
+        at(145, sub_p, 0)
+        at(146, hazard, 0, 2, "V")
+        at(147, hazard, 0, 6, "P")
+        at(148, k_times_l, 1, "P")
+        at(149, layer1, 2, 0, 0)
+        at(150, head, 1, 2)
+        at(151, relu_h, 2, 0, 1, "A")
+        at(152, power, 1, 3)
+        at(153, neg_p, 1, "A")
+        at(154, turn_w, 0, 4, "T")
+        at(155, power, 1, 2)
+        at(156, min_w, 0, 5)
+        at(157, relu_h, 2, 0, 0, "V")
+        at(158, layer1, 2, 1, 1)
+        at(159, relu_h, 2, 1, 1, "A")
+        at(160, power, 1, 0)
+        at(161, amp, 1)
+        at(162, turn_w, 0, 2, "T")
+        at(163, sub_w, 0, 5)
+        at(164, turn_x, 3, 1, 0)
+        at(165, turn_w, 0, 7, "T")
+        at(166, layer1, 2, 1, 3)
+        at(167, min_w, 0, 4)
+        at(168, dup_p, 0)
+        at(169, power, 1, 5)
+        at(170, min_w, 0, 2)
+        at(171, layer1, 2, 1, 0)
+        at(172, sub_w, 0, 4)
+        at(173, exp_p, 0)
+        at(174, turn_w, 0, 6, "T")
+        at(175, sum_p, 0)
+        at(176, min_w, 0, 7)
+        at(177, relu_h, 2, 1, 3, "V")
+        at(178, sub_w, 0, 2)
+        at(179, lay_h, 2, 0, 1, "P")
+        at(180, relu_h, 2, 1, 0, "A")
+        at(181, warm_pe, 10)
+        at(182, sub_w, 0, 7)
+        at(183, min_w, 0, 6)
+        at(184, exp_w, 0, 2)
+        at(185, copy_x, 3, 1, 0, "A")
+        at(186, lay_h, 2, 0, 0, "P")
+        at(187, warm_pe, 2)
+        at(188, warm_pe, 6)
+        at(189, hazard, 1, 3, "P")
+        at(190, sum_w, 0, 0)
+        at(191, power, 1, 1)
+        at(192, turn_x, 3, 0, 1)
+        at(193, sub_w, 0, 6)
+        at(194, turn_x, 3, 0, 0)
+        at(195, sum_w, 0, 2)
+        at(196, exp_w, 0, 1)
+        at(197, keep_norm, 0, "V")
+        at(198, hazard, 1, 2, "V")
+        at(199, lay_h, 2, 1, 0, "V")
+        at(200, copy_x, 3, 0, 1, "A")
+        at(201, power, 1, 6)
+        at(202, copy_x, 3, 0, 0, "A")
+        at(203, quant_h, 2, 0)
+        at(204, turn_w, 1, 3, "T")
+        at(205, lay_h, 2, 1, 1, "P")
+        at(206, quant_h, 2, 1)
+        at(207, head, 2, 0)
+        at(208, head, 2, 1)
+        at(209, shape_k, 2)
+        at(210, exp_w, 0, 3)
+        at(211, log_scale, 2)
+        at(212, hazard, 1, 0, "V")
+        at(213, hazard, 1, 1, "V")
+        at(214, turn_w, 1, 0, "T")
+        at(215, quant_x, 3, 0)
+        at(216, turn_w, 1, 2, "T")
+        at(217, turn_p, 1)
+        at(218, exp_k, 2)
+        at(219, power, 1, 4)
+        at(220, quant_x, 3, 1)
+        at(221, hazard, 1, 5, "V")
+        at(222, layer1, 3, 0, 2)
+        at(223, layer1, 3, 0, 3)
+        at(224, relu_h, 3, 0, 2, "A")
+        at(225, layer1, 3, 0, 1)
+        at(226, layer1, 3, 0, 0)
+        at(227, min_p, 1)
+        at(228, min_w, 1, 3)
+        at(229, hazard, 1, 6, "P")
+        at(230, min_w, 1, 0)
+        at(231, relu_h, 3, 0, 3, "A")
+        at(232, power, 1, 7)
+        at(233, relu_h, 3, 0, 0, "A")
+        at(234, relu_h, 3, 0, 1, "A")
+        at(235, k_times_l, 2, "P")
+        at(236, sub_w, 1, 3)
+        at(237, amp, 2)
+        at(238, turn_w, 1, 1, "T")
+        at(239, sum_w, 0, 3)
+        at(240, hazard, 1, 4, "P")
+        at(241, layer1, 3, 1, 2)
+        at(242, power, 2, 0)
+        at(243, sum_w, 0, 1)
+        at(244, layer1, 3, 1, 0)
+        at(245, dup_p, 1)
+        at(246, relu_h, 3, 1, 2, "A")
+        at(247, sub_w, 1, 0)
+        at(248, hazard, 1, 7, "P")
+        at(249, layer1, 3, 1, 1)
+        at(250, min_w, 1, 2)
+        at(251, power, 2, 2)
+        at(252, sub_p, 1)
+        at(253, turn_w, 1, 4, "M")
+        at(254, power, 2, 3)
+        at(255, relu_h, 3, 1, 0, "A")
+        at(256, keep_sums, 0, "A")
+        at(257, exp_p, 1)
+        at(258, layer1, 3, 1, 3)
+        at(259, sub_w, 1, 2)
+        at(260, min_w, 1, 1)
+        at(261, lay_h, 3, 0, 1, "V")
+        at(262, exp_w, 1, 1)
+        at(263, lay_h, 3, 0, 0, "P")
+        at(264, turn_w, 1, 5, "T")
+        at(265, relu_h, 3, 1, 3, "A")
+        at(266, power, 2, 5)
+        at(267, sub_w, 1, 1)
+        at(268, turn_w, 1, 6, "M")
+        at(269, hazard, 2, 3, "P")
+        at(270, hazard, 2, 2, "P")
+        at(271, relu_h, 3, 1, 1, "V")
+        at(272, lay_h, 3, 1, 0, "P")
+        at(273, lay_h, 3, 1, 1, "P")
+        at(274, hazard, 2, 0, "V")
+        at(275, head, 2, 2)
+        at(276, quant_h, 3, 0)
+        at(277, min_w, 1, 4)
+        at(278, min_w, 1, 5)
+        at(279, sub_w, 1, 5)
+        at(280, power, 2, 1)
+        at(281, sum_w, 1, 1)
+        at(282, sub_w, 1, 4)
+        at(283, sum_p, 1)
+        at(284, turn_w, 1, 7, "M")
+        at(285, exp_w, 1, 2)
+        at(286, exp_w, 1, 0)
+        at(287, min_w, 1, 6)
+        at(288, neg_p, 2, "V")
+        at(289, turn_w, 2, 2, "M")
+        at(290, sub_w, 1, 6)
+        at(291, min_w, 1, 7)
+        at(292, keep_norm, 1, "V")
+        at(293, sum_w, 1, 2)
+        at(294, sub_w, 1, 7)
+        at(295, power, 2, 4)
+        at(296, hazard, 2, 4, "P")
+        at(297, quant_h, 3, 1)
+        at(298, power, 2, 6)
+        at(299, exp_w, 1, 3)
+        at(300, min_w, 2, 2)
+        at(301, turn_w, 2, 3, "M")
+        at(302, turn_p, 2)
+        at(303, head, 3, 0)
+        at(304, shape_k, 3)
+        at(305, head, 3, 1)
+        at(306, log_scale, 3)
+        at(307, min_w, 2, 3)
+        at(308, exp_k, 3)
+        at(309, hazard, 2, 5, "P")
+        at(310, sub_w, 2, 2)
+        at(311, hazard, 2, 1, "P")
+        at(312, power, 2, 7)
+        at(313, turn_w, 2, 0, "T")
+        at(314, sub_w, 2, 3)
+        at(315, min_p, 2)
+        at(316, sum_w, 1, 0)
+        at(317, min_w, 2, 0)
+        at(318, sub_p, 2)
+        at(319, exp_w, 2, 1)
+        at(320, k_times_l, 3, "P")
+        at(321, hazard, 2, 6, "P")
+        at(322, sub_w, 2, 0)
+        at(323, turn_w, 2, 4, "T")
+        at(324, min_w, 2, 4)
+        at(325, turn_w, 2, 5, "M")
+        at(326, power, 3, 0)
+        at(327, exp_p, 2)
+        at(328, power, 3, 1)
+        at(329, amp, 3)
+        at(330, power, 3, 5)
+        at(331, turn_w, 2, 1, "M")
+        at(332, min_w, 2, 5)
+        at(333, sum_w, 1, 3)
+        at(334, sub_w, 2, 4)
+        at(335, min_w, 2, 1)
+        at(336, hazard, 2, 7, "P")
+        at(337, sub_w, 2, 5)
+        at(338, sub_w, 2, 1)
+        at(339, keep_sums, 1, "V")
+        at(340, turn_w, 2, 6, "T")
+        at(341, min_w, 2, 6)
+        at(342, turn_w, 2, 7, "T")
+        at(343, head, 3, 2)
+        at(344, neg_p, 3, "V")
+        at(345, hazard, 3, 0, "P")
+        at(346, power, 3, 2)
+        at(347, exp_w, 2, 2)
+        at(348, min_w, 2, 7)
+        at(349, sub_w, 2, 6)
+        at(350, sum_w, 2, 1)
+        at(351, hazard, 3, 1, "P")
+        at(352, sum_w, 2, 2)
+        at(353, power, 3, 3)
+        at(354, exp_w, 2, 0)
+        at(355, power, 3, 4)
+        at(356, sub_w, 2, 7)
+        at(357, hazard, 3, 5, "P")
+        at(358, turn_w, 3, 0, "T")
+        at(359, power, 3, 7)
+        at(360, dup_p, 2)
+        at(361, turn_w, 3, 1, "T")
+        at(362, sum_p, 2)
+        at(363, hazard, 3, 2, "P")
+        at(364, turn_w, 3, 5, "M")
+        at(365, min_w, 3, 0)
+        at(366, exp_w, 2, 3)
+        at(367, min_w, 3, 1)
+        at(368, sum_w, 2, 0)
+        at(369, power, 3, 6)
+        at(370, log_norm, 0)
+        at(371, keep_norm, 2, "V")
+        at(372, sub_w, 3, 0)
+        at(373, logs, 0)
+        at(374, log_norm, 2)
+        at(375, log_norm, 1)
+        at(376, logs, 1)
+        at(377, min_w, 3, 5)
+        at(378, sub_w, 3, 1)
+        at(379, sum_w, 2, 3)
+        at(380, keep_sums, 2, "V")
+        at(381, turn_p, 3)
+        at(382, min_p, 3)
+        at(383, logs, 2)
+        at(384, hazard, 3, 4, "P")
+        at(385, hazard, 3, 3, "P")
+        at(386, turn_w, 3, 4, "T")
+        at(387, sub_w, 3, 5)
+        at(388, min_w, 3, 4)
+        at(389, turn_w, 3, 2, "T")
+        at(390, min_w, 3, 2)
+        at(391, sub_w, 3, 4)
+        at(392, sub_w, 3, 2)
+        at(393, turn_w, 3, 3, "M")
+        at(394, min_w, 3, 3)
+        at(395, hazard, 3, 6, "P")
+        at(396, offset, 1, "P")
+        at(397, turn_w, 3, 6, "M")
+        at(398, offset, 0, "P")
+        at(399, sub_p, 3)
+        at(400, hazard, 3, 7, "P")
+        at(401, turn_w, 3, 7, "T")
+        at(402, min_w, 3, 6)
+        at(403, turn_back, 1, "T")
+        at(404, exp_w, 3, 0)
+        at(405, exp_p, 3)
+        at(406, exp_w, 3, 2)
+        at(407, sum_w, 3, 0)
+        at(408, min_w, 3, 7)
+        at(409, sub_w, 3, 3)
+        at(410, turn_back, 0, "T")
+        at(411, sub_w, 3, 6)
+        at(412, sum_w, 3, 2)
+        at(413, sub_w, 3, 7)
+        at(414, offset, 2, "P")
+        at(415, result, 0)
+        at(416, dup_p, 3)
+        at(417, sum_p, 3)
+        at(418, exp_w, 3, 1)
+        at(419, exp_w, 3, 3)
+        at(420, keep_norm, 3, "V")
+        at(421, log_norm, 3)
+        at(422, sum_w, 3, 1)
+        at(423, result, 1)
+        at(424, lay_out, 0, "P")
+        at(425, sum_w, 3, 3)
+        at(426, turn_back, 2, "M")
+        at(427, offset, 3, "V")
+        at(428, logs, 3)
+        at(429, result, 2)
+        at(430, lay_out, 1, "A")
+        at(431, turn_back, 3, "T")
+        at(432, quant_out, 0)
+        at(433, lay_out, 2, "A")
+        at(434, result, 3)
+        at(435, quant_out, 1)
+        at(436, lay_out, 3, "V")
+        at(437, quant_out, 2)
+        at(438, quant_out, 3)
 
         for when, n, fn, args in sorted(plan, key=lambda e: e[0:2]):
             fn(*args)

@@ -178,6 +178,8 @@ def tile_deepsurvivalmachinesweibullriskcurves_x2_kernel(
             dst = st["hl", g, hg][:, cols, :].rearrange("p (c i) j -> p c j i", i=4)
             src = st["h", g, hg][:, :, cols].rearrange("p j (c i) -> p c j i", i=4)
             if eng == "P":
+                dst = st["hl", g, hg][:, cols, :]
+                src = st["h", g, hg][:, :, cols].rearrange("p j n -> p n j")
                 nc.gpsimd.tensor_scalar(out=dst, in0=src, scalar1=1.0, scalar2=0.0, op0=ALU.mult, op1=ALU.add)
             else:
                 move(eng, dst, src)
@@ -271,12 +273,13 @@ def tile_deepsurvivalmachinesweibullriskcurves_x2_kernel(
             nc.scalar.activation(out=e0[:, M, :], in_=st["z0", g][:, 0, :], func=ACT.Exp, scale=-1.0)
             st["e0", g] = e0
 
-        def sum_p(g):
+        def sum_p(g, eng):
             bank = psum.tile([P, G], F32, name="misc", bufs=1)
             e0 = st["e0", g][:].rearrange("p m c -> p (m c)")
             for m in range(M):
                 nc.tensor.matmul(
-                    bank[:, 0:P], e0[:, SR * m : SR * m + P], ident[:], start=(m == 0), stop=(m == M - 1), is_transpose=True
+                    bank[:, 0:P], e0[:, SR * m : SR * m + P], ident[:], start=(m == 0), stop=(m == M - 1),
+                    is_transpose=(m not in (1, 3)[: "TMN".index(eng)]),
                 )
             nc.tensor.transpose(bank[:, P : 2 * P], st["w0", g][:].rearrange("p d c -> p (d c)"), ident[:])
             st["s0", g] = bank
@@ -305,7 +308,7 @@ def tile_deepsurvivalmachinesweibullriskcurves_x2_kernel(
             for s in range(4):
                 cols = slice(P * s, P * (s + 1))
                 nc.tensor.matmul(bank[:, cols], st["cum", g, i][:, cols], ident[:], start=True, stop=False, is_transpose=True)
-                nc.tensor.matmul(bank[:, cols], st["np", g][:, cols], ident[:], start=False, stop=True, is_transpose=(eng == "T" or s > 0))
+                nc.tensor.matmul(bank[:, cols], st["np", g][:, cols], ident[:], start=False, stop=True, is_transpose=(s >= "TMN".index(eng)))
             st["w", g, i] = bank
 
         def min_w(g, i):
@@ -330,13 +333,13 @@ def tile_deepsurvivalmachinesweibullriskcurves_x2_kernel(
             )
             st["e", g, q] = e
 
-        def sum_w(g, q):
+        def sum_w(g, q, eng):
             if ("s", g) not in st:
                 st["s", g] = psum.tile([P, G], F32, name="sbank", bufs=1)
             for m in range(M):
                 nc.tensor.matmul(
                     st["s", g][:, P * q : P * (q + 1)], st["e", g, q][:, m, :], ident[:],
-                    start=(m == 0), stop=(m == M - 1), is_transpose=True,
+                    start=(m == 0), stop=(m == M - 1), is_transpose=(m not in (1, 3)[: "TMN".index(eng)]),
                 )
 
         def keep_sums(g, eng):
@@ -363,7 +366,7 @@ def tile_deepsurvivalmachinesweibullriskcurves_x2_kernel(
             for q in range(4):
                 cols = slice(P * q, P * (q + 1))
                 nc.tensor.matmul(bank[:, cols], st["ln", g][:, cols], ident[:], start=True, stop=False, is_transpose=True)
-                nc.tensor.matmul(bank[:, cols], st["c0", g][:], ident[:], start=False, stop=True, is_transpose=(eng == "T" or q > 0))
+                nc.tensor.matmul(bank[:, cols], st["c0", g][:], ident[:], start=False, stop=True, is_transpose=(q >= "TMN".index(eng)))
             st["fin", g] = bank
 
         def result(g):
@@ -401,442 +404,442 @@ def tile_deepsurvivalmachinesweibullriskcurves_x2_kernel(
         def at(when, fn, *args):
             plan.append((when, len(plan), fn, args))
 
-        at(0, warm_pe, 8)
-        at(1, warm_pe, 4)
-        at(2, turn_x, 0, 0, 1)
-        at(3, warm_pe, 7)
-        at(4, warm_pe, 3)
-        at(5, turn_x, 0, 0, 0)
-        at(6, turn_x, 0, 1, 1)
-        at(7, order_s1, 0)
-        at(8, order_w1, 0, 0)
-        at(9, copy_x, 0, 0, 1, "A")
-        at(10, order_w1, 0, 1)
-        at(11, warm_pe, 5)
-        at(12, order_s1, 1)
-        at(13, order_w1, 1, 1)
-        at(14, copy_x, 0, 0, 0, "A")
-        at(15, turn_x, 0, 1, 0)
-        at(16, copy_x, 0, 1, 1, "A")
-        at(17, quant_x, 0, 0)
-        at(18, warm_pe, 9)
-        at(19, copy_x, 0, 1, 0, "A")
-        at(20, quant_x, 0, 1)
-        at(21, turn_x, 1, 0, 0)
-        at(22, copy_x, 1, 0, 0, "A")
+        at(0, warm_pe, 3)
+        at(1, warm_pe, 5)
+        at(2, turn_x, 0, 0, 0)
+        at(3, warm_pe, 2)
+        at(4, warm_pe, 4)
+        at(5, order_w1, 0, 0)
+        at(6, copy_x, 0, 0, 0, "A")
+        at(7, turn_x, 0, 0, 1)
+        at(8, order_w1, 0, 1)
+        at(9, turn_x, 0, 1, 1)
+        at(10, turn_x, 0, 1, 0)
+        at(11, order_s1, 1)
+        at(12, copy_x, 0, 0, 1, "A")
+        at(13, order_s1, 0)
+        at(14, warm_pe, 1)
+        at(15, copy_x, 0, 1, 1, "A")
+        at(16, warm_pe, 7)
+        at(17, order_w1, 1, 0)
+        at(18, turn_x, 1, 0, 0)
+        at(19, quant_x, 0, 0)
+        at(20, copy_x, 0, 1, 0, "A")
+        at(21, copy_x, 1, 0, 0, "A")
+        at(22, quant_x, 0, 1)
         at(23, layer1, 0, 0, 1)
-        at(24, order_w1, 1, 0)
-        at(25, layer1, 0, 0, 0)
-        at(26, relu_h, 0, 0, 1, "A")
-        at(27, relu_h, 0, 0, 0, "A")
-        at(28, layer1, 0, 0, 2)
-        at(29, relu_h, 0, 0, 2, "A")
-        at(30, layer1, 0, 0, 3)
-        at(31, relu_h, 0, 0, 3, "A")
-        at(32, layer1, 0, 1, 0)
-        at(33, relu_h, 0, 1, 0, "A")
-        at(34, layer1, 0, 1, 3)
-        at(35, layer1, 0, 1, 2)
-        at(36, relu_h, 0, 1, 3, "A")
-        at(37, lay_head, 1)
-        at(38, relu_h, 0, 1, 2, "A")
+        at(24, layer1, 0, 0, 2)
+        at(25, relu_h, 0, 0, 1, "A")
+        at(26, relu_h, 0, 0, 2, "A")
+        at(27, layer1, 0, 0, 0)
+        at(28, relu_h, 0, 0, 0, "A")
+        at(29, layer1, 0, 0, 3)
+        at(30, relu_h, 0, 0, 3, "A")
+        at(31, order_w1, 1, 1)
+        at(32, layer1, 0, 1, 2)
+        at(33, relu_h, 0, 1, 2, "A")
+        at(34, layer1, 0, 1, 0)
+        at(35, layer1, 0, 1, 3)
+        at(36, lay_head, 0)
+        at(37, lay_head, 2)
+        at(38, relu_h, 0, 1, 0, "A")
         at(39, layer1, 0, 1, 1)
-        at(40, lay_head, 0)
-        at(41, turn_x, 1, 0, 1)
-        at(42, relu_h, 0, 1, 1, "A")
-        at(43, turn_x, 2, 0, 0)
-        at(44, copy_x, 2, 0, 0, "A")
-        at(45, quant_head, 1)
-        at(46, lay_head, 2)
-        at(47, quant_head, 0)
-        at(48, lay_h, 0, 0, 0, "V")
-        at(49, warm_pe, 0)
+        at(40, relu_h, 0, 1, 3, "A")
+        at(41, relu_h, 0, 1, 1, "A")
+        at(42, turn_x, 1, 1, 0)
+        at(43, turn_x, 2, 0, 1)
+        at(44, quant_head, 0)
+        at(45, lay_head, 1)
+        at(46, lay_h, 0, 0, 0, "V")
+        at(47, warm_pe, 8)
+        at(48, copy_x, 2, 0, 1, "A")
+        at(49, warm_pe, 10)
         at(50, lay_h, 0, 0, 1, "V")
-        at(51, quant_h, 0, 0)
-        at(52, copy_x, 1, 0, 1, "A")
-        at(53, lay_h, 0, 1, 1, "V")
+        at(51, quant_head, 1)
+        at(52, turn_x, 1, 1, 1)
+        at(53, quant_h, 0, 0)
         at(54, lay_h, 0, 1, 0, "V")
-        at(55, turn_x, 1, 1, 0)
-        at(56, quant_h, 0, 1)
-        at(57, copy_x, 1, 1, 0, "A")
-        at(58, turn_x, 1, 1, 1)
-        at(59, turn_x, 2, 0, 1)
-        at(60, quant_x, 1, 0)
-        at(61, copy_x, 1, 1, 1, "A")
-        at(62, quant_x, 1, 1)
+        at(55, turn_x, 1, 0, 1)
+        at(56, turn_x, 2, 0, 0)
+        at(57, warm_pe, 6)
+        at(58, lay_h, 0, 1, 1, "V")
+        at(59, copy_x, 1, 1, 0, "A")
+        at(60, copy_x, 1, 1, 1, "A")
+        at(61, quant_h, 0, 1)
+        at(62, copy_x, 1, 0, 1, "A")
         at(63, head, 0, 0)
-        at(64, head, 0, 1)
-        at(65, copy_x, 2, 0, 1, "A")
-        at(66, shape_k, 0)
-        at(67, log_scale, 0)
-        at(68, layer1, 1, 1, 1)
-        at(69, quant_x, 2, 0)
-        at(70, quant_head, 2)
+        at(64, copy_x, 2, 0, 0, "A")
+        at(65, quant_head, 2)
+        at(66, quant_x, 1, 0)
+        at(67, head, 0, 1)
+        at(68, shape_k, 0)
+        at(69, log_scale, 0)
+        at(70, quant_x, 1, 1)
         at(71, exp_k, 0)
-        at(72, layer1, 1, 1, 3)
-        at(73, relu_h, 1, 1, 1, "V")
-        at(74, relu_h, 1, 1, 3, "A")
-        at(75, layer1, 1, 0, 2)
-        at(76, power, 0, 0)
-        at(77, layer1, 1, 1, 0)
-        at(78, k_times_l, 0, "V")
-        at(79, layer1, 1, 1, 2)
-        at(80, amp, 0)
-        at(81, relu_h, 1, 1, 0, "A")
-        at(82, relu_h, 1, 0, 2, "V")
-        at(83, head, 0, 2)
-        at(84, power, 0, 5)
-        at(85, power, 0, 1)
-        at(86, layer1, 1, 0, 3)
-        at(87, relu_h, 1, 1, 2, "V")
-        at(88, neg_p, 0, "V")
-        at(89, layer1, 1, 0, 0)
-        at(90, layer1, 1, 0, 1)
-        at(91, hazard, 0, 0, "P")
-        at(92, relu_h, 1, 0, 3, "A")
-        at(93, turn_x, 2, 1, 0)
-        at(94, power, 0, 3)
-        at(95, lay_h, 1, 1, 0, "V")
-        at(96, hazard, 0, 5, "V")
-        at(97, turn_p, 0)
-        at(98, hazard, 0, 1, "V")
-        at(99, turn_w, 0, 1, "T")
-        at(100, relu_h, 1, 0, 0, "A")
-        at(101, relu_h, 1, 0, 1, "A")
-        at(102, lay_h, 1, 1, 1, "V")
-        at(103, turn_w, 0, 0, "M")
-        at(104, turn_x, 2, 1, 1)
-        at(105, turn_x, 3, 1, 1)
-        at(106, power, 0, 4)
-        at(107, copy_x, 2, 1, 0, "A")
-        at(108, hazard, 0, 3, "V")
-        at(109, min_w, 0, 1)
-        at(110, power, 0, 6)
-        at(111, lay_h, 1, 0, 0, "P")
-        at(112, copy_x, 2, 1, 1, "A")
-        at(113, warm_pe, 1)
-        at(114, copy_x, 3, 1, 1, "A")
-        at(115, turn_w, 0, 3, "T")
-        at(116, sub_w, 0, 1)
-        at(117, power, 0, 2)
-        at(118, min_w, 0, 0)
-        at(119, sub_w, 0, 0)
-        at(120, quant_x, 2, 1)
-        at(121, exp_w, 0, 0)
-        at(122, turn_w, 0, 5, "T")
-        at(123, layer1, 2, 0, 2)
-        at(124, warm_pe, 11)
-        at(125, power, 0, 7)
-        at(126, hazard, 0, 4, "P")
-        at(127, lay_h, 1, 0, 1, "V")
-        at(128, layer1, 2, 0, 3)
-        at(129, relu_h, 2, 0, 2, "A")
-        at(130, relu_h, 2, 0, 3, "A")
-        at(131, quant_h, 1, 1)
-        at(132, quant_h, 1, 0)
-        at(133, layer1, 2, 1, 2)
-        at(134, head, 1, 0)
-        at(135, head, 1, 1)
-        at(136, min_w, 0, 3)
-        at(137, min_p, 0)
-        at(138, relu_h, 2, 1, 2, "A")
-        at(139, shape_k, 1)
-        at(140, sub_w, 0, 3)
-        at(141, layer1, 2, 0, 1)
-        at(142, hazard, 0, 7, "P")
-        at(143, log_scale, 1)
-        at(144, exp_k, 1)
-        at(145, sub_p, 0)
-        at(146, hazard, 0, 2, "V")
-        at(147, hazard, 0, 6, "P")
-        at(148, k_times_l, 1, "P")
-        at(149, layer1, 2, 0, 0)
-        at(150, head, 1, 2)
-        at(151, relu_h, 2, 0, 1, "A")
-        at(152, power, 1, 3)
-        at(153, neg_p, 1, "A")
-        at(154, turn_w, 0, 4, "T")
-        at(155, power, 1, 2)
-        at(156, min_w, 0, 5)
-        at(157, relu_h, 2, 0, 0, "V")
-        at(158, layer1, 2, 1, 1)
-        at(159, relu_h, 2, 1, 1, "A")
-        at(160, power, 1, 0)
-        at(161, amp, 1)
-        at(162, turn_w, 0, 2, "T")
-        at(163, sub_w, 0, 5)
-        at(164, turn_x, 3, 1, 0)
-        at(165, turn_w, 0, 7, "T")
-        at(166, layer1, 2, 1, 3)
-        at(167, min_w, 0, 4)
-        at(168, dup_p, 0)
-        at(169, power, 1, 5)
-        at(170, min_w, 0, 2)
-        at(171, layer1, 2, 1, 0)
-        at(172, sub_w, 0, 4)
-        at(173, exp_p, 0)
-        at(174, turn_w, 0, 6, "T")
-        at(175, sum_p, 0)
-        at(176, min_w, 0, 7)
-        at(177, relu_h, 2, 1, 3, "V")
-        at(178, sub_w, 0, 2)
-        at(179, lay_h, 2, 0, 1, "P")
-        at(180, relu_h, 2, 1, 0, "A")
-        at(181, warm_pe, 10)
-        at(182, sub_w, 0, 7)
-        at(183, min_w, 0, 6)
-        at(184, exp_w, 0, 2)
-        at(185, copy_x, 3, 1, 0, "A")
-        at(186, lay_h, 2, 0, 0, "P")
-        at(187, warm_pe, 2)
-        at(188, warm_pe, 6)
-        at(189, hazard, 1, 3, "P")
-        at(190, sum_w, 0, 0)
-        at(191, power, 1, 1)
-        at(192, turn_x, 3, 0, 1)
-        at(193, sub_w, 0, 6)
-        at(194, turn_x, 3, 0, 0)
-        at(195, sum_w, 0, 2)
-        at(196, exp_w, 0, 1)
-        at(197, keep_norm, 0, "V")
-        at(198, hazard, 1, 2, "V")
-        at(199, lay_h, 2, 1, 0, "V")
-        at(200, copy_x, 3, 0, 1, "A")
-        at(201, power, 1, 6)
-        at(202, copy_x, 3, 0, 0, "A")
-        at(203, quant_h, 2, 0)
-        at(204, turn_w, 1, 3, "T")
-        at(205, lay_h, 2, 1, 1, "P")
-        at(206, quant_h, 2, 1)
-        at(207, head, 2, 0)
-        at(208, head, 2, 1)
-        at(209, shape_k, 2)
-        at(210, exp_w, 0, 3)
-        at(211, log_scale, 2)
-        at(212, hazard, 1, 0, "V")
-        at(213, hazard, 1, 1, "V")
-        at(214, turn_w, 1, 0, "T")
-        at(215, quant_x, 3, 0)
-        at(216, turn_w, 1, 2, "T")
-        at(217, turn_p, 1)
-        at(218, exp_k, 2)
-        at(219, power, 1, 4)
-        at(220, quant_x, 3, 1)
-        at(221, hazard, 1, 5, "V")
-        at(222, layer1, 3, 0, 2)
-        at(223, layer1, 3, 0, 3)
-        at(224, relu_h, 3, 0, 2, "A")
-        at(225, layer1, 3, 0, 1)
-        at(226, layer1, 3, 0, 0)
-        at(227, min_p, 1)
-        at(228, min_w, 1, 3)
-        at(229, hazard, 1, 6, "P")
-        at(230, min_w, 1, 0)
-        at(231, relu_h, 3, 0, 3, "A")
-        at(232, power, 1, 7)
-        at(233, relu_h, 3, 0, 0, "A")
-        at(234, relu_h, 3, 0, 1, "A")
-        at(235, k_times_l, 2, "P")
-        at(236, sub_w, 1, 3)
-        at(237, amp, 2)
-        at(238, turn_w, 1, 1, "T")
-        at(239, sum_w, 0, 3)
-        at(240, hazard, 1, 4, "P")
-        at(241, layer1, 3, 1, 2)
-        at(242, power, 2, 0)
-        at(243, sum_w, 0, 1)
-        at(244, layer1, 3, 1, 0)
-        at(245, dup_p, 1)
-        at(246, relu_h, 3, 1, 2, "A")
-        at(247, sub_w, 1, 0)
-        at(248, hazard, 1, 7, "P")
-        at(249, layer1, 3, 1, 1)
-        at(250, min_w, 1, 2)
-        at(251, power, 2, 2)
-        at(252, sub_p, 1)
-        at(253, turn_w, 1, 4, "M")
-        at(254, power, 2, 3)
-        at(255, relu_h, 3, 1, 0, "A")
-        at(256, keep_sums, 0, "A")
-        at(257, exp_p, 1)
-        at(258, layer1, 3, 1, 3)
-        at(259, sub_w, 1, 2)
-        at(260, min_w, 1, 1)
-        at(261, lay_h, 3, 0, 1, "V")
-        at(262, exp_w, 1, 1)
-        at(263, lay_h, 3, 0, 0, "P")
-        at(264, turn_w, 1, 5, "T")
-        at(265, relu_h, 3, 1, 3, "A")
-        at(266, power, 2, 5)
+        at(72, head, 0, 2)
+        at(73, layer1, 1, 1, 3)
+        at(74, neg_p, 0, "V")
+        at(75, layer1, 1, 1, 2)
+        at(76, layer1, 1, 1, 0)
+        at(77, relu_h, 1, 1, 3, "A")
+        at(78, quant_x, 2, 0)
+        at(79, layer1, 1, 1, 1)
+        at(80, relu_h, 1, 1, 2, "V")
+        at(81, power, 0, 1)
+        at(82, turn_x, 2, 1, 1)
+        at(83, relu_h, 1, 1, 1, "V")
+        at(84, relu_h, 1, 1, 0, "A")
+        at(85, turn_x, 2, 1, 0)
+        at(86, power, 0, 2)
+        at(87, copy_x, 2, 1, 1, "V")
+        at(88, k_times_l, 0, "P")
+        at(89, amp, 0)
+        at(90, lay_h, 1, 1, 1, "V")
+        at(91, hazard, 0, 2, "V")
+        at(92, copy_x, 2, 1, 0, "A")
+        at(93, quant_x, 2, 1)
+        at(94, lay_h, 1, 1, 0, "V")
+        at(95, warm_pe, 9)
+        at(96, turn_p, 0)
+        at(97, hazard, 0, 1, "V")
+        at(98, power, 0, 0)
+        at(99, layer1, 1, 0, 3)
+        at(100, relu_h, 1, 0, 3, "A")
+        at(101, min_p, 0)
+        at(102, layer1, 1, 0, 2)
+        at(103, layer1, 1, 0, 1)
+        at(104, power, 0, 3)
+        at(105, turn_w, 0, 2, "T")
+        at(106, relu_h, 1, 0, 2, "A")
+        at(107, min_w, 0, 2)
+        at(108, relu_h, 1, 0, 1, "A")
+        at(109, layer1, 2, 0, 1)
+        at(110, layer1, 1, 0, 0)
+        at(111, relu_h, 2, 0, 1, "A")
+        at(112, power, 0, 5)
+        at(113, hazard, 0, 3, "P")
+        at(114, dup_p, 0)
+        at(115, layer1, 2, 0, 3)
+        at(116, sub_p, 0)
+        at(117, relu_h, 1, 0, 0, "V")
+        at(118, power, 0, 6)
+        at(119, relu_h, 2, 0, 3, "A")
+        at(120, exp_p, 0)
+        at(121, turn_w, 0, 1, "T")
+        at(122, layer1, 2, 1, 0)
+        at(123, sub_w, 0, 2)
+        at(124, lay_h, 1, 0, 1, "V")
+        at(125, quant_h, 1, 1)
+        at(126, hazard, 0, 0, "P")
+        at(127, lay_h, 1, 0, 0, "V")
+        at(128, relu_h, 2, 1, 0, "A")
+        at(129, layer1, 2, 0, 0)
+        at(130, layer1, 2, 0, 2)
+        at(131, relu_h, 2, 0, 2, "A")
+        at(132, turn_w, 0, 3, "T")
+        at(133, turn_w, 0, 0, "T")
+        at(134, relu_h, 2, 0, 0, "A")
+        at(135, power, 0, 4)
+        at(136, hazard, 0, 5, "V")
+        at(137, quant_h, 1, 0)
+        at(138, power, 0, 7)
+        at(139, layer1, 2, 1, 1)
+        at(140, relu_h, 2, 1, 1, "V")
+        at(141, layer1, 2, 1, 2)
+        at(142, relu_h, 2, 1, 2, "A")
+        at(143, layer1, 2, 1, 3)
+        at(144, relu_h, 2, 1, 3, "A")
+        at(145, lay_h, 2, 0, 1, "P")
+        at(146, min_w, 0, 1)
+        at(147, min_w, 0, 3)
+        at(148, sub_w, 0, 1)
+        at(149, min_w, 0, 0)
+        at(150, hazard, 0, 6, "P")
+        at(151, hazard, 0, 4, "V")
+        at(152, hazard, 0, 7, "P")
+        at(153, lay_h, 2, 1, 0, "P")
+        at(154, turn_x, 3, 1, 0)
+        at(155, copy_x, 3, 1, 0, "A")
+        at(156, turn_x, 3, 0, 1)
+        at(157, copy_x, 3, 0, 1, "A")
+        at(158, turn_x, 3, 0, 0)
+        at(159, copy_x, 3, 0, 0, "A")
+        at(160, sub_w, 0, 3)
+        at(161, head, 1, 0)
+        at(162, head, 1, 1)
+        at(163, turn_w, 0, 5, "T")
+        at(164, shape_k, 1)
+        at(165, sub_w, 0, 0)
+        at(166, log_scale, 1)
+        at(167, min_w, 0, 5)
+        at(168, exp_k, 1)
+        at(169, exp_w, 0, 1)
+        at(170, turn_x, 3, 1, 1)
+        at(171, copy_x, 3, 1, 1, "V")
+        at(172, sub_w, 0, 5)
+        at(173, quant_x, 3, 0)
+        at(174, lay_h, 2, 0, 0, "V")
+        at(175, quant_x, 3, 1)
+        at(176, power, 1, 4)
+        at(177, exp_w, 0, 0)
+        at(178, k_times_l, 1, "V")
+        at(179, head, 1, 2)
+        at(180, neg_p, 1, "A")
+        at(181, power, 1, 3)
+        at(182, turn_w, 0, 4, "T")
+        at(183, turn_w, 0, 6, "M")
+        at(184, lay_h, 2, 1, 1, "V")
+        at(185, turn_w, 0, 7, "M")
+        at(186, power, 1, 2)
+        at(187, amp, 1)
+        at(188, power, 1, 5)
+        at(189, warm_pe, 0)
+        at(190, warm_pe, 11)
+        at(191, sum_w, 0, 0, "T")
+        at(192, layer1, 3, 1, 1)
+        at(193, layer1, 3, 0, 3)
+        at(194, relu_h, 3, 1, 1, "A")
+        at(195, quant_h, 2, 0)
+        at(196, quant_h, 2, 1)
+        at(197, hazard, 1, 4, "P")
+        at(198, sum_p, 0, "M")
+        at(199, min_w, 0, 4)
+        at(200, hazard, 1, 3, "P")
+        at(201, hazard, 1, 5, "P")
+        at(202, head, 2, 0)
+        at(203, layer1, 3, 0, 2)
+        at(204, relu_h, 3, 0, 3, "A")
+        at(205, layer1, 3, 1, 3)
+        at(206, min_w, 0, 7)
+        at(207, sum_w, 0, 1, "T")
+        at(208, sub_w, 0, 4)
+        at(209, keep_norm, 0, "A")
+        at(210, min_w, 0, 6)
+        at(211, sub_w, 0, 7)
+        at(212, turn_p, 1)
+        at(213, hazard, 1, 2, "P")
+        at(214, shape_k, 2)
+        at(215, power, 1, 6)
+        at(216, sub_w, 0, 6)
+        at(217, turn_w, 1, 4, "M")
+        at(218, relu_h, 3, 0, 2, "V")
+        at(219, layer1, 3, 0, 0)
+        at(220, relu_h, 3, 1, 3, "A")
+        at(221, exp_k, 2)
+        at(222, min_p, 1)
+        at(223, layer1, 3, 0, 1)
+        at(224, min_w, 1, 4)
+        at(225, sub_p, 1)
+        at(226, turn_w, 1, 5, "T")
+        at(227, relu_h, 3, 0, 1, "V")
+        at(228, exp_w, 0, 2)
+        at(229, power, 1, 7)
+        at(230, relu_h, 3, 0, 0, "A")
+        at(231, turn_w, 1, 3, "T")
+        at(232, power, 1, 1)
+        at(233, sub_w, 1, 4)
+        at(234, hazard, 1, 6, "P")
+        at(235, power, 1, 0)
+        at(236, layer1, 3, 1, 0)
+        at(237, min_w, 1, 3)
+        at(238, min_w, 1, 5)
+        at(239, dup_p, 1)
+        at(240, turn_w, 1, 2, "T")
+        at(241, hazard, 1, 7, "V")
+        at(242, sub_w, 1, 5)
+        at(243, sub_w, 1, 3)
+        at(244, min_w, 1, 2)
+        at(245, hazard, 1, 1, "P")
+        at(246, exp_p, 1)
+        at(247, exp_w, 0, 3)
+        at(248, head, 2, 1)
+        at(249, log_scale, 2)
+        at(250, power, 2, 4)
+        at(251, sum_w, 0, 2, "T")
+        at(252, relu_h, 3, 1, 0, "A")
+        at(253, exp_w, 1, 2)
+        at(254, layer1, 3, 1, 2)
+        at(255, k_times_l, 2, "V")
+        at(256, turn_w, 1, 6, "T")
+        at(257, power, 2, 2)
+        at(258, amp, 2)
+        at(259, turn_w, 1, 1, "T")
+        at(260, sum_w, 0, 3, "N")
+        at(261, sub_w, 1, 2)
+        at(262, min_w, 1, 6)
+        at(263, head, 2, 2)
+        at(264, turn_w, 1, 7, "T")
+        at(265, min_w, 1, 1)
+        at(266, sub_w, 1, 6)
         at(267, sub_w, 1, 1)
-        at(268, turn_w, 1, 6, "M")
-        at(269, hazard, 2, 3, "P")
-        at(270, hazard, 2, 2, "P")
-        at(271, relu_h, 3, 1, 1, "V")
-        at(272, lay_h, 3, 1, 0, "P")
-        at(273, lay_h, 3, 1, 1, "P")
-        at(274, hazard, 2, 0, "V")
-        at(275, head, 2, 2)
-        at(276, quant_h, 3, 0)
-        at(277, min_w, 1, 4)
-        at(278, min_w, 1, 5)
-        at(279, sub_w, 1, 5)
-        at(280, power, 2, 1)
-        at(281, sum_w, 1, 1)
-        at(282, sub_w, 1, 4)
-        at(283, sum_p, 1)
-        at(284, turn_w, 1, 7, "M")
-        at(285, exp_w, 1, 2)
-        at(286, exp_w, 1, 0)
-        at(287, min_w, 1, 6)
-        at(288, neg_p, 2, "V")
-        at(289, turn_w, 2, 2, "M")
-        at(290, sub_w, 1, 6)
-        at(291, min_w, 1, 7)
-        at(292, keep_norm, 1, "V")
-        at(293, sum_w, 1, 2)
-        at(294, sub_w, 1, 7)
-        at(295, power, 2, 4)
-        at(296, hazard, 2, 4, "P")
-        at(297, quant_h, 3, 1)
-        at(298, power, 2, 6)
-        at(299, exp_w, 1, 3)
-        at(300, min_w, 2, 2)
-        at(301, turn_w, 2, 3, "M")
-        at(302, turn_p, 2)
-        at(303, head, 3, 0)
-        at(304, shape_k, 3)
-        at(305, head, 3, 1)
-        at(306, log_scale, 3)
-        at(307, min_w, 2, 3)
-        at(308, exp_k, 3)
-        at(309, hazard, 2, 5, "P")
-        at(310, sub_w, 2, 2)
-        at(311, hazard, 2, 1, "P")
-        at(312, power, 2, 7)
-        at(313, turn_w, 2, 0, "T")
-        at(314, sub_w, 2, 3)
-        at(315, min_p, 2)
-        at(316, sum_w, 1, 0)
-        at(317, min_w, 2, 0)
-        at(318, sub_p, 2)
-        at(319, exp_w, 2, 1)
-        at(320, k_times_l, 3, "P")
-        at(321, hazard, 2, 6, "P")
-        at(322, sub_w, 2, 0)
-        at(323, turn_w, 2, 4, "T")
-        at(324, min_w, 2, 4)
-        at(325, turn_w, 2, 5, "M")
-        at(326, power, 3, 0)
-        at(327, exp_p, 2)
-        at(328, power, 3, 1)
-        at(329, amp, 3)
-        at(330, power, 3, 5)
-        at(331, turn_w, 2, 1, "M")
-        at(332, min_w, 2, 5)
-        at(333, sum_w, 1, 3)
-        at(334, sub_w, 2, 4)
-        at(335, min_w, 2, 1)
-        at(336, hazard, 2, 7, "P")
-        at(337, sub_w, 2, 5)
-        at(338, sub_w, 2, 1)
+        at(268, keep_sums, 0, "A")
+        at(269, power, 2, 6)
+        at(270, lay_h, 3, 0, 0, "P")
+        at(271, hazard, 2, 2, "V")
+        at(272, hazard, 1, 0, "P")
+        at(273, hazard, 2, 4, "V")
+        at(274, relu_h, 3, 1, 2, "A")
+        at(275, lay_h, 3, 0, 1, "P")
+        at(276, min_w, 1, 7)
+        at(277, turn_w, 1, 0, "M")
+        at(278, sum_p, 1, "N")
+        at(279, min_w, 1, 0)
+        at(280, neg_p, 2, "A")
+        at(281, exp_w, 1, 1)
+        at(282, sum_w, 1, 2, "T")
+        at(283, keep_norm, 1, "A")
+        at(284, turn_w, 2, 2, "N")
+        at(285, sub_w, 1, 7)
+        at(286, lay_h, 3, 1, 0, "V")
+        at(287, lay_h, 3, 1, 1, "P")
+        at(288, power, 2, 5)
+        at(289, quant_h, 3, 0)
+        at(290, sum_w, 1, 1, "M")
+        at(291, quant_h, 3, 1)
+        at(292, hazard, 2, 6, "V")
+        at(293, sub_w, 1, 0)
+        at(294, exp_w, 1, 3)
+        at(295, turn_p, 2)
+        at(296, min_p, 2)
+        at(297, min_w, 2, 2)
+        at(298, head, 3, 0)
+        at(299, power, 2, 3)
+        at(300, head, 3, 1)
+        at(301, sum_w, 1, 3, "T")
+        at(302, sub_p, 2)
+        at(303, sub_w, 2, 2)
+        at(304, turn_w, 2, 4, "N")
+        at(305, power, 2, 7)
+        at(306, hazard, 2, 3, "P")
+        at(307, turn_w, 2, 3, "T")
+        at(308, power, 2, 1)
+        at(309, shape_k, 3)
+        at(310, hazard, 2, 5, "P")
+        at(311, min_w, 2, 4)
+        at(312, turn_w, 2, 5, "N")
+        at(313, hazard, 2, 7, "P")
+        at(314, min_w, 2, 3)
+        at(315, log_scale, 3)
+        at(316, exp_k, 3)
+        at(317, exp_w, 1, 0)
+        at(318, sub_w, 2, 4)
+        at(319, power, 2, 0)
+        at(320, sum_w, 1, 0, "M")
+        at(321, sub_w, 2, 3)
+        at(322, power, 3, 2)
+        at(323, min_w, 2, 5)
+        at(324, turn_w, 2, 6, "T")
+        at(325, head, 3, 2)
+        at(326, exp_p, 2)
+        at(327, min_w, 2, 6)
+        at(328, k_times_l, 3, "P")
+        at(329, power, 3, 4)
+        at(330, dup_p, 2)
+        at(331, hazard, 2, 1, "P")
+        at(332, sub_w, 2, 5)
+        at(333, amp, 3)
+        at(334, turn_w, 2, 7, "T")
+        at(335, exp_w, 2, 1)
+        at(336, sub_w, 2, 6)
+        at(337, min_w, 2, 7)
+        at(338, hazard, 2, 0, "P")
         at(339, keep_sums, 1, "V")
-        at(340, turn_w, 2, 6, "T")
-        at(341, min_w, 2, 6)
-        at(342, turn_w, 2, 7, "T")
-        at(343, head, 3, 2)
-        at(344, neg_p, 3, "V")
-        at(345, hazard, 3, 0, "P")
-        at(346, power, 3, 2)
-        at(347, exp_w, 2, 2)
-        at(348, min_w, 2, 7)
-        at(349, sub_w, 2, 6)
-        at(350, sum_w, 2, 1)
-        at(351, hazard, 3, 1, "P")
-        at(352, sum_w, 2, 2)
-        at(353, power, 3, 3)
-        at(354, exp_w, 2, 0)
-        at(355, power, 3, 4)
-        at(356, sub_w, 2, 7)
-        at(357, hazard, 3, 5, "P")
-        at(358, turn_w, 3, 0, "T")
-        at(359, power, 3, 7)
-        at(360, dup_p, 2)
-        at(361, turn_w, 3, 1, "T")
-        at(362, sum_p, 2)
-        at(363, hazard, 3, 2, "P")
-        at(364, turn_w, 3, 5, "M")
-        at(365, min_w, 3, 0)
-        at(366, exp_w, 2, 3)
-        at(367, min_w, 3, 1)
-        at(368, sum_w, 2, 0)
-        at(369, power, 3, 6)
-        at(370, log_norm, 0)
-        at(371, keep_norm, 2, "V")
-        at(372, sub_w, 3, 0)
-        at(373, logs, 0)
-        at(374, log_norm, 2)
-        at(375, log_norm, 1)
-        at(376, logs, 1)
-        at(377, min_w, 3, 5)
-        at(378, sub_w, 3, 1)
-        at(379, sum_w, 2, 3)
-        at(380, keep_sums, 2, "V")
-        at(381, turn_p, 3)
-        at(382, min_p, 3)
-        at(383, logs, 2)
-        at(384, hazard, 3, 4, "P")
-        at(385, hazard, 3, 3, "P")
-        at(386, turn_w, 3, 4, "T")
+        at(340, hazard, 3, 2, "P")
+        at(341, sub_w, 2, 7)
+        at(342, hazard, 3, 4, "P")
+        at(343, sum_p, 2, "M")
+        at(344, exp_w, 2, 2)
+        at(345, turn_w, 2, 1, "M")
+        at(346, min_w, 2, 1)
+        at(347, turn_w, 2, 0, "M")
+        at(348, power, 3, 0)
+        at(349, neg_p, 3, "V")
+        at(350, sum_w, 2, 1, "M")
+        at(351, min_w, 2, 0)
+        at(352, power, 3, 5)
+        at(353, power, 3, 6)
+        at(354, sum_w, 2, 2, "M")
+        at(355, sub_w, 2, 1)
+        at(356, turn_w, 3, 4, "M")
+        at(357, sub_w, 2, 0)
+        at(358, exp_w, 2, 3)
+        at(359, turn_w, 3, 2, "T")
+        at(360, min_w, 3, 4)
+        at(361, min_w, 3, 2)
+        at(362, hazard, 3, 0, "P")
+        at(363, turn_w, 3, 0, "N")
+        at(364, power, 3, 3)
+        at(365, power, 3, 7)
+        at(366, sub_w, 3, 4)
+        at(367, exp_w, 2, 0)
+        at(368, keep_norm, 2, "V")
+        at(369, min_w, 3, 0)
+        at(370, sub_w, 3, 2)
+        at(371, hazard, 3, 5, "P")
+        at(372, power, 3, 1)
+        at(373, sum_w, 2, 3, "T")
+        at(374, sub_w, 3, 0)
+        at(375, hazard, 3, 3, "P")
+        at(376, log_norm, 2)
+        at(377, log_norm, 0)
+        at(378, hazard, 3, 1, "P")
+        at(379, offset, 0, "P")
+        at(380, sum_w, 2, 0, "N")
+        at(381, turn_w, 3, 5, "T")
+        at(382, logs, 0)
+        at(383, keep_sums, 2, "V")
+        at(384, hazard, 3, 7, "P")
+        at(385, turn_w, 3, 1, "N")
+        at(386, min_w, 3, 5)
         at(387, sub_w, 3, 5)
-        at(388, min_w, 3, 4)
-        at(389, turn_w, 3, 2, "T")
-        at(390, min_w, 3, 2)
-        at(391, sub_w, 3, 4)
-        at(392, sub_w, 3, 2)
-        at(393, turn_w, 3, 3, "M")
-        at(394, min_w, 3, 3)
-        at(395, hazard, 3, 6, "P")
-        at(396, offset, 1, "P")
-        at(397, turn_w, 3, 6, "M")
-        at(398, offset, 0, "P")
-        at(399, sub_p, 3)
-        at(400, hazard, 3, 7, "P")
-        at(401, turn_w, 3, 7, "T")
-        at(402, min_w, 3, 6)
-        at(403, turn_back, 1, "T")
-        at(404, exp_w, 3, 0)
-        at(405, exp_p, 3)
-        at(406, exp_w, 3, 2)
-        at(407, sum_w, 3, 0)
-        at(408, min_w, 3, 7)
-        at(409, sub_w, 3, 3)
-        at(410, turn_back, 0, "T")
-        at(411, sub_w, 3, 6)
-        at(412, sum_w, 3, 2)
-        at(413, sub_w, 3, 7)
-        at(414, offset, 2, "P")
-        at(415, result, 0)
-        at(416, dup_p, 3)
-        at(417, sum_p, 3)
-        at(418, exp_w, 3, 1)
-        at(419, exp_w, 3, 3)
-        at(420, keep_norm, 3, "V")
-        at(421, log_norm, 3)
-        at(422, sum_w, 3, 1)
-        at(423, result, 1)
-        at(424, lay_out, 0, "P")
-        at(425, sum_w, 3, 3)
-        at(426, turn_back, 2, "M")
+        at(388, min_w, 3, 1)
+        at(389, logs, 1)
+        at(390, turn_p, 3)
+        at(391, turn_w, 3, 3, "N")
+        at(392, min_p, 3)
+        at(393, min_w, 3, 3)
+        at(394, sub_w, 3, 1)
+        at(395, sub_p, 3)
+        at(396, turn_w, 3, 7, "M")
+        at(397, logs, 2)
+        at(398, log_norm, 1)
+        at(399, hazard, 3, 6, "P")
+        at(400, turn_back, 0, "N")
+        at(401, sub_w, 3, 3)
+        at(402, turn_w, 3, 6, "T")
+        at(403, exp_w, 3, 2)
+        at(404, exp_p, 3)
+        at(405, min_w, 3, 7)
+        at(406, min_w, 3, 6)
+        at(407, exp_w, 3, 0)
+        at(408, sum_w, 3, 2, "N")
+        at(409, dup_p, 3)
+        at(410, sub_w, 3, 7)
+        at(411, exp_w, 3, 1)
+        at(412, sub_w, 3, 6)
+        at(413, sum_p, 3, "M")
+        at(414, offset, 1, "P")
+        at(415, sum_w, 3, 0, "T")
+        at(416, turn_back, 1, "N")
+        at(417, result, 1)
+        at(418, exp_w, 3, 3)
+        at(419, sum_w, 3, 1, "T")
+        at(420, offset, 2, "P")
+        at(421, keep_norm, 3, "V")
+        at(422, sum_w, 3, 3, "M")
+        at(423, log_norm, 3)
+        at(424, result, 0)
+        at(425, lay_out, 1, "P")
+        at(426, turn_back, 2, "N")
         at(427, offset, 3, "V")
-        at(428, logs, 3)
-        at(429, result, 2)
-        at(430, lay_out, 1, "A")
+        at(428, result, 2)
+        at(429, logs, 3)
+        at(430, lay_out, 0, "A")
         at(431, turn_back, 3, "T")
-        at(432, quant_out, 0)
-        at(433, lay_out, 2, "A")
-        at(434, result, 3)
-        at(435, quant_out, 1)
+        at(432, quant_out, 1)
+        at(433, result, 3)
+        at(434, lay_out, 2, "A")
+        at(435, quant_out, 0)
         at(436, lay_out, 3, "V")
         at(437, quant_out, 2)
         at(438, quant_out, 3)

@@ -48,7 +48,7 @@ def tile_deepsurvivalmachinesweibullriskcurves_x2_kernel(
         x_sb = [[keep.tile([P, 4, G], BF16, name="x_sb%d_%d" % (g, kg)) for kg in range(2)] for g in range(GROUPS)]
         wmin = [keep.tile([P, T, SR], F32, name="wmin%d" % g) for g in range(GROUPS)]
         sums = [keep.tile([P, 4, P], F32, name="sums%d" % g) for g in range(GROUPS)]
-        norm = [keep.tile([P, 2, P], F32, name="norm%d" % g) for g in range(GROUPS)]
+        norm = keep.tile([P, 2, GROUPS, P], F32, name="norm")
         out_scales = keep.tile([P, GROUPS, P], U8, name="out_scales", align_bytes=AL)
 
         def load_x(g, kg):
@@ -100,9 +100,13 @@ def tile_deepsurvivalmachinesweibullriskcurves_x2_kernel(
                 in_=s1_raw[:, :, G * hg : G * (hg + 1)].rearrange("p g (m j) -> p g j m", j=4),
             )
 
-        def lay_head(j):
+        def lay_head(j, eng):
             laid = work.tile([P, 2, P, 4], BF16, name="head_laid", bufs=3, align_bytes=AL)
-            nc.vector.tensor_copy(out=laid[:], in_=hw_raw[j][:].rearrange("p g j n -> p g n j"))
+            src = hw_raw[j][:].rearrange("p g j n -> p g n j")
+            if eng == "P":
+                nc.gpsimd.tensor_scalar(out=laid[:], in0=src, scalar1=1.0, scalar2=0.0, op0=ALU.mult, op1=ALU.add)
+            else:
+                nc.vector.tensor_copy(out=laid[:], in_=src)
             st["head", j] = laid
 
         def quant_head(j):
@@ -291,7 +295,7 @@ def tile_deepsurvivalmachinesweibullriskcurves_x2_kernel(
                 nc.vector.tensor_copy(out=dst, in_=src)
 
         def keep_norm(g, eng):
-            move(eng, norm[g][:].rearrange("p d c -> p (d c)"), st["s0", g][:, 0 : 2 * P])
+            move(eng, norm[:, :, g, :], st["s0", g][:, 0 : 2 * P].rearrange("p (d c) -> p d c", d=2))
 
         def power(g, i):
             e = work.tile([P, G], F32, name="pow", bufs=4)
@@ -346,9 +350,9 @@ def tile_deepsurvivalmachinesweibullriskcurves_x2_kernel(
             move(eng, sums[g][:].rearrange("p q c -> p (q c)"), st["s", g][:])
 
         def log_norm(g):
-            ln0 = work.tile([P, P], F32, name="ln0", bufs=4)
-            nc.scalar.activation(out=ln0[:], in_=norm[g][:, 0, :], func=ACT.Ln)
-            st["ln0", g] = ln0
+            ln0 = work.tile([P, GROUPS, P], F32, name="ln0", bufs=1)
+            nc.scalar.activation(out=ln0[:], in_=norm[:, 0], func=ACT.Ln)
+            st["ln0"] = ln0
 
         def logs(g):
             lns = work.tile([P, G], F32, name="lns", bufs=4)
@@ -357,16 +361,16 @@ def tile_deepsurvivalmachinesweibullriskcurves_x2_kernel(
             st["ln", g] = lns
 
         def offset(g, eng):
-            c0 = work.tile([P, P], F32, name="c0", bufs=4)
-            (nc.vector if eng == "V" else nc.gpsimd).tensor_tensor(out=c0[:], in0=norm[g][:, 1, :], in1=st["ln0", g][:], op=ALU.subtract)
-            st["c0", g] = c0
+            c0 = work.tile([P, GROUPS, P], F32, name="c0", bufs=1)
+            (nc.vector if eng == "V" else nc.gpsimd).tensor_tensor(out=c0[:], in0=norm[:, 1], in1=st["ln0"][:], op=ALU.subtract)
+            st["c0"] = c0
 
         def turn_back(g, eng):
             bank = front_bank()
             for q in range(4):
                 cols = slice(P * q, P * (q + 1))
                 nc.tensor.matmul(bank[:, cols], st["ln", g][:, cols], ident[:], start=True, stop=False, is_transpose=True)
-                nc.tensor.matmul(bank[:, cols], st["c0", g][:], ident[:], start=False, stop=True, is_transpose=(q >= "TMN".index(eng)))
+                nc.tensor.matmul(bank[:, cols], st["c0"][:, g, :], ident[:], start=False, stop=True, is_transpose=(q >= "TMN".index(eng)))
             st["fin", g] = bank
 
         def result(g):
@@ -404,445 +408,433 @@ def tile_deepsurvivalmachinesweibullriskcurves_x2_kernel(
         def at(when, fn, *args):
             plan.append((when, len(plan), fn, args))
 
-        at(0, warm_pe, 3)
-        at(1, warm_pe, 5)
-        at(2, turn_x, 0, 0, 0)
-        at(3, warm_pe, 2)
-        at(4, warm_pe, 4)
-        at(5, order_w1, 0, 0)
-        at(6, copy_x, 0, 0, 0, "A")
-        at(7, turn_x, 0, 0, 1)
-        at(8, order_w1, 0, 1)
-        at(9, turn_x, 0, 1, 1)
-        at(10, turn_x, 0, 1, 0)
-        at(11, order_s1, 1)
-        at(12, copy_x, 0, 0, 1, "A")
-        at(13, order_s1, 0)
-        at(14, warm_pe, 1)
-        at(15, copy_x, 0, 1, 1, "A")
-        at(16, warm_pe, 7)
-        at(17, order_w1, 1, 0)
-        at(18, turn_x, 1, 0, 0)
-        at(19, quant_x, 0, 0)
-        at(20, copy_x, 0, 1, 0, "A")
-        at(21, copy_x, 1, 0, 0, "A")
-        at(22, quant_x, 0, 1)
-        at(23, layer1, 0, 0, 1)
-        at(24, layer1, 0, 0, 2)
+        at(0, turn_x, 0, 0, 0)
+        at(1, warm_pe, 2)
+        at(2, order_s1, 0)
+        at(3, turn_x, 0, 0, 1)
+        at(4, copy_x, 0, 0, 0, "A")
+        at(5, copy_x, 0, 0, 1, "A")
+        at(6, order_w1, 0, 1)
+        at(7, turn_x, 0, 1, 1)
+        at(8, copy_x, 0, 1, 1, "A")
+        at(9, turn_x, 0, 1, 0)
+        at(10, order_s1, 1)
+        at(11, order_w1, 1, 1)
+        at(12, warm_pe, 1)
+        at(13, order_w1, 1, 0)
+        at(14, copy_x, 0, 1, 0, "A")
+        at(15, lay_head, 1, "P")
+        at(16, turn_x, 1, 0, 0)
+        at(17, turn_x, 1, 0, 1)
+        at(18, quant_x, 0, 0)
+        at(19, order_w1, 0, 0)
+        at(20, quant_x, 0, 1)
+        at(21, layer1, 0, 0, 1)
+        at(22, copy_x, 1, 0, 0, "A")
+        at(23, lay_head, 2, "P")
+        at(24, copy_x, 1, 0, 1, "A")
         at(25, relu_h, 0, 0, 1, "A")
-        at(26, relu_h, 0, 0, 2, "A")
-        at(27, layer1, 0, 0, 0)
-        at(28, relu_h, 0, 0, 0, "A")
-        at(29, layer1, 0, 0, 3)
-        at(30, relu_h, 0, 0, 3, "A")
-        at(31, order_w1, 1, 1)
-        at(32, layer1, 0, 1, 2)
-        at(33, relu_h, 0, 1, 2, "A")
-        at(34, layer1, 0, 1, 0)
-        at(35, layer1, 0, 1, 3)
-        at(36, lay_head, 0)
-        at(37, lay_head, 2)
-        at(38, relu_h, 0, 1, 0, "A")
-        at(39, layer1, 0, 1, 1)
-        at(40, relu_h, 0, 1, 3, "A")
-        at(41, relu_h, 0, 1, 1, "A")
-        at(42, turn_x, 1, 1, 0)
-        at(43, turn_x, 2, 0, 1)
-        at(44, quant_head, 0)
-        at(45, lay_head, 1)
-        at(46, lay_h, 0, 0, 0, "V")
-        at(47, warm_pe, 8)
-        at(48, copy_x, 2, 0, 1, "A")
-        at(49, warm_pe, 10)
-        at(50, lay_h, 0, 0, 1, "V")
-        at(51, quant_head, 1)
-        at(52, turn_x, 1, 1, 1)
-        at(53, quant_h, 0, 0)
-        at(54, lay_h, 0, 1, 0, "V")
-        at(55, turn_x, 1, 0, 1)
-        at(56, turn_x, 2, 0, 0)
-        at(57, warm_pe, 6)
-        at(58, lay_h, 0, 1, 1, "V")
-        at(59, copy_x, 1, 1, 0, "A")
-        at(60, copy_x, 1, 1, 1, "A")
-        at(61, quant_h, 0, 1)
-        at(62, copy_x, 1, 0, 1, "A")
-        at(63, head, 0, 0)
-        at(64, copy_x, 2, 0, 0, "A")
-        at(65, quant_head, 2)
-        at(66, quant_x, 1, 0)
-        at(67, head, 0, 1)
-        at(68, shape_k, 0)
-        at(69, log_scale, 0)
-        at(70, quant_x, 1, 1)
-        at(71, exp_k, 0)
-        at(72, head, 0, 2)
-        at(73, layer1, 1, 1, 3)
-        at(74, neg_p, 0, "V")
-        at(75, layer1, 1, 1, 2)
-        at(76, layer1, 1, 1, 0)
-        at(77, relu_h, 1, 1, 3, "A")
-        at(78, quant_x, 2, 0)
-        at(79, layer1, 1, 1, 1)
-        at(80, relu_h, 1, 1, 2, "V")
-        at(81, power, 0, 1)
-        at(82, turn_x, 2, 1, 1)
-        at(83, relu_h, 1, 1, 1, "V")
-        at(84, relu_h, 1, 1, 0, "A")
-        at(85, turn_x, 2, 1, 0)
-        at(86, power, 0, 2)
-        at(87, copy_x, 2, 1, 1, "V")
-        at(88, k_times_l, 0, "P")
-        at(89, amp, 0)
-        at(90, lay_h, 1, 1, 1, "V")
-        at(91, hazard, 0, 2, "V")
-        at(92, copy_x, 2, 1, 0, "A")
-        at(93, quant_x, 2, 1)
-        at(94, lay_h, 1, 1, 0, "V")
-        at(95, warm_pe, 9)
-        at(96, turn_p, 0)
-        at(97, hazard, 0, 1, "V")
-        at(98, power, 0, 0)
-        at(99, layer1, 1, 0, 3)
-        at(100, relu_h, 1, 0, 3, "A")
-        at(101, min_p, 0)
-        at(102, layer1, 1, 0, 2)
-        at(103, layer1, 1, 0, 1)
-        at(104, power, 0, 3)
-        at(105, turn_w, 0, 2, "T")
-        at(106, relu_h, 1, 0, 2, "A")
-        at(107, min_w, 0, 2)
-        at(108, relu_h, 1, 0, 1, "A")
-        at(109, layer1, 2, 0, 1)
-        at(110, layer1, 1, 0, 0)
-        at(111, relu_h, 2, 0, 1, "A")
-        at(112, power, 0, 5)
-        at(113, hazard, 0, 3, "P")
-        at(114, dup_p, 0)
-        at(115, layer1, 2, 0, 3)
-        at(116, sub_p, 0)
-        at(117, relu_h, 1, 0, 0, "V")
-        at(118, power, 0, 6)
-        at(119, relu_h, 2, 0, 3, "A")
-        at(120, exp_p, 0)
-        at(121, turn_w, 0, 1, "T")
-        at(122, layer1, 2, 1, 0)
-        at(123, sub_w, 0, 2)
-        at(124, lay_h, 1, 0, 1, "V")
-        at(125, quant_h, 1, 1)
-        at(126, hazard, 0, 0, "P")
-        at(127, lay_h, 1, 0, 0, "V")
-        at(128, relu_h, 2, 1, 0, "A")
-        at(129, layer1, 2, 0, 0)
-        at(130, layer1, 2, 0, 2)
-        at(131, relu_h, 2, 0, 2, "A")
-        at(132, turn_w, 0, 3, "T")
-        at(133, turn_w, 0, 0, "T")
-        at(134, relu_h, 2, 0, 0, "A")
-        at(135, power, 0, 4)
-        at(136, hazard, 0, 5, "V")
-        at(137, quant_h, 1, 0)
-        at(138, power, 0, 7)
-        at(139, layer1, 2, 1, 1)
-        at(140, relu_h, 2, 1, 1, "V")
-        at(141, layer1, 2, 1, 2)
-        at(142, relu_h, 2, 1, 2, "A")
-        at(143, layer1, 2, 1, 3)
-        at(144, relu_h, 2, 1, 3, "A")
-        at(145, lay_h, 2, 0, 1, "P")
-        at(146, min_w, 0, 1)
-        at(147, min_w, 0, 3)
-        at(148, sub_w, 0, 1)
-        at(149, min_w, 0, 0)
-        at(150, hazard, 0, 6, "P")
-        at(151, hazard, 0, 4, "V")
-        at(152, hazard, 0, 7, "P")
-        at(153, lay_h, 2, 1, 0, "P")
-        at(154, turn_x, 3, 1, 0)
-        at(155, copy_x, 3, 1, 0, "A")
-        at(156, turn_x, 3, 0, 1)
-        at(157, copy_x, 3, 0, 1, "A")
-        at(158, turn_x, 3, 0, 0)
-        at(159, copy_x, 3, 0, 0, "A")
-        at(160, sub_w, 0, 3)
-        at(161, head, 1, 0)
-        at(162, head, 1, 1)
-        at(163, turn_w, 0, 5, "T")
-        at(164, shape_k, 1)
-        at(165, sub_w, 0, 0)
-        at(166, log_scale, 1)
-        at(167, min_w, 0, 5)
-        at(168, exp_k, 1)
-        at(169, exp_w, 0, 1)
-        at(170, turn_x, 3, 1, 1)
-        at(171, copy_x, 3, 1, 1, "V")
-        at(172, sub_w, 0, 5)
-        at(173, quant_x, 3, 0)
-        at(174, lay_h, 2, 0, 0, "V")
-        at(175, quant_x, 3, 1)
-        at(176, power, 1, 4)
-        at(177, exp_w, 0, 0)
-        at(178, k_times_l, 1, "V")
-        at(179, head, 1, 2)
-        at(180, neg_p, 1, "A")
-        at(181, power, 1, 3)
-        at(182, turn_w, 0, 4, "T")
-        at(183, turn_w, 0, 6, "M")
-        at(184, lay_h, 2, 1, 1, "V")
-        at(185, turn_w, 0, 7, "M")
-        at(186, power, 1, 2)
-        at(187, amp, 1)
-        at(188, power, 1, 5)
-        at(189, warm_pe, 0)
-        at(190, warm_pe, 11)
-        at(191, sum_w, 0, 0, "T")
-        at(192, layer1, 3, 1, 1)
-        at(193, layer1, 3, 0, 3)
-        at(194, relu_h, 3, 1, 1, "A")
-        at(195, quant_h, 2, 0)
-        at(196, quant_h, 2, 1)
-        at(197, hazard, 1, 4, "P")
-        at(198, sum_p, 0, "M")
-        at(199, min_w, 0, 4)
-        at(200, hazard, 1, 3, "P")
-        at(201, hazard, 1, 5, "P")
-        at(202, head, 2, 0)
-        at(203, layer1, 3, 0, 2)
-        at(204, relu_h, 3, 0, 3, "A")
-        at(205, layer1, 3, 1, 3)
-        at(206, min_w, 0, 7)
-        at(207, sum_w, 0, 1, "T")
-        at(208, sub_w, 0, 4)
-        at(209, keep_norm, 0, "A")
-        at(210, min_w, 0, 6)
-        at(211, sub_w, 0, 7)
-        at(212, turn_p, 1)
-        at(213, hazard, 1, 2, "P")
-        at(214, shape_k, 2)
-        at(215, power, 1, 6)
-        at(216, sub_w, 0, 6)
-        at(217, turn_w, 1, 4, "M")
-        at(218, relu_h, 3, 0, 2, "V")
-        at(219, layer1, 3, 0, 0)
-        at(220, relu_h, 3, 1, 3, "A")
-        at(221, exp_k, 2)
-        at(222, min_p, 1)
-        at(223, layer1, 3, 0, 1)
-        at(224, min_w, 1, 4)
+        at(26, lay_head, 0, "V")
+        at(27, layer1, 0, 0, 3)
+        at(28, relu_h, 0, 0, 3, "A")
+        at(29, layer1, 0, 0, 2)
+        at(30, layer1, 0, 0, 0)
+        at(31, layer1, 0, 1, 1)
+        at(32, relu_h, 0, 0, 2, "A")
+        at(33, quant_x, 1, 0)
+        at(34, turn_x, 1, 1, 1)
+        at(35, turn_x, 2, 0, 1)
+        at(36, turn_x, 1, 1, 0)
+        at(37, relu_h, 0, 0, 0, "A")
+        at(38, relu_h, 0, 1, 1, "A")
+        at(39, turn_x, 2, 1, 0)
+        at(40, copy_x, 1, 1, 1, "A")
+        at(41, turn_x, 2, 1, 1)
+        at(42, copy_x, 2, 0, 1, "A")
+        at(43, copy_x, 2, 1, 0, "A")
+        at(44, copy_x, 2, 1, 1, "A")
+        at(45, layer1, 0, 1, 0)
+        at(46, copy_x, 1, 1, 0, "V")
+        at(47, relu_h, 0, 1, 0, "A")
+        at(48, layer1, 0, 1, 3)
+        at(49, relu_h, 0, 1, 3, "A")
+        at(50, layer1, 0, 1, 2)
+        at(51, quant_x, 1, 1)
+        at(52, lay_h, 0, 0, 1, "P")
+        at(53, layer1, 1, 1, 2)
+        at(54, relu_h, 0, 1, 2, "A")
+        at(55, quant_head, 1)
+        at(56, lay_h, 0, 0, 0, "V")
+        at(57, quant_x, 2, 1)
+        at(58, relu_h, 1, 1, 2, "A")
+        at(59, layer1, 1, 1, 0)
+        at(60, quant_h, 0, 0)
+        at(61, layer1, 1, 1, 3)
+        at(62, relu_h, 1, 1, 0, "A")
+        at(63, lay_h, 0, 1, 1, "V")
+        at(64, lay_h, 0, 1, 0, "P")
+        at(65, relu_h, 1, 1, 3, "A")
+        at(66, turn_x, 2, 0, 0)
+        at(67, copy_x, 2, 0, 0, "A")
+        at(68, layer1, 1, 1, 1)
+        at(69, relu_h, 1, 1, 1, "A")
+        at(70, layer1, 1, 0, 3)
+        at(71, quant_head, 0)
+        at(72, relu_h, 1, 0, 3, "A")
+        at(73, quant_h, 0, 1)
+        at(74, quant_x, 2, 0)
+        at(75, quant_head, 2)
+        at(76, lay_h, 1, 1, 1, "V")
+        at(77, layer1, 1, 0, 1)
+        at(78, relu_h, 1, 0, 1, "A")
+        at(79, layer1, 1, 0, 0)
+        at(80, relu_h, 1, 0, 0, "A")
+        at(81, layer1, 1, 0, 2)
+        at(82, relu_h, 1, 0, 2, "A")
+        at(83, head, 0, 0)
+        at(84, layer1, 2, 0, 3)
+        at(85, lay_h, 1, 0, 1, "P")
+        at(86, lay_h, 1, 1, 0, "V")
+        at(87, shape_k, 0)
+        at(88, head, 0, 1)
+        at(89, exp_k, 0)
+        at(90, relu_h, 2, 0, 3, "V")
+        at(91, layer1, 2, 0, 1)
+        at(92, log_scale, 0)
+        at(93, relu_h, 2, 0, 1, "V")
+        at(94, lay_h, 1, 0, 0, "V")
+        at(95, power, 0, 0)
+        at(96, power, 0, 1)
+        at(97, power, 0, 2)
+        at(98, turn_x, 3, 1, 1)
+        at(99, layer1, 2, 1, 2)
+        at(100, turn_x, 3, 1, 0)
+        at(101, copy_x, 3, 1, 1, "V")
+        at(102, copy_x, 3, 1, 0, "A")
+        at(103, relu_h, 2, 1, 2, "V")
+        at(104, head, 0, 2)
+        at(105, quant_h, 1, 0)
+        at(106, turn_x, 3, 0, 0)
+        at(107, k_times_l, 0, "P")
+        at(108, amp, 0)
+        at(109, neg_p, 0, "A")
+        at(110, quant_x, 3, 1)
+        at(111, quant_h, 1, 1)
+        at(112, hazard, 0, 1, "V")
+        at(113, layer1, 2, 0, 0)
+        at(114, layer1, 2, 0, 2)
+        at(115, copy_x, 3, 0, 0, "A")
+        at(116, relu_h, 2, 0, 0, "A")
+        at(117, hazard, 0, 0, "V")
+        at(118, power, 0, 7)
+        at(119, turn_x, 3, 0, 1)
+        at(120, power, 0, 5)
+        at(121, copy_x, 3, 0, 1, "A")
+        at(122, hazard, 0, 2, "V")
+        at(123, power, 0, 6)
+        at(124, turn_p, 0)
+        at(125, power, 0, 4)
+        at(126, turn_w, 0, 1, "T")
+        at(127, relu_h, 2, 0, 2, "V")
+        at(128, hazard, 0, 7, "P")
+        at(129, turn_w, 0, 0, "T")
+        at(130, min_w, 0, 1)
+        at(131, power, 0, 3)
+        at(132, layer1, 2, 1, 0)
+        at(133, relu_h, 2, 1, 0, "A")
+        at(134, hazard, 0, 6, "P")
+        at(135, quant_x, 3, 0)
+        at(136, min_w, 0, 0)
+        at(137, sub_w, 0, 1)
+        at(138, head, 1, 0)
+        at(139, lay_h, 2, 0, 0, "V")
+        at(140, shape_k, 1)
+        at(141, layer1, 3, 1, 2)
+        at(142, min_p, 0)
+        at(143, hazard, 0, 5, "P")
+        at(144, turn_w, 0, 2, "T")
+        at(145, min_w, 0, 2)
+        at(146, sub_w, 0, 0)
+        at(147, head, 1, 1)
+        at(148, relu_h, 3, 1, 2, "A")
+        at(149, exp_k, 1)
+        at(150, turn_w, 0, 7, "T")
+        at(151, log_scale, 1)
+        at(152, sub_w, 0, 2)
+        at(153, layer1, 2, 1, 3)
+        at(154, power, 1, 3)
+        at(155, layer1, 2, 1, 1)
+        at(156, min_w, 0, 7)
+        at(157, relu_h, 2, 1, 3, "A")
+        at(158, lay_h, 2, 0, 1, "P")
+        at(159, layer1, 3, 1, 0)
+        at(160, sub_p, 0)
+        at(161, relu_h, 2, 1, 1, "A")
+        at(162, sub_w, 0, 7)
+        at(163, layer1, 3, 1, 3)
+        at(164, layer1, 3, 1, 1)
+        at(165, k_times_l, 1, "V")
+        at(166, relu_h, 3, 1, 0, "A")
+        at(167, dup_p, 0)
+        at(168, relu_h, 3, 1, 3, "A")
+        at(169, hazard, 0, 3, "P")
+        at(170, head, 1, 2)
+        at(171, lay_h, 2, 1, 0, "V")
+        at(172, hazard, 0, 4, "V")
+        at(173, lay_h, 2, 1, 1, "V")
+        at(174, exp_p, 0)
+        at(175, quant_h, 2, 0)
+        at(176, neg_p, 1, "A")
+        at(177, layer1, 3, 0, 2)
+        at(178, amp, 1)
+        at(179, relu_h, 3, 1, 1, "A")
+        at(180, turn_w, 0, 6, "T")
+        at(181, relu_h, 3, 0, 2, "A")
+        at(182, turn_w, 0, 3, "M")
+        at(183, power, 1, 2)
+        at(184, quant_h, 2, 1)
+        at(185, turn_w, 0, 5, "M")
+        at(186, power, 1, 5)
+        at(187, lay_h, 3, 1, 1, "V")
+        at(188, exp_w, 0, 0)
+        at(189, sum_p, 0, "M")
+        at(190, hazard, 1, 2, "V")
+        at(191, layer1, 3, 0, 1)
+        at(192, min_w, 0, 6)
+        at(193, relu_h, 3, 0, 1, "A")
+        at(194, hazard, 1, 5, "P")
+        at(195, head, 2, 0)
+        at(196, min_w, 0, 3)
+        at(197, min_w, 0, 5)
+        at(198, layer1, 3, 0, 0)
+        at(199, head, 2, 1)
+        at(200, shape_k, 2)
+        at(201, hazard, 1, 3, "P")
+        at(202, layer1, 3, 0, 3)
+        at(203, keep_norm, 0, "V")
+        at(204, power, 1, 4)
+        at(205, turn_p, 1)
+        at(206, sub_w, 0, 6)
+        at(207, relu_h, 3, 0, 0, "A")
+        at(208, sub_w, 0, 3)
+        at(209, min_p, 1)
+        at(210, lay_h, 3, 1, 0, "P")
+        at(211, warm_pe, 3)
+        at(212, dup_p, 1)
+        at(213, power, 1, 7)
+        at(214, turn_w, 1, 3, "T")
+        at(215, log_scale, 2)
+        at(216, turn_w, 1, 2, "M")
+        at(217, warm_pe, 5)
+        at(218, exp_k, 2)
+        at(219, sub_w, 0, 5)
+        at(220, k_times_l, 2, "P")
+        at(221, exp_w, 0, 1)
+        at(222, quant_h, 3, 1)
+        at(223, min_w, 1, 3)
+        at(224, relu_h, 3, 0, 3, "A")
         at(225, sub_p, 1)
-        at(226, turn_w, 1, 5, "T")
-        at(227, relu_h, 3, 0, 1, "V")
-        at(228, exp_w, 0, 2)
-        at(229, power, 1, 7)
-        at(230, relu_h, 3, 0, 0, "A")
-        at(231, turn_w, 1, 3, "T")
-        at(232, power, 1, 1)
-        at(233, sub_w, 1, 4)
-        at(234, hazard, 1, 6, "P")
-        at(235, power, 1, 0)
-        at(236, layer1, 3, 1, 0)
-        at(237, min_w, 1, 3)
+        at(226, power, 1, 1)
+        at(227, min_w, 1, 2)
+        at(228, warm_pe, 0)
+        at(229, turn_w, 0, 4, "M")
+        at(230, head, 2, 2)
+        at(231, warm_pe, 4)
+        at(232, sub_w, 1, 3)
+        at(233, sub_w, 1, 2)
+        at(234, exp_p, 1)
+        at(235, sum_w, 0, 0, "T")
+        at(236, min_w, 0, 4)
+        at(237, turn_w, 1, 5, "T")
         at(238, min_w, 1, 5)
-        at(239, dup_p, 1)
-        at(240, turn_w, 1, 2, "T")
-        at(241, hazard, 1, 7, "V")
-        at(242, sub_w, 1, 5)
-        at(243, sub_w, 1, 3)
-        at(244, min_w, 1, 2)
-        at(245, hazard, 1, 1, "P")
-        at(246, exp_p, 1)
-        at(247, exp_w, 0, 3)
-        at(248, head, 2, 1)
-        at(249, log_scale, 2)
-        at(250, power, 2, 4)
-        at(251, sum_w, 0, 2, "T")
-        at(252, relu_h, 3, 1, 0, "A")
-        at(253, exp_w, 1, 2)
-        at(254, layer1, 3, 1, 2)
-        at(255, k_times_l, 2, "V")
-        at(256, turn_w, 1, 6, "T")
-        at(257, power, 2, 2)
-        at(258, amp, 2)
-        at(259, turn_w, 1, 1, "T")
-        at(260, sum_w, 0, 3, "N")
-        at(261, sub_w, 1, 2)
-        at(262, min_w, 1, 6)
-        at(263, head, 2, 2)
-        at(264, turn_w, 1, 7, "T")
-        at(265, min_w, 1, 1)
-        at(266, sub_w, 1, 6)
-        at(267, sub_w, 1, 1)
-        at(268, keep_sums, 0, "A")
-        at(269, power, 2, 6)
-        at(270, lay_h, 3, 0, 0, "P")
-        at(271, hazard, 2, 2, "V")
-        at(272, hazard, 1, 0, "P")
-        at(273, hazard, 2, 4, "V")
-        at(274, relu_h, 3, 1, 2, "A")
-        at(275, lay_h, 3, 0, 1, "P")
-        at(276, min_w, 1, 7)
-        at(277, turn_w, 1, 0, "M")
-        at(278, sum_p, 1, "N")
+        at(239, sub_w, 0, 4)
+        at(240, hazard, 1, 7, "P")
+        at(241, hazard, 1, 4, "P")
+        at(242, hazard, 1, 1, "P")
+        at(243, lay_h, 3, 0, 1, "V")
+        at(244, sum_w, 0, 1, "T")
+        at(245, turn_w, 1, 4, "T")
+        at(246, neg_p, 2, "A")
+        at(247, power, 1, 0)
+        at(248, amp, 2)
+        at(249, exp_w, 0, 3)
+        at(250, power, 1, 6)
+        at(251, sub_w, 1, 5)
+        at(252, sum_p, 1, "M")
+        at(253, lay_h, 3, 0, 0, "P")
+        at(254, keep_norm, 1, "V")
+        at(255, min_w, 1, 4)
+        at(256, turn_w, 1, 7, "T")
+        at(257, exp_w, 0, 2)
+        at(258, min_w, 1, 7)
+        at(259, sub_w, 1, 4)
+        at(260, sum_w, 0, 3, "T")
+        at(261, hazard, 1, 0, "P")
+        at(262, quant_h, 3, 0)
+        at(263, power, 2, 3)
+        at(264, turn_w, 1, 1, "M")
+        at(265, turn_p, 2)
+        at(266, min_p, 2)
+        at(267, hazard, 1, 6, "P")
+        at(268, dup_p, 2)
+        at(269, sum_w, 0, 2, "M")
+        at(270, sub_w, 1, 7)
+        at(271, exp_w, 1, 1)
+        at(272, power, 2, 2)
+        at(273, power, 2, 0)
+        at(274, sub_p, 2)
+        at(275, min_w, 1, 1)
+        at(276, turn_w, 1, 0, "M")
+        at(277, exp_w, 1, 2)
+        at(278, hazard, 2, 3, "P")
         at(279, min_w, 1, 0)
-        at(280, neg_p, 2, "A")
-        at(281, exp_w, 1, 1)
-        at(282, sum_w, 1, 2, "T")
-        at(283, keep_norm, 1, "A")
-        at(284, turn_w, 2, 2, "N")
-        at(285, sub_w, 1, 7)
-        at(286, lay_h, 3, 1, 0, "V")
-        at(287, lay_h, 3, 1, 1, "P")
-        at(288, power, 2, 5)
-        at(289, quant_h, 3, 0)
-        at(290, sum_w, 1, 1, "M")
-        at(291, quant_h, 3, 1)
-        at(292, hazard, 2, 6, "V")
-        at(293, sub_w, 1, 0)
-        at(294, exp_w, 1, 3)
-        at(295, turn_p, 2)
-        at(296, min_p, 2)
-        at(297, min_w, 2, 2)
-        at(298, head, 3, 0)
-        at(299, power, 2, 3)
-        at(300, head, 3, 1)
-        at(301, sum_w, 1, 3, "T")
-        at(302, sub_p, 2)
-        at(303, sub_w, 2, 2)
-        at(304, turn_w, 2, 4, "N")
-        at(305, power, 2, 7)
-        at(306, hazard, 2, 3, "P")
-        at(307, turn_w, 2, 3, "T")
-        at(308, power, 2, 1)
-        at(309, shape_k, 3)
-        at(310, hazard, 2, 5, "P")
-        at(311, min_w, 2, 4)
-        at(312, turn_w, 2, 5, "N")
-        at(313, hazard, 2, 7, "P")
-        at(314, min_w, 2, 3)
-        at(315, log_scale, 3)
-        at(316, exp_k, 3)
-        at(317, exp_w, 1, 0)
-        at(318, sub_w, 2, 4)
-        at(319, power, 2, 0)
-        at(320, sum_w, 1, 0, "M")
-        at(321, sub_w, 2, 3)
-        at(322, power, 3, 2)
-        at(323, min_w, 2, 5)
-        at(324, turn_w, 2, 6, "T")
-        at(325, head, 3, 2)
-        at(326, exp_p, 2)
-        at(327, min_w, 2, 6)
-        at(328, k_times_l, 3, "P")
-        at(329, power, 3, 4)
-        at(330, dup_p, 2)
-        at(331, hazard, 2, 1, "P")
-        at(332, sub_w, 2, 5)
-        at(333, amp, 3)
-        at(334, turn_w, 2, 7, "T")
-        at(335, exp_w, 2, 1)
-        at(336, sub_w, 2, 6)
-        at(337, min_w, 2, 7)
-        at(338, hazard, 2, 0, "P")
-        at(339, keep_sums, 1, "V")
-        at(340, hazard, 3, 2, "P")
-        at(341, sub_w, 2, 7)
-        at(342, hazard, 3, 4, "P")
-        at(343, sum_p, 2, "M")
-        at(344, exp_w, 2, 2)
-        at(345, turn_w, 2, 1, "M")
-        at(346, min_w, 2, 1)
-        at(347, turn_w, 2, 0, "M")
-        at(348, power, 3, 0)
-        at(349, neg_p, 3, "V")
-        at(350, sum_w, 2, 1, "M")
-        at(351, min_w, 2, 0)
-        at(352, power, 3, 5)
-        at(353, power, 3, 6)
-        at(354, sum_w, 2, 2, "M")
-        at(355, sub_w, 2, 1)
-        at(356, turn_w, 3, 4, "M")
-        at(357, sub_w, 2, 0)
-        at(358, exp_w, 2, 3)
-        at(359, turn_w, 3, 2, "T")
-        at(360, min_w, 3, 4)
-        at(361, min_w, 3, 2)
-        at(362, hazard, 3, 0, "P")
-        at(363, turn_w, 3, 0, "N")
-        at(364, power, 3, 3)
+        at(280, head, 3, 0)
+        at(281, power, 2, 1)
+        at(282, head, 3, 1)
+        at(283, shape_k, 3)
+        at(284, head, 3, 2)
+        at(285, sub_w, 1, 1)
+        at(286, turn_w, 1, 6, "T")
+        at(287, exp_p, 2)
+        at(288, sum_p, 2, "T")
+        at(289, turn_w, 2, 3, "T")
+        at(290, keep_sums, 0, "V")
+        at(291, sub_w, 1, 0)
+        at(292, hazard, 2, 2, "P")
+        at(293, log_scale, 3)
+        at(294, min_w, 1, 6)
+        at(295, keep_norm, 2, "V")
+        at(296, hazard, 2, 1, "P")
+        at(297, sum_w, 1, 1, "T")
+        at(298, min_w, 2, 3)
+        at(299, sub_w, 1, 6)
+        at(300, sub_w, 2, 3)
+        at(301, neg_p, 3, "A")
+        at(302, turn_p, 3)
+        at(303, sum_w, 1, 2, "T")
+        at(304, power, 2, 5)
+        at(305, power, 2, 4)
+        at(306, min_p, 3)
+        at(307, turn_w, 2, 2, "T")
+        at(308, min_w, 2, 2)
+        at(309, exp_k, 3)
+        at(310, turn_w, 2, 1, "T")
+        at(311, hazard, 2, 0, "P")
+        at(312, exp_w, 1, 0)
+        at(313, min_w, 2, 1)
+        at(314, sub_w, 2, 2)
+        at(315, turn_w, 2, 0, "T")
+        at(316, min_w, 2, 0)
+        at(317, sub_p, 3)
+        at(318, power, 2, 7)
+        at(319, exp_w, 1, 3)
+        at(320, hazard, 2, 5, "P")
+        at(321, hazard, 2, 4, "P")
+        at(322, sub_w, 2, 1)
+        at(323, power, 2, 6)
+        at(324, sum_w, 1, 0, "T")
+        at(325, sum_w, 1, 3, "M")
+        at(326, keep_sums, 1, "V")
+        at(327, turn_w, 2, 4, "T")
+        at(328, sub_w, 2, 0)
+        at(329, k_times_l, 3, "P")
+        at(330, turn_w, 2, 5, "N")
+        at(331, min_w, 2, 4)
+        at(332, min_w, 2, 5)
+        at(333, power, 3, 2)
+        at(334, sub_w, 2, 4)
+        at(335, sub_w, 2, 5)
+        at(336, exp_w, 2, 1)
+        at(337, amp, 3)
+        at(338, hazard, 2, 7, "P")
+        at(339, turn_w, 2, 7, "T")
+        at(340, power, 3, 3)
+        at(341, hazard, 2, 6, "P")
+        at(342, sum_w, 2, 1, "N")
+        at(343, min_w, 2, 7)
+        at(344, turn_w, 2, 6, "T")
+        at(345, min_w, 2, 6)
+        at(346, power, 3, 0)
+        at(347, sub_w, 2, 7)
+        at(348, exp_w, 2, 0)
+        at(349, exp_p, 3)
+        at(350, sub_w, 2, 6)
+        at(351, power, 3, 1)
+        at(352, hazard, 3, 2, "P")
+        at(353, turn_w, 3, 2, "T")
+        at(354, hazard, 3, 3, "P")
+        at(355, hazard, 3, 0, "P")
+        at(356, sum_w, 2, 0, "M")
+        at(357, hazard, 3, 1, "P")
+        at(358, min_w, 3, 2)
+        at(359, power, 3, 4)
+        at(360, turn_w, 3, 3, "T")
+        at(361, min_w, 3, 3)
+        at(362, exp_w, 2, 2)
+        at(363, sub_w, 3, 2)
+        at(364, dup_p, 3)
         at(365, power, 3, 7)
-        at(366, sub_w, 3, 4)
-        at(367, exp_w, 2, 0)
-        at(368, keep_norm, 2, "V")
-        at(369, min_w, 3, 0)
-        at(370, sub_w, 3, 2)
-        at(371, hazard, 3, 5, "P")
-        at(372, power, 3, 1)
-        at(373, sum_w, 2, 3, "T")
-        at(374, sub_w, 3, 0)
-        at(375, hazard, 3, 3, "P")
-        at(376, log_norm, 2)
-        at(377, log_norm, 0)
-        at(378, hazard, 3, 1, "P")
-        at(379, offset, 0, "P")
-        at(380, sum_w, 2, 0, "N")
-        at(381, turn_w, 3, 5, "T")
-        at(382, logs, 0)
-        at(383, keep_sums, 2, "V")
-        at(384, hazard, 3, 7, "P")
-        at(385, turn_w, 3, 1, "N")
-        at(386, min_w, 3, 5)
-        at(387, sub_w, 3, 5)
-        at(388, min_w, 3, 1)
-        at(389, logs, 1)
-        at(390, turn_p, 3)
-        at(391, turn_w, 3, 3, "N")
-        at(392, min_p, 3)
-        at(393, min_w, 3, 3)
-        at(394, sub_w, 3, 1)
-        at(395, sub_p, 3)
-        at(396, turn_w, 3, 7, "M")
-        at(397, logs, 2)
-        at(398, log_norm, 1)
-        at(399, hazard, 3, 6, "P")
-        at(400, turn_back, 0, "N")
-        at(401, sub_w, 3, 3)
-        at(402, turn_w, 3, 6, "T")
-        at(403, exp_w, 3, 2)
-        at(404, exp_p, 3)
-        at(405, min_w, 3, 7)
-        at(406, min_w, 3, 6)
-        at(407, exp_w, 3, 0)
-        at(408, sum_w, 3, 2, "N")
-        at(409, dup_p, 3)
-        at(410, sub_w, 3, 7)
-        at(411, exp_w, 3, 1)
-        at(412, sub_w, 3, 6)
-        at(413, sum_p, 3, "M")
-        at(414, offset, 1, "P")
-        at(415, sum_w, 3, 0, "T")
-        at(416, turn_back, 1, "N")
-        at(417, result, 1)
-        at(418, exp_w, 3, 3)
-        at(419, sum_w, 3, 1, "T")
-        at(420, offset, 2, "P")
-        at(421, keep_norm, 3, "V")
-        at(422, sum_w, 3, 3, "M")
-        at(423, log_norm, 3)
-        at(424, result, 0)
-        at(425, lay_out, 1, "P")
-        at(426, turn_back, 2, "N")
-        at(427, offset, 3, "V")
-        at(428, result, 2)
-        at(429, logs, 3)
-        at(430, lay_out, 0, "A")
-        at(431, turn_back, 3, "T")
-        at(432, quant_out, 1)
-        at(433, result, 3)
-        at(434, lay_out, 2, "A")
-        at(435, quant_out, 0)
-        at(436, lay_out, 3, "V")
-        at(437, quant_out, 2)
-        at(438, quant_out, 3)
+        at(366, power, 3, 6)
+        at(367, exp_w, 2, 3)
+        at(368, turn_w, 3, 0, "T")
+        at(369, sum_w, 2, 2, "M")
+        at(370, sub_w, 3, 3)
+        at(371, turn_w, 3, 1, "M")
+        at(372, min_w, 3, 0)
+        at(373, min_w, 3, 1)
+        at(374, power, 3, 5)
+        at(375, sub_w, 3, 0)
+        at(376, exp_w, 3, 1)
+        at(377, hazard, 3, 4, "P")
+        at(378, logs, 1)
+        at(379, sum_w, 2, 3, "M")
+        at(380, sum_p, 3, "N")
+        at(381, sub_w, 3, 1)
+        at(382, keep_sums, 2, "V")
+        at(383, logs, 2)
+        at(384, keep_norm, 3, "V")
+        at(385, log_norm, 0)
+        at(386, logs, 0)
+        at(387, hazard, 3, 6, "P")
+        at(388, turn_w, 3, 6, "T")
+        at(389, min_w, 3, 6)
+        at(390, hazard, 3, 7, "P")
+        at(391, turn_w, 3, 4, "T")
+        at(392, hazard, 3, 5, "P")
+        at(393, sub_w, 3, 6)
+        at(394, offset, 0, "P")
+        at(395, exp_w, 3, 0)
+        at(396, turn_w, 3, 7, "N")
+        at(397, turn_w, 3, 5, "M")
+        at(398, min_w, 3, 4)
+        at(399, sum_w, 3, 1, "M")
+        at(400, min_w, 3, 7)
+        at(401, min_w, 3, 5)
+        at(402, turn_back, 1, "N")
+        at(403, sum_w, 3, 0, "T")
+        at(404, sub_w, 3, 7)
+        at(405, sub_w, 3, 5)
+        at(406, turn_back, 0, "T")
+        at(407, sub_w, 3, 4)
+        at(408, exp_w, 3, 3)
+        at(409, exp_w, 3, 2)
+        at(410, sum_w, 3, 3, "T")
+        at(411, sum_w, 3, 2, "M")
+        at(412, result, 1)
+        at(413, result, 0)
+        at(414, lay_out, 0, "P")
+        at(415, lay_out, 1, "P")
+        at(416, turn_back, 2, "M")
+        at(417, logs, 3)
+        at(418, turn_back, 3, "T")
+        at(419, result, 2)
+        at(420, quant_out, 0)
+        at(421, result, 3)
+        at(422, quant_out, 1)
+        at(423, lay_out, 2, "P")
+        at(424, lay_out, 3, "V")
+        at(425, quant_out, 2)
+        at(426, quant_out, 3)
 
         for when, n, fn, args in sorted(plan, key=lambda e: e[0:2]):
             fn(*args)

from contextlib import ExitStack

import concourse.mybir as mybir
from concourse.masks import make_identity

N, D, H, R, M, T = 2048, 1024, 1024, 16, 8, 8
FLOPS = 2 * N * D * H + 3 * 2 * N * H * R * M

F32 = mybir.dt.float32
BF16 = mybir.dt.bfloat16
I32 = mybir.dt.int32
U32 = mybir.dt.uint32
U8 = mybir.dt.uint8
FP8X4 = mybir.dt.float8_e4m3fn_x4
FP4X4 = mybir.dt.float4_e2m1fn_x4
ACT = mybir.ActivationFunctionType
ALU = mybir.AluOpType
AX = mybir.AxisListType

P = 128
G = 512
GROUPS = N // G
SR = 4 * R
AL = 64


def tile_deepsurvivalmachinesweibullriskcurves_x2_kernel(
    tc, x, w1_words, w1_scales, b1, ws, wc, wp, t, out_0, out_1, out_2
):
    nc = tc.nc
    with ExitStack() as ctx:
        keep = ctx.enter_context(tc.tile_pool(name="keep", bufs=1))
        work = ctx.enter_context(tc.tile_pool(name="work", bufs=2))
        psum = ctx.enter_context(tc.psum_pool(name="psum", bufs=1))
        ctx.enter_context(tc.manual_schedule())

        ident = keep.tile([P, P], F32, name="ident")
        w1_raw = [keep.tile([P, 2, 2 * G], U8, name="w1_raw%d" % j, align_bytes=AL) for j in range(2)]
        s1_raw = keep.tile([P, 2, H], U8, name="s1_raw", align_bytes=AL)
        w1c = [keep.tile([P, 2, 2 * G], U8, name="w1c%d" % j, align_bytes=AL) for j in range(2)]
        w1s = [keep.tile([P, 2, G], U8, name="w1s%d" % j, align_bytes=AL) for j in range(2)]
        bias = keep.tile([P, 2, 4], BF16, name="bias")
        t_sb = keep.tile([P, T], BF16, name="t_sb")
        logt = keep.tile([P, T], F32, name="logt")
        hw_raw = [keep.tile([P, 2, 4, P], BF16, name="hw_raw%d" % j) for j in range(3)]
        hwc = [keep.tile([P, 2, P], U32, name="hwc%d" % j, align_bytes=AL) for j in range(3)]
        hws = [keep.tile([P, 2, P], U8, name="hws%d" % j, align_bytes=AL) for j in range(3)]
        x_sb = [[keep.tile([P, 4, G], BF16, name="x_sb%d_%d" % (g, kg)) for kg in range(2)] for g in range(GROUPS)]
        wmin = [keep.tile([P, T, SR], F32, name="wmin%d" % g) for g in range(GROUPS)]
        sums = [keep.tile([P, 4, P], F32, name="sums%d" % g) for g in range(GROUPS)]
        norm = keep.tile([P, 2, GROUPS, P], F32, name="norm")
        out_scales = keep.tile([P, GROUPS, P], U8, name="out_scales", align_bytes=AL)

        def load_x(g, kg):
            rows = x[G * g : G * (g + 1), G * kg : G * (kg + 1)]
            nc.sync.dma_start(out=x_sb[g][kg][:], in_=rows.rearrange("(p s) k -> p s k", s=4))

        def load_w1(hg):
            src = w1_words[:, :, 2 * G * hg : 2 * G * (hg + 1)].rearrange("g p b -> p g b")
            nc.sync.dma_start(out=w1_raw[hg][:].bitcast(I32), in_=src.bitcast(I32))

        nc.vector.memset(s1_raw[:].bitcast(I32), 0)
        make_identity(nc, ident[:])
        nc.scalar.dma_start(out=t_sb[:], in_=t.partition_broadcast(P))
        for q in range(4):
            nc.scalar.dma_start(
                out=s1_raw[32 * q : 32 * q + 4].bitcast(I32),
                in_=w1_scales[:, 4 * q : 4 * q + 4, :].rearrange("g r n -> r g n").bitcast(I32),
            )
        load_x(0, 0)
        load_w1(0)
        load_x(0, 1)
        load_w1(1)
        nc.sync.dma_start(out=bias[:], in_=b1.rearrange("(g p j) -> p g j", g=2, j=4))
        load_x(1, 0)
        for j, w in enumerate((ws, wc, wp)):
            nc.sync.dma_start(out=hw_raw[j][:], in_=w.rearrange("(g p j) r m -> p g j (r m)", g=2, j=4))
        load_x(1, 1)
        for g in range(2, GROUPS):
            load_x(g, 0)
            load_x(g, 1)
        nc.scalar.activation(out=logt[:], in_=t_sb[:], func=ACT.Ln)
        warm = keep.tile([P, 1], F32, name="warm")
        nc.scalar.activation(out=warm[:], in_=logt[:, 0:1], func=ACT.Tanh)

        warm_bank = psum.tile([P, G], F32, name="sbank", bufs=1)

        def warm_pe(j):
            nc.tensor.matmul(warm_bank[:, P * (j % 4) : P * (j % 4 + 1)], ident[:], ident[:], start=True, stop=True)

        def order_w1(hg, kg):
            nc.vector.tensor_copy(
                out=w1c[hg][:, kg, :].rearrange("p (j m e) -> p j m e", j=4, e=2),
                in_=w1_raw[hg][:, kg, :].rearrange("p (m j e) -> p j m e", j=4, e=2),
            )

        def order_s1(hg):
            nc.vector.tensor_copy(
                out=w1s[hg][:].rearrange("p g (j m) -> p g j m", j=4),
                in_=s1_raw[:, :, G * hg : G * (hg + 1)].rearrange("p g (m j) -> p g j m", j=4),
            )

        def lay_head(j, eng):
            laid = work.tile([P, 2, P, 4], BF16, name="head_laid", bufs=3, align_bytes=AL)
            src = hw_raw[j][:].rearrange("p g j n -> p g n j")
            if eng == "P":
                nc.gpsimd.tensor_scalar(out=laid[:], in0=src, scalar1=1.0, scalar2=0.0, op0=ALU.mult, op1=ALU.add)
            else:
                nc.vector.tensor_copy(out=laid[:], in_=src)
            st["head", j] = laid

        def quant_head(j):
            nc.vector.quantize_mx(
                out=hwc[j][:].rearrange("p g n -> p (g n)").bitcast(FP8X4),
                scales=hws[j][:].rearrange("p g n -> p (g n)"),
                in_=st["head", j][:].rearrange("p g n j -> p (g n j)"),
            )

        st = {}

        def front_bank():
            return psum.tile([P, G], F32, name="front", bufs=3)

        def w_bank():
            return psum.tile([P, G], F32, name="wbank", bufs=3)

        def turn_x(g, kg, sp):
            if ("xg", g, kg) not in st:
                st["xg", g, kg] = work.tile([P, G, 4], BF16, name="xg", bufs=3, align_bytes=AL)
            bank = w_bank() if g < 2 else front_bank()
            words = x_sb[g][kg][:].bitcast(F32)
            for s in range(2):
                for u in range(2):
                    c = P * (2 * s + u)
                    nc.tensor.transpose(bank[:, c : c + P], words[:, 2 * sp + s, u : 256 : 2], ident[:])
            st["xb", g, kg, sp] = bank

        def copy_x(g, kg, sp, eng):
            dst = st["xg", g, kg][:, 256 * sp : 256 * (sp + 1), :].bitcast(F32).rearrange("p (s n) u -> p s n u", s=2)
            src = st["xb", g, kg, sp][:].rearrange("p (s u n) -> p s n u", s=2, u=2)
            if eng == "A":
                nc.scalar.copy(out=dst, in_=src)
            else:
                nc.vector.tensor_copy(out=dst, in_=src)

        def quant_x(g, kg):
            codes = work.tile([P, G], U32, name="xc", bufs=4, align_bytes=AL)
            scales = work.tile([P, G], U8, name="xs", bufs=4, align_bytes=AL)
            nc.vector.quantize_mx(
                out=codes[:].bitcast(FP8X4), scales=scales[:], in_=st["xg", g, kg][:].rearrange("p n j -> p (n j)")
            )
            st["xq", g, kg] = (codes, scales)

        def layer1(g, hg, j):
            bank = front_bank()
            for kg in range(2):
                codes, scales = st["xq", g, kg]
                nc.tensor.matmul_mx(
                    out=bank[:],
                    lhsT=w1c[hg][:, kg, 2 * P * j : 2 * P * (j + 1)].bitcast(FP4X4),
                    lhsT_scale=w1s[hg][:, kg, P * j : P * (j + 1)],
                    rhs=codes[:].bitcast(FP8X4),
                    rhs_scale=scales[:],
                    start=(kg == 0),
                    stop=(kg == 1),
                )
            st["hb", g, hg, j] = bank

        def relu_h(g, hg, j, eng):
            if ("h", g, hg) not in st:
                st["h", g, hg] = work.tile([P, 4, G], BF16, name="h", bufs=3)
            dst, src, b = st["h", g, hg][:, j, :], st["hb", g, hg, j][:], bias[:, hg, j : j + 1]
            if eng == "A":
                nc.scalar.activation(out=dst, in_=src, func=ACT.Relu, bias=b)
            else:
                nc.vector.tensor_scalar(out=dst, in0=src, scalar1=b, scalar2=0.0, op0=ALU.add, op1=ALU.max)

        def lay_h(g, hg, half, eng):
            if ("hl", g, hg) not in st:
                st["hl", g, hg] = work.tile([P, G, 4], BF16, name="h_laid", bufs=2, align_bytes=AL)
            cols = slice(256 * half, 256 * (half + 1))
            dst = st["hl", g, hg][:, cols, :].rearrange("p (c i) j -> p c j i", i=4)
            src = st["h", g, hg][:, :, cols].rearrange("p j (c i) -> p c j i", i=4)
            if eng == "P":
                dst = st["hl", g, hg][:, cols, :]
                src = st["h", g, hg][:, :, cols].rearrange("p j n -> p n j")
                nc.gpsimd.tensor_scalar(out=dst, in0=src, scalar1=1.0, scalar2=0.0, op0=ALU.mult, op1=ALU.add)
            else:
                move(eng, dst, src)

        def quant_h(g, hg):
            codes = work.tile([P, G], U32, name="hc", bufs=3, align_bytes=AL)
            scales = work.tile([P, G], U8, name="hs", bufs=3, align_bytes=AL)
            nc.vector.quantize_mx(
                out=codes[:].bitcast(FP8X4), scales=scales[:], in_=st["hl", g, hg][:].rearrange("p n j -> p (n j)")
            )
            st["hq", g, hg] = (codes, scales)

        def head(g, j):
            bank = front_bank()
            for hg in range(2):
                codes, scales = st["hq", g, hg]
                nc.tensor.matmul_mx(
                    out=bank[:],
                    lhsT=hwc[j][:, hg, :].bitcast(FP8X4),
                    lhsT_scale=hws[j][:, hg, :],
                    rhs=codes[:].bitcast(FP8X4),
                    rhs_scale=scales[:],
                    start=(hg == 0),
                    stop=(hg == 1),
                )
            st["head_bank", g, j] = bank

        def shape_k(g):
            ths = work.tile([P, G], F32, name="ths", bufs=1)
            nc.scalar.activation(out=ths[:], in_=st["head_bank", g, 0][:], func=ACT.Tanh)
            st["ths", g] = ths

        def log_scale(g):
            lsc = work.tile([P, G], F32, name="lsc", bufs=1)
            nc.scalar.activation(out=lsc[:], in_=st["head_bank", g, 1][:], func=ACT.Tanh)
            st["l", g] = lsc

        def exp_k(g):
            k = work.tile([P, G], F32, name="k", bufs=2)
            nc.scalar.activation(out=k[:], in_=st["ths", g][:], func=ACT.Exp, scale=0.5)
            st["k", g] = k

        def neg_p(g, eng):
            negp = work.tile([P, G], F32, name="negp", bufs=2)
            src = st["head_bank", g, 2][:]
            if eng == "A":
                nc.scalar.activation(out=negp[:], in_=src, func=ACT.Copy, scale=-1.0)
            else:
                nc.vector.tensor_scalar(out=negp[:], in0=src, scalar1=-1.0, scalar2=None, op0=ALU.mult)
            st["np", g] = negp

        def k_times_l(g, eng):
            kl = work.tile([P, G], F32, name="kl", bufs=1)
            (nc.vector if eng == "V" else nc.gpsimd).tensor_tensor(out=kl[:], in0=st["k", g][:], in1=st["l", g][:], op=ALU.mult)
            st["kl", g] = kl

        def amp(g):
            a = work.tile([P, G], F32, name="amp", bufs=2)
            nc.scalar.activation(out=a[:], in_=st["kl", g][:], func=ACT.Exp, scale=-1.0)
            st["A", g] = a

        def turn_p(g):
            bank = psum.tile([P, G], F32, name="misc", bufs=1)
            for s in range(4):
                nc.tensor.transpose(bank[:, P * s : P * (s + 1)], st["np", g][:, P * s : P * (s + 1)], ident[:])
            st["p0", g] = bank

        def min_p(g):
            w0 = work.tile([P, 2, SR], F32, name="w0", bufs=1)
            nc.vector.tensor_reduce(
                out=w0[:, 0, :], in_=st["p0", g][:].rearrange("p (c m) -> p c m", m=M), axis=AX.X, op=ALU.min
            )
            st["w0", g] = w0

        def dup_p(g):
            nc.gpsimd.tensor_copy(out=st["w0", g][:, 1, :], in_=st["w0", g][:, 0, :])

        def sub_p(g):
            z0 = work.tile([P, M, SR], F32, name="z0", bufs=1)
            nc.vector.tensor_tensor(
                out=z0[:],
                in0=st["p0", g][:].rearrange("p (c m) -> p m c", m=M),
                in1=st["w0", g][:, 0:1, :].to_broadcast([P, M, SR]),
                op=ALU.subtract,
            )
            st["z0", g] = z0

        def exp_p(g):
            e0 = work.tile([P, M + 1, SR], F32, name="e0", bufs=1)
            nc.scalar.activation(out=e0[:, 0:M, :], in_=st["z0", g][:], func=ACT.Exp, scale=-1.0)
            nc.scalar.activation(out=e0[:, M, :], in_=st["z0", g][:, 0, :], func=ACT.Exp, scale=-1.0)
            st["e0", g] = e0

        def sum_p(g, eng):
            bank = psum.tile([P, G], F32, name="misc", bufs=1)
            e0 = st["e0", g][:].rearrange("p m c -> p (m c)")
            for m in range(M):
                nc.tensor.matmul(
                    bank[:, 0:P], e0[:, SR * m : SR * m + P], ident[:], start=(m == 0), stop=(m == M - 1),
                    is_transpose=(m not in (1, 3)[: "TMN".index(eng)]),
                )
            nc.tensor.transpose(bank[:, P : 2 * P], st["w0", g][:].rearrange("p d c -> p (d c)"), ident[:])
            st["s0", g] = bank

        def move(eng, dst, src):
            if eng == "A":
                nc.scalar.copy(out=dst, in_=src)
            else:
                nc.vector.tensor_copy(out=dst, in_=src)

        def keep_norm(g, eng):
            move(eng, norm[:, :, g, :], st["s0", g][:, 0 : 2 * P].rearrange("p (d c) -> p d c", d=2))

        def power(g, i):
            e = work.tile([P, G], F32, name="pow", bufs=4)
            nc.scalar.activation(out=e[:], in_=st["k", g][:], func=ACT.Exp, scale=logt[:, i : i + 1])
            st["E", g, i] = e

        def hazard(g, i, eng):
            cum = work.tile([P, G], F32, name="cum", bufs=4)
            (nc.vector if eng == "V" else nc.gpsimd).tensor_tensor(out=cum[:], in0=st["E", g, i][:], in1=st["A", g][:], op=ALU.mult)
            st["cum", g, i] = cum

        def turn_w(g, i, eng):
            bank = w_bank()
            for s in range(4):
                cols = slice(P * s, P * (s + 1))
                nc.tensor.matmul(bank[:, cols], st["cum", g, i][:, cols], ident[:], start=True, stop=False, is_transpose=True)
                nc.tensor.matmul(bank[:, cols], st["np", g][:, cols], ident[:], start=False, stop=True, is_transpose=(s >= "TMN".index(eng)))
            st["w", g, i] = bank

        def min_w(g, i):
            nc.vector.tensor_reduce(
                out=wmin[g][:, i, :], in_=st["w", g, i][:].rearrange("p (c m) -> p c m", m=M), axis=AX.X, op=ALU.min
            )

        def sub_w(g, i):
            if ("z", g, i // 2) not in st:
                st["z", g, i // 2] = work.tile([P, M, 2, SR], F32, name="z", bufs=3)
            nc.vector.tensor_tensor(
                out=st["z", g, i // 2][:, :, i % 2, :],
                in0=st["w", g, i][:].rearrange("p (c m) -> p m c", m=M),
                in1=wmin[g][:, i : i + 1, :].to_broadcast([P, M, SR]),
                op=ALU.subtract,
            )

        def exp_w(g, q):
            e = work.tile([P, M, P], F32, name="e", bufs=2)
            nc.scalar.activation(
                out=e[:], in_=st["z", g, q][:].rearrange("p m d c -> p m (d c)"), func=ACT.Exp, scale=-1.0
            )
            st["e", g, q] = e

        def sum_w(g, q, eng):
            if ("s", g) not in st:
                st["s", g] = psum.tile([P, G], F32, name="sbank", bufs=1)
            for m in range(M):
                nc.tensor.matmul(
                    st["s", g][:, P * q : P * (q + 1)], st["e", g, q][:, m, :], ident[:],
                    start=(m == 0), stop=(m == M - 1), is_transpose=(m not in (1, 3)[: "TMN".index(eng)]),
                )

        def keep_sums(g, eng):
            move(eng, sums[g][:].rearrange("p q c -> p (q c)"), st["s", g][:])

        def log_norm(g):
            ln0 = work.tile([P, GROUPS, P], F32, name="ln0", bufs=1)
            nc.scalar.activation(out=ln0[:], in_=norm[:, 0], func=ACT.Ln)
            st["ln0"] = ln0

        def logs(g):
            lns = work.tile([P, G], F32, name="lns", bufs=4)
            src = st["s", g][:] if g == GROUPS - 1 else sums[g][:].rearrange("p q c -> p (q c)")
            nc.scalar.activation(out=lns[:], in_=src, func=ACT.Ln)
            st["ln", g] = lns

        def offset(g, eng):
            c0 = work.tile([P, GROUPS, P], F32, name="c0", bufs=1)
            (nc.vector if eng == "V" else nc.gpsimd).tensor_tensor(out=c0[:], in0=norm[:, 1], in1=st["ln0"][:], op=ALU.subtract)
            st["c0"] = c0

        def turn_back(g, eng):
            bank = front_bank()
            for q in range(4):
                cols = slice(P * q, P * (q + 1))
                nc.tensor.matmul(bank[:, cols], st["ln", g][:, cols], ident[:], start=True, stop=False, is_transpose=True)
                nc.tensor.matmul(bank[:, cols], st["c0"][:, g, :], ident[:], start=False, stop=True, is_transpose=(q >= "TMN".index(eng)))
            st["fin", g] = bank

        def result(g):
            res = work.tile([P, SR, T], F32, name="res", bufs=4)
            for hf in range(2):
                nc.vector.tensor_tensor(
                    out=res[:, :, 4 * hf : 4 * hf + 4],
                    in0=st["fin", g][:].rearrange("p (i c) -> p c i", i=T)[:, :, 4 * hf : 4 * hf + 4],
                    in1=wmin[g][:].rearrange("p i c -> p c i")[:, :, 4 * hf : 4 * hf + 4],
                    op=ALU.subtract,
                )
            nc.sync.dma_start(
                out=out_0[G * g : G * (g + 1)].rearrange("(p s) r i -> p (s r) i", s=4), in_=res[:]
            )
            st["res", g] = res

        def lay_out(g, eng):
            laid = work.tile([P, P, 4], BF16, name="out_laid", bufs=4, align_bytes=AL)
            src = st["res", g][:].rearrange("p (s r) i -> p (r i) s", s=4)
            if eng == "P":
                nc.gpsimd.tensor_scalar(out=laid[:], in0=src, scalar1=1.0, scalar2=0.0, op0=ALU.mult, op1=ALU.add)
            else:
                move(eng, laid[:], src)
            st["ol", g] = laid

        def quant_out(g):
            codes = work.tile([P, P], U32, name="out_codes", bufs=4, align_bytes=AL)
            nc.vector.quantize_mx(
                out=codes[:].bitcast(FP8X4), scales=out_scales[:, g, :], in_=st["ol", g][:].rearrange("p n j -> p (n j)")
            )
            nc.sync.dma_start(out=out_1[g].rearrange("p m j -> p (m j)").bitcast(I32), in_=codes[:].bitcast(I32))

        plan = []

        def at(when, fn, *args):
            plan.append((when, len(plan), fn, args))

        at(0, turn_x, 0, 0, 0)
        at(1, warm_pe, 2)
        at(2, order_s1, 0)
        at(3, turn_x, 0, 0, 1)
        at(4, copy_x, 0, 0, 0, "A")
        at(5, copy_x, 0, 0, 1, "A")
        at(6, order_w1, 0, 1)
        at(7, turn_x, 0, 1, 1)
        at(8, copy_x, 0, 1, 1, "A")
        at(9, turn_x, 0, 1, 0)
        at(10, order_s1, 1)
        at(11, order_w1, 1, 1)
        at(12, warm_pe, 1)
        at(13, order_w1, 1, 0)
        at(14, copy_x, 0, 1, 0, "A")
        at(15, lay_head, 1, "P")
        at(16, turn_x, 1, 0, 0)
        at(17, turn_x, 1, 0, 1)
        at(18, quant_x, 0, 0)
        at(19, order_w1, 0, 0)
        at(20, quant_x, 0, 1)
        at(21, layer1, 0, 0, 1)
        at(22, copy_x, 1, 0, 0, "A")
        at(23, lay_head, 2, "P")
        at(24, copy_x, 1, 0, 1, "A")
        at(25, relu_h, 0, 0, 1, "A")
        at(26, lay_head, 0, "V")
        at(27, layer1, 0, 0, 3)
        at(28, relu_h, 0, 0, 3, "A")
        at(29, layer1, 0, 0, 2)
        at(30, layer1, 0, 0, 0)
        at(31, layer1, 0, 1, 1)
        at(32, relu_h, 0, 0, 2, "A")
        at(33, quant_x, 1, 0)
        at(34, turn_x, 1, 1, 1)
        at(35, turn_x, 2, 0, 1)
        at(36, turn_x, 1, 1, 0)
        at(37, relu_h, 0, 0, 0, "A")
        at(38, relu_h, 0, 1, 1, "A")
        at(39, turn_x, 2, 1, 0)
        at(40, copy_x, 1, 1, 1, "A")
        at(41, turn_x, 2, 1, 1)
        at(42, copy_x, 2, 0, 1, "A")
        at(43, copy_x, 2, 1, 0, "A")
        at(44, copy_x, 2, 1, 1, "A")
        at(45, layer1, 0, 1, 0)
        at(46, copy_x, 1, 1, 0, "V")
        at(47, relu_h, 0, 1, 0, "A")
        at(48, layer1, 0, 1, 3)
        at(49, relu_h, 0, 1, 3, "A")
        at(50, layer1, 0, 1, 2)
        at(51, quant_x, 1, 1)
        at(52, lay_h, 0, 0, 1, "P")
        at(53, layer1, 1, 1, 2)
        at(54, relu_h, 0, 1, 2, "A")
        at(55, quant_head, 1)
        at(56, lay_h, 0, 0, 0, "V")
        at(57, quant_x, 2, 1)
        at(58, relu_h, 1, 1, 2, "A")
        at(59, layer1, 1, 1, 0)
        at(60, quant_h, 0, 0)
        at(61, layer1, 1, 1, 3)
        at(62, relu_h, 1, 1, 0, "A")
        at(63, lay_h, 0, 1, 1, "V")
        at(64, lay_h, 0, 1, 0, "P")
        at(65, relu_h, 1, 1, 3, "A")
        at(66, turn_x, 2, 0, 0)
        at(67, copy_x, 2, 0, 0, "A")
        at(68, layer1, 1, 1, 1)
        at(69, relu_h, 1, 1, 1, "A")
        at(70, layer1, 1, 0, 3)
        at(71, quant_head, 0)
        at(72, relu_h, 1, 0, 3, "A")
        at(73, quant_h, 0, 1)
        at(74, quant_x, 2, 0)
        at(75, quant_head, 2)
        at(76, lay_h, 1, 1, 1, "V")
        at(77, layer1, 1, 0, 1)
        at(78, relu_h, 1, 0, 1, "A")
        at(79, layer1, 1, 0, 0)
        at(80, relu_h, 1, 0, 0, "A")
        at(81, layer1, 1, 0, 2)
        at(82, relu_h, 1, 0, 2, "A")
        at(83, head, 0, 0)
        at(84, layer1, 2, 0, 3)
        at(85, lay_h, 1, 0, 1, "P")
        at(86, lay_h, 1, 1, 0, "V")
        at(87, shape_k, 0)
        at(88, head, 0, 1)
        at(89, exp_k, 0)
        at(90, relu_h, 2, 0, 3, "V")
        at(91, layer1, 2, 0, 1)
        at(92, log_scale, 0)
        at(93, relu_h, 2, 0, 1, "V")
        at(94, lay_h, 1, 0, 0, "V")
        at(95, power, 0, 0)
        at(96, power, 0, 1)
        at(97, power, 0, 2)
        at(98, turn_x, 3, 1, 1)
        at(99, layer1, 2, 1, 2)
        at(100, turn_x, 3, 1, 0)
        at(101, copy_x, 3, 1, 1, "V")
        at(102, copy_x, 3, 1, 0, "A")
        at(103, relu_h, 2, 1, 2, "V")
        at(104, head, 0, 2)
        at(105, quant_h, 1, 0)
        at(106, turn_x, 3, 0, 0)
        at(107, k_times_l, 0, "P")
        at(108, amp, 0)
        at(109, neg_p, 0, "A")
        at(110, quant_x, 3, 1)
        at(111, quant_h, 1, 1)
        at(112, hazard, 0, 1, "V")
        at(113, layer1, 2, 0, 0)
        at(114, layer1, 2, 0, 2)
        at(115, copy_x, 3, 0, 0, "A")
        at(116, relu_h, 2, 0, 0, "A")
        at(117, hazard, 0, 0, "V")
        at(118, power, 0, 7)
        at(119, turn_x, 3, 0, 1)
        at(120, power, 0, 5)
        at(121, copy_x, 3, 0, 1, "A")
        at(122, hazard, 0, 2, "V")
        at(123, power, 0, 6)
        at(124, turn_p, 0)
        at(125, power, 0, 4)
        at(126, turn_w, 0, 1, "T")
        at(127, relu_h, 2, 0, 2, "V")
        at(128, hazard, 0, 7, "P")
        at(129, turn_w, 0, 0, "T")
        at(130, min_w, 0, 1)
        at(131, power, 0, 3)
        at(132, layer1, 2, 1, 0)
        at(133, relu_h, 2, 1, 0, "A")
        at(134, hazard, 0, 6, "P")
        at(135, quant_x, 3, 0)
        at(136, min_w, 0, 0)
        at(137, sub_w, 0, 1)
        at(138, head, 1, 0)
        at(139, lay_h, 2, 0, 0, "V")
        at(140, shape_k, 1)
        at(141, layer1, 3, 1, 2)
        at(142, min_p, 0)
        at(143, hazard, 0, 5, "P")
        at(144, turn_w, 0, 2, "T")
        at(145, min_w, 0, 2)
        at(146, sub_w, 0, 0)
        at(147, head, 1, 1)
        at(148, relu_h, 3, 1, 2, "A")
        at(149, exp_k, 1)
        at(150, turn_w, 0, 7, "T")
        at(151, log_scale, 1)
        at(152, sub_w, 0, 2)
        at(153, layer1, 2, 1, 3)
        at(154, power, 1, 3)
        at(155, layer1, 2, 1, 1)
        at(156, min_w, 0, 7)
        at(157, relu_h, 2, 1, 3, "A")
        at(158, lay_h, 2, 0, 1, "P")
        at(159, layer1, 3, 1, 0)
        at(160, sub_p, 0)
        at(161, relu_h, 2, 1, 1, "A")
        at(162, sub_w, 0, 7)
        at(163, layer1, 3, 1, 3)
        at(164, layer1, 3, 1, 1)
        at(165, k_times_l, 1, "V")
        at(166, relu_h, 3, 1, 0, "A")
        at(167, dup_p, 0)
        at(168, relu_h, 3, 1, 3, "A")
        at(169, hazard, 0, 3, "P")
        at(170, head, 1, 2)
        at(171, lay_h, 2, 1, 0, "V")
        at(172, hazard, 0, 4, "V")
        at(173, lay_h, 2, 1, 1, "V")
        at(174, exp_p, 0)
        at(175, quant_h, 2, 0)
        at(176, neg_p, 1, "A")
        at(177, layer1, 3, 0, 2)
        at(178, amp, 1)
        at(179, relu_h, 3, 1, 1, "A")
        at(180, turn_w, 0, 6, "T")
        at(181, relu_h, 3, 0, 2, "A")
        at(182, turn_w, 0, 3, "M")
        at(183, power, 1, 2)
        at(184, quant_h, 2, 1)
        at(185, turn_w, 0, 5, "M")
        at(186, power, 1, 5)
        at(187, lay_h, 3, 1, 1, "V")
        at(188, exp_w, 0, 0)
        at(189, sum_p, 0, "M")
        at(190, hazard, 1, 2, "V")
        at(191, layer1, 3, 0, 1)
        at(192, min_w, 0, 6)
        at(193, relu_h, 3, 0, 1, "A")
        at(194, hazard, 1, 5, "P")
        at(195, head, 2, 0)
        at(196, min_w, 0, 3)
        at(197, min_w, 0, 5)
        at(198, layer1, 3, 0, 0)
        at(199, head, 2, 1)
        at(200, shape_k, 2)
        at(201, hazard, 1, 3, "P")
        at(202, layer1, 3, 0, 3)
        at(203, keep_norm, 0, "V")
        at(204, power, 1, 4)
        at(205, turn_p, 1)
        at(206, sub_w, 0, 6)
        at(207, relu_h, 3, 0, 0, "A")
        at(208, sub_w, 0, 3)
        at(209, min_p, 1)
        at(210, lay_h, 3, 1, 0, "P")
        at(211, warm_pe, 3)
        at(212, dup_p, 1)
        at(213, power, 1, 7)
        at(214, turn_w, 1, 3, "T")
        at(215, log_scale, 2)
        at(216, turn_w, 1, 2, "M")
        at(217, warm_pe, 5)
        at(218, exp_k, 2)
        at(219, sub_w, 0, 5)
        at(220, k_times_l, 2, "P")
        at(221, exp_w, 0, 1)
        at(222, quant_h, 3, 1)
        at(223, min_w, 1, 3)
        at(224, relu_h, 3, 0, 3, "A")
        at(225, sub_p, 1)
        at(226, power, 1, 1)
        at(227, min_w, 1, 2)
        at(228, warm_pe, 0)
        at(229, turn_w, 0, 4, "M")
        at(230, head, 2, 2)
        at(231, warm_pe, 4)
        at(232, sub_w, 1, 3)
        at(233, sub_w, 1, 2)
        at(234, exp_p, 1)
        at(235, sum_w, 0, 0, "T")
        at(236, min_w, 0, 4)
        at(237, turn_w, 1, 5, "T")
        at(238, min_w, 1, 5)
        at(239, sub_w, 0, 4)
        at(240, hazard, 1, 7, "P")
        at(241, hazard, 1, 4, "P")
        at(242, hazard, 1, 1, "P")
        at(243, lay_h, 3, 0, 1, "V")
        at(244, sum_w, 0, 1, "T")
        at(245, turn_w, 1, 4, "T")
        at(246, neg_p, 2, "A")
        at(247, power, 1, 0)
        at(248, amp, 2)
        at(249, exp_w, 0, 3)
        at(250, power, 1, 6)
        at(251, sub_w, 1, 5)
        at(252, sum_p, 1, "M")
        at(253, lay_h, 3, 0, 0, "P")
        at(254, keep_norm, 1, "V")
        at(255, min_w, 1, 4)
        at(256, turn_w, 1, 7, "T")
        at(257, exp_w, 0, 2)
        at(258, min_w, 1, 7)
        at(259, sub_w, 1, 4)
        at(260, sum_w, 0, 3, "T")
        at(261, hazard, 1, 0, "P")
        at(262, quant_h, 3, 0)
        at(263, power, 2, 3)
        at(264, turn_w, 1, 1, "M")
        at(265, turn_p, 2)
        at(266, min_p, 2)
        at(267, hazard, 1, 6, "P")
        at(268, dup_p, 2)
        at(269, sum_w, 0, 2, "M")
        at(270, sub_w, 1, 7)
        at(271, exp_w, 1, 1)
        at(272, power, 2, 2)
        at(273, power, 2, 0)
        at(274, sub_p, 2)
        at(275, min_w, 1, 1)
        at(276, turn_w, 1, 0, "M")
        at(277, exp_w, 1, 2)
        at(278, hazard, 2, 3, "P")
        at(279, min_w, 1, 0)
        at(280, head, 3, 0)
        at(281, power, 2, 1)
        at(282, head, 3, 1)
        at(283, shape_k, 3)
        at(284, head, 3, 2)
        at(285, sub_w, 1, 1)
        at(286, turn_w, 1, 6, "T")
        at(287, exp_p, 2)
        at(288, sum_p, 2, "T")
        at(289, turn_w, 2, 3, "T")
        at(290, keep_sums, 0, "V")
        at(291, sub_w, 1, 0)
        at(292, hazard, 2, 2, "P")
        at(293, log_scale, 3)
        at(294, min_w, 1, 6)
        at(295, keep_norm, 2, "V")
        at(296, hazard, 2, 1, "P")
        at(297, sum_w, 1, 1, "T")
        at(298, min_w, 2, 3)
        at(299, sub_w, 1, 6)
        at(300, sub_w, 2, 3)
        at(301, neg_p, 3, "A")
        at(302, turn_p, 3)
        at(303, sum_w, 1, 2, "T")
        at(304, power, 2, 5)
        at(305, power, 2, 4)
        at(306, min_p, 3)
        at(307, turn_w, 2, 2, "T")
        at(308, min_w, 2, 2)
        at(309, exp_k, 3)
        at(310, turn_w, 2, 1, "T")
        at(311, hazard, 2, 0, "P")
        at(312, exp_w, 1, 0)
        at(313, min_w, 2, 1)
        at(314, sub_w, 2, 2)
        at(315, turn_w, 2, 0, "T")
        at(316, min_w, 2, 0)
        at(317, sub_p, 3)
        at(318, power, 2, 7)
        at(319, exp_w, 1, 3)
        at(320, hazard, 2, 5, "P")
        at(321, hazard, 2, 4, "P")
        at(322, sub_w, 2, 1)
        at(323, power, 2, 6)
        at(324, sum_w, 1, 0, "T")
        at(325, sum_w, 1, 3, "M")
        at(326, keep_sums, 1, "V")
        at(327, turn_w, 2, 4, "T")
        at(328, sub_w, 2, 0)
        at(329, k_times_l, 3, "P")
        at(330, turn_w, 2, 5, "N")
        at(331, min_w, 2, 4)
        at(332, min_w, 2, 5)
        at(333, power, 3, 2)
        at(334, sub_w, 2, 4)
        at(335, sub_w, 2, 5)
        at(336, exp_w, 2, 1)
        at(337, amp, 3)
        at(338, hazard, 2, 7, "P")
        at(339, turn_w, 2, 7, "T")
        at(340, power, 3, 3)
        at(341, hazard, 2, 6, "P")
        at(342, sum_w, 2, 1, "N")
        at(343, min_w, 2, 7)
        at(344, turn_w, 2, 6, "T")
        at(345, min_w, 2, 6)
        at(346, power, 3, 0)
        at(347, sub_w, 2, 7)
        at(348, exp_w, 2, 0)
        at(349, exp_p, 3)
        at(350, sub_w, 2, 6)
        at(351, power, 3, 1)
        at(352, hazard, 3, 2, "P")
        at(353, turn_w, 3, 2, "T")
        at(354, hazard, 3, 3, "P")
        at(355, hazard, 3, 0, "P")
        at(356, sum_w, 2, 0, "M")
        at(357, hazard, 3, 1, "P")
        at(358, min_w, 3, 2)
        at(359, power, 3, 4)
        at(360, turn_w, 3, 3, "T")
        at(361, min_w, 3, 3)
        at(362, exp_w, 2, 2)
        at(363, sub_w, 3, 2)
        at(364, dup_p, 3)
        at(365, power, 3, 7)
        at(366, power, 3, 6)
        at(367, exp_w, 2, 3)
        at(368, turn_w, 3, 0, "T")
        at(369, sum_w, 2, 2, "M")
        at(370, sub_w, 3, 3)
        at(371, turn_w, 3, 1, "M")
        at(372, min_w, 3, 0)
        at(373, min_w, 3, 1)
        at(374, power, 3, 5)
        at(375, sub_w, 3, 0)
        at(376, exp_w, 3, 1)
        at(377, hazard, 3, 4, "P")
        at(378, logs, 1)
        at(379, sum_w, 2, 3, "M")
        at(380, sum_p, 3, "N")
        at(381, sub_w, 3, 1)
        at(382, keep_sums, 2, "V")
        at(383, logs, 2)
        at(384, keep_norm, 3, "V")
        at(385, log_norm, 0)
        at(386, logs, 0)
        at(387, hazard, 3, 6, "P")
        at(388, turn_w, 3, 6, "T")
        at(389, min_w, 3, 6)
        at(390, hazard, 3, 7, "P")
        at(391, turn_w, 3, 4, "T")
        at(392, hazard, 3, 5, "P")
        at(393, sub_w, 3, 6)
        at(394, offset, 0, "P")
        at(395, exp_w, 3, 0)
        at(396, turn_w, 3, 7, "N")
        at(397, turn_w, 3, 5, "M")
        at(398, min_w, 3, 4)
        at(399, sum_w, 3, 1, "M")
        at(400, min_w, 3, 7)
        at(401, min_w, 3, 5)
        at(402, turn_back, 1, "N")
        at(403, sum_w, 3, 0, "T")
        at(404, sub_w, 3, 7)
        at(405, sub_w, 3, 5)
        at(406, turn_back, 0, "T")
        at(407, sub_w, 3, 4)
        at(408, exp_w, 3, 3)
        at(409, exp_w, 3, 2)
        at(410, sum_w, 3, 3, "T")
        at(411, sum_w, 3, 2, "M")
        at(412, result, 1)
        at(413, result, 0)
        at(414, lay_out, 0, "P")
        at(415, lay_out, 1, "P")
        at(416, turn_back, 2, "M")
        at(417, logs, 3)
        at(418, turn_back, 3, "T")
        at(419, result, 2)
        at(420, quant_out, 0)
        at(421, result, 3)
        at(422, quant_out, 1)
        at(423, lay_out, 2, "P")
        at(424, lay_out, 3, "V")
        at(425, quant_out, 2)
        at(426, quant_out, 3)

        for when, n, fn, args in sorted(plan, key=lambda e: e[0:2]):
            fn(*args)

        for q in range(4):
            eng = nc.sync if q % 2 == 0 else nc.scalar
            eng.dma_start(
                out=out_2[:, 4 * q : 4 * q + 4, :].rearrange("g r m -> r g m").bitcast(I32),
                in_=out_scales[32 * q : 32 * q + 4].bitcast(I32),
            )
